import numpy as np
import ml_dtypes


def mxq(x, axis, fmt="e4m3"):
    dtype, down = {"e4m3": (ml_dtypes.float8_e4m3fn, 7), "e5m2": (ml_dtypes.float8_e5m2, 14)}[fmt]
    v = np.moveaxis(np.asarray(x, np.float32).astype(ml_dtypes.bfloat16).astype(np.float64), axis, -1)
    blocks = v.reshape(v.shape[:-1] + (-1, 32))
    amax = np.abs(blocks).max(-1, keepdims=True)
    byte = np.maximum(np.where(amax > 0, np.frexp(amax)[1] - 1 + 127, 0) - down, 1)
    scale = np.exp2(byte - 127.0)
    codes = (blocks / scale).astype(np.float32).astype(dtype).astype(np.float64)
    return np.moveaxis((codes * scale).reshape(v.shape), -1, axis)


WIDE = False


def mx_kscale(k):
    if not WIDE:
        return np.ones(k)
    levels = np.array([10, -10, 5, -5, 0])
    if k % 512:
        return np.exp2(np.random.permutation(np.resize(levels, k // 32))).repeat(32)
    a = np.empty((k // 512, 16))
    for p in range(k // 512):
        a[p, :8] = np.random.permutation(np.resize(levels, 8))
        for g in range(8):
            far = levels[np.abs(levels - a[p, g]) >= 10]
            a[p, g + 8] = far[np.random.randint(len(far))]
    return np.exp2(a.ravel()).repeat(32)


BF16 = ml_dtypes.bfloat16


def bf(x):
    return np.asarray(x, np.float32).astype(BF16)


def f64(x):
    return np.asarray(x).astype(np.float64)


E2M1 = np.array([0.0, 0.5, 1.0, 1.5, 2.0, 3.0, 4.0, 6.0, -0.0, -0.5, -1.0, -1.5, -2.0, -3.0, -4.0, -6.0])


def pack_weight(w, fmt):
    k, n = w.shape
    w = f64(bf(w)).reshape(k // 32, 32, n)
    amax = np.abs(w).max(1)
    if fmt == "e4m3":
        byte = np.frexp(amax)[1] - 1 + 127 - 7
    else:
        mant, ex = np.frexp(amax / 6.0)
        byte = np.where(mant > 0.5, ex, ex - 1) + 127
    byte = np.clip(np.where(amax > 0, byte, 1), 1, 254)
    scaled = (w * np.exp2(127.0 - byte)[:, None, :]).reshape(k, n).astype(np.float32)
    by_word = np.ascontiguousarray(scaled.reshape(k // 512, 128, 4, n).transpose(0, 1, 3, 2))
    if fmt == "e4m3":
        words = by_word.astype(ml_dtypes.float8_e4m3fn).view(np.uint8)
    else:
        c = by_word.astype(ml_dtypes.float4_e2m1fn).view(np.uint8) & 0xF
        words = c[..., 0::2] | (c[..., 1::2] << 4)
    return np.ascontiguousarray(words), np.ascontiguousarray(byte.astype(np.uint8).reshape(k // 512, 16, n))


def unpack_weight(words, scales, fmt):
    g, p, n, _ = words.shape
    if fmt == "e4m3":
        vals = np.ascontiguousarray(words).view(ml_dtypes.float8_e4m3fn).astype(np.float64)
    else:
        nib = np.empty((g, p, n, 4), np.uint8)
        nib[..., 0::2] = words & 0xF
        nib[..., 1::2] = words >> 4
        vals = E2M1[nib]
    vals = vals * np.repeat(np.exp2(scales.astype(np.float64) - 127.0), 8, axis=1)[..., None]
    return vals.transpose(0, 1, 3, 2).reshape(g * 512, n)
def pack4(w):
    words, scales = pack_weight(w, "e2m1")
    return words.reshape(words.shape[0], 128, -1), scales


def unpack4(words, scales):
    return unpack_weight(words.reshape(words.shape[0], 128, -1, 2), scales, "e2m1")


T, D, R = 2048, 1024, 512


def setup_inputs():
    s = mx_kscale(D)
    r = mx_kscale(T)
    c = mx_kscale(R)
    x = np.random.standard_normal((T, D)) * s * r[:, None]
    pos = np.random.standard_normal((T, R)) * r[:, None] * c
    keep = (1 + 0.1 * np.random.standard_normal(T)) / r
    gate = np.random.standard_normal((T, D))
    down = np.random.standard_normal((D, R)) / (3 * np.sqrt(D)) / s[:, None] * c
    mix = np.random.standard_normal((T, T)) / (3 * np.sqrt(T)) / r[:, None]
    up = np.random.standard_normal((R, D)) / np.sqrt(R) / c[:, None]
    down_words, down_scales = pack4(down)
    mix_words, mix_scales = pack4(mix)
    up_words, up_scales = pack4(up)
    return {"x": bf(x), "pos": bf(pos), "keep": bf(keep), "gate": bf(gate),
            "down_words": down_words, "down_scales": down_scales,
            "mix_words": mix_words, "mix_scales": mix_scales,
            "up_words": up_words, "up_scales": up_scales}


def reference(x, pos, keep, gate, down_words, down_scales, mix_words, mix_scales, up_words, up_scales):
    down = unpack4(down_words, down_scales)
    mix = unpack4(mix_words, mix_scales)
    up = unpack4(up_words, up_scales)
    u = f64(pos) + (mxq(f64(x), 1, "e4m3") @ down)
    v = f64(keep)[:, None] * u + (mix.T @ mxq(u, 0, "e4m3"))
    return (mxq(v, 1, "e4m3") @ up) / (1 + np.exp(-f64(gate)))

@@ -1,0 +1,301 @@
+from contextlib import ExitStack
+
+import concourse.mybir as mybir
+from concourse.masks import make_identity
+
+T, D, R = 2048, 1024, 512
+FLOPS = 2 * T * D * R + 2 * T * T * R + 2 * T * R * D
+
+F32 = mybir.dt.float32
+BF16 = mybir.dt.bfloat16
+I32 = mybir.dt.int32
+U32 = mybir.dt.uint32
+U8 = mybir.dt.uint8
+FP8X4 = mybir.dt.float8_e4m3fn_x4
+FP4X4 = mybir.dt.float4_e2m1fn_x4
+ADD = mybir.AluOpType.add
+MULT = mybir.AluOpType.mult
+SIGMOID = mybir.ActivationFunctionType.Sigmoid
+
+P = 128
+EARLY_W = {5: [(0, 0)], 6: [(0, 1), (0, 2)], 7: [(0, 3), (1, 0)], 8: [(1, 1), (1, 2)], 9: [(1, 3), (2, 0)], 10: [(2, 1), (2, 2), (2, 3), (3, 0), (3, 1), (3, 2), (3, 3)]}
+W_ON_VECTOR = {(2, 1), (2, 3), (3, 1)}
+SG = (1, 3, 5, 7, 9, 11, 13, 14)
+D_ON_SCALAR = {(0, 0), (1, 0), (2, 0), (3, 0)}
+GROUPS = T // 512
+BLOCKS = T // P
+
+
+def tile_low_rank_row_mixer_t2_kernel(
+    tc, x, pos, keep, gate, down_words, down_scales, mix_words, mix_scales, up_words, up_scales, out
+):
+    nc = tc.nc
+    with ExitStack() as ctx:
+        const = ctx.enter_context(tc.tile_pool(name="const", bufs=1))
+        work = ctx.enter_context(tc.tile_pool(name="work", bufs=2))
+        psum = ctx.enter_context(tc.psum_pool(name="psum", bufs=2))
+        ctx.enter_context(tc.manual_schedule())
+
+        def scale_plane(width, name):
+            plane = const.tile([P, width], U8, name=name, align_bytes=64)
+            nc.vector.memset(plane[:].bitcast(I32), 0)
+            return plane
+
+        def load_scales(queue, plane, scales, groups):
+            src = scales.bitcast(I32).rearrange("g q n -> q g n")
+            dst = plane[:].bitcast(I32).rearrange("p (g n) -> p g n", g=groups)
+            for quad in range(4):
+                queue.dma_start(out=dst[32 * quad : 32 * quad + 4], in_=src[4 * quad : 4 * quad + 4])
+
+        down_sc = scale_plane(2 * R, "down_sc")
+        load_scales(nc.sync, down_sc, down_scales, 2)
+        warm = const.tile([P, 1], F32, name="warm")
+        nc.vector.memset(warm[:], 0.0)
+        nc.scalar.activation(warm[:], warm[:], SIGMOID)
+        ident = const.tile([P, P], F32, name="ident")
+        make_identity(nc, ident[:])
+
+        mix_sc = scale_plane(4 * T, "mix_sc")
+        up_sc = scale_plane(D, "up_sc")
+
+        down_sb = const.tile([P, 2 * 2 * R], U8, name="down_sb", align_bytes=64)
+        mix_sb = const.tile([P, 4 * 2 * T], U8, name="mix_sb", align_bytes=64)
+        up_sb = const.tile([P, 2 * D], U8, name="up_sb", align_bytes=64)
+
+        x_rows = x.rearrange("(g p t) k -> g p t k", p=P, t=4)
+        pos_rows = pos.rearrange("(g p t) r -> g p t r", p=P, t=4)
+        gate_rows = gate.rearrange("(q b p) c -> q p b c", p=P, b=4)
+
+        x_sb = [work.tile([P, 4, D], BF16, name="x", bufs=3) for g in range(GROUPS)]
+        pos_sb = [const.tile([P, 4, R], BF16, name="pos%d" % g) for g in range(GROUPS)]
+        gate_sb = [const.tile([P, 4, D], BF16, name="gate%d" % q) for q in range(4)]
+
+        keep_bf = const.tile([P, GROUPS, 4], BF16, name="keep_bf")
+        nc.gpsimd.dma_start(out=keep_bf[:], in_=keep.rearrange("(g p t) -> p g t", p=P, t=4))
+        keep_f = const.tile([P, GROUPS, 4], F32, name="keep_f")
+        nc.gpsimd.tensor_copy(out=keep_f[:], in_=keep_bf[:])
+
+        for t in range(4):
+            nc.sync.dma_start(out=x_sb[0][:, t], in_=x_rows[0][:, t])
+        nc.sync.dma_start(
+            out=down_sb[:].bitcast(I32).rearrange("p (g n) -> p g n", g=2),
+            in_=down_words.bitcast(I32).rearrange("g p n -> p g n"),
+        )
+        nc.sync.dma_start(out=pos_sb[0][:], in_=pos_rows[0])
+        for g in range(1, GROUPS):
+            for h in range(2):
+                nc.sync.dma_start(out=x_sb[g][:, 2 * h : 2 * h + 2], in_=x_rows[g][:, 2 * h : 2 * h + 2])
+            nc.sync.dma_start(out=pos_sb[g][:], in_=pos_rows[g])
+        mix_dst = mix_sb[:].bitcast(I32).rearrange("p (g n) -> p g n", g=4)
+        mix_src = mix_words.bitcast(I32).rearrange("g p n -> p g n")
+        for h in range(2):
+            nc.sync.dma_start(out=mix_dst[:, :, 512 * h : 512 * h + 512], in_=mix_src[:, :, 512 * h : 512 * h + 512])
+        nc.sync.dma_start(
+            out=up_sb[:].bitcast(I32),
+            in_=up_words.bitcast(I32).rearrange("g p n -> p (g n)"),
+        )
+        load_scales(nc.sync, mix_sc, mix_scales, 4)
+        load_scales(nc.sync, up_sc, up_scales, 1)
+        for q in range(4):
+            nc.sync.dma_start(out=gate_sb[q][:], in_=gate_rows[q])
+
+        xt_banks, xg, xc, xs, s1_banks, u, w, ug, uc, us, w_t = {}, {}, {}, {}, {}, {}, {}, {}, {}, {}, {}
+
+        def t_x(j):
+            for tt in range(2):
+                words = x_sb[j // 2][:, 2 * (j % 2) + tt].bitcast(F32)
+                bank = psum.tile([P, 2, 2, P], F32, name="xt", tag="bank_a", bufs=3)
+                for kc in range(2):
+                    for half in range(2):
+                        nc.tensor.transpose(bank[:, kc, half], words[:, 256 * kc + half : 256 * (kc + 1) : 2], ident[:])
+                xt_banks[j, tt] = bank
+
+        def a_x(j):
+            xg[j] = work.tile([P, 2, 2 * P * 4], BF16, name="xg", bufs=3, align_bytes=64)
+            for tt in range(2):
+                nc.scalar.copy(
+                    out=xg[j][:, tt].bitcast(F32).rearrange("p (k r u) -> p k r u", k=2, u=2),
+                    in_=xt_banks[j, tt][:].rearrange("p k u r -> p k r u"),
+                )
+
+        def b_x(j):
+            xc[j] = work.tile([P, 512], U32, name="xc", bufs=3, align_bytes=64)
+            xs[j] = work.tile([P, 512], U8, name="xs", bufs=3, align_bytes=64)
+            nc.vector.quantize_mx(
+                out=xc[j][:].bitcast(FP8X4), scales=xs[j][:], in_=xg[j][:].rearrange("p a b -> p (a b)")
+            )
+
+        def stage1(j):
+            for tt in range(2):
+                bank = psum.tile([P, R], F32, name="s1", tag="bank_b", bufs=2)
+                for kc in range(2):
+                    cols = slice(256 * tt + 128 * kc, 256 * tt + 128 * kc + 128)
+                    nc.tensor.matmul_mx(
+                        out=bank[:],
+                        lhsT=xc[j][:, cols].bitcast(FP8X4),
+                        lhsT_scale=xs[j][:, cols],
+                        rhs=down_sb[:, 2 * R * kc : 2 * R * (kc + 1)].bitcast(FP4X4),
+                        rhs_scale=down_sc[:, R * kc : R * (kc + 1)],
+                        start=(kc == 0),
+                        stop=(kc == 1),
+                    )
+                s1_banks[j, tt] = bank
+
+        def c_u(j):
+            g = j // 2
+            if j % 2 == 0:
+                u[g] = work.tile([P, 4, R], F32, name="u", bufs=2)
+                w[g] = work.tile([P, 4, R], F32, name="w", bufs=2)
+            for tt in range(2):
+                t = 2 * (j % 2) + tt
+                nc.vector.tensor_tensor(
+                    out=u[g][:, t].rearrange("p (a m) -> p a m", a=4),
+                    in0=s1_banks[j, tt][:].rearrange("p (m a) -> p a m", a=4),
+                    in1=pos_sb[g][:, t].rearrange("p (m a) -> p a m", a=4),
+                    op=ADD,
+                )
+                if True:
+                    nc.gpsimd.tensor_scalar(
+                        out=w[g][:, t], in0=u[g][:, t], scalar1=keep_f[:, g, t : t + 1], scalar2=0.0, op0=MULT, op1=ADD
+                    )
+
+        def d_u(g):
+            ug[g] = work.tile([P, R, 4], BF16, name="ug", bufs=2, align_bytes=64)
+            src = u[g][:].rearrange("p t c -> p c t")
+            for h in range(2):
+                cols = slice(256 * h, 256 * h + 256)
+                if (g, h) in D_ON_SCALAR:
+                    nc.scalar.copy(out=ug[g][:, cols], in_=src[:, cols])
+                else:
+                    nc.vector.tensor_copy(out=ug[g][:, cols], in_=src[:, cols])
+
+        def e_u(g):
+            uc[g] = const.tile([P, R], U32, name="uc%d" % g, align_bytes=64)
+            us[g] = const.tile([P, R], U8, name="us%d" % g, align_bytes=64)
+            for h in (1, 0):
+                cols = slice(256 * h, 256 * h + 256)
+                nc.vector.quantize_mx(
+                    out=uc[g][:, cols].bitcast(FP8X4),
+                    scales=us[g][:, cols],
+                    in_=ug[g][:, cols].rearrange("p c t -> p (c t)"),
+                )
+
+        def w_turn(g, a):
+            if a == 0:
+                w_t[g] = work.tile([P, 4, 512], F32, name="w_t", bufs=4)
+            bank = psum.tile([P, 4, P], F32, name="wt", tag="bank_c", bufs=3)
+            for t in range(4):
+                nc.tensor.transpose(bank[:, t], w[g][:, t, P * a : P * (a + 1)], ident[:])
+            copy = nc.vector.tensor_copy if (g, a) in W_ON_VECTOR else nc.scalar.copy
+            copy(out=w_t[g][:, a].rearrange("m (p t) -> m p t", t=4), in_=bank[:].rearrange("m t p -> m p t"))
+
+        def w_run(banks):
+            for g, a in banks:
+                w_turn(g, a)
+
+        for j in range(10):
+            g = (j - 3) // 2
+            if j < 8:
+                t_x(j)
+            if 1 <= j < 9:
+                stage1(j - 1)
+            if j < 8:
+                a_x(j)
+            if j % 2 == 1 and g >= 0:
+                d_u(g)
+            w_run(EARLY_W.get(j, []))
+            if j < 8:
+                b_x(j)
+            if 1 <= j < 9:
+                c_u(j - 1)
+            if j % 2 == 1 and g >= 0:
+                e_u(g)
+        w_run(EARLY_W[10])
+
+        s2_banks, vg, vc, vs, s3_banks, sig = {}, {}, {}, {}, {}, {}
+
+        def stage2(n):
+            bank = psum.tile([P, 4, P], F32, name="s2", tag="bank_a", bufs=3)
+            for a in range(4):
+                for g in range(GROUPS):
+                    cols = slice(P * a, P * (a + 1))
+                    first = T * g + P * n
+                    nc.tensor.matmul_mx(
+                        out=bank[:, a],
+                        lhsT=uc[g][:, cols].bitcast(FP8X4),
+                        lhsT_scale=us[g][:, cols],
+                        rhs=mix_sb[:, 2 * first : 2 * (first + P)].bitcast(FP4X4),
+                        rhs_scale=mix_sc[:, first : first + P],
+                        start=(g == 0),
+                        stop=(g == GROUPS - 1),
+                    )
+            s2_banks[n] = bank
+
+        def f_v(n):
+            vg[n] = work.tile([P, P, 4], BF16, name="vg", bufs=3, align_bytes=64)
+            col = P * (n % 4)
+            nc.vector.tensor_tensor(
+                out=vg[n][:],
+                in0=s2_banks[n][:].rearrange("m a n -> m n a"),
+                in1=w_t[n // 4][:, :, col : col + P].rearrange("m a n -> m n a"),
+                op=ADD,
+            )
+
+        def h_v(n):
+            vc[n] = work.tile([P, P], U32, name="vc", bufs=3, align_bytes=64)
+            vs[n] = work.tile([P, P], U8, name="vs", bufs=3, align_bytes=64)
+            nc.vector.quantize_mx(
+                out=vc[n][:].bitcast(FP8X4), scales=vs[n][:], in_=vg[n][:].rearrange("m n a -> m (n a)")
+            )
+
+        def stage3(n):
+            for h, tag, bufs in ((0, "bank_b", 2), (1, "bank_c", 3)):
+                bank = psum.tile([P, 512], F32, name="s3", tag=tag, bufs=bufs)
+                nc.tensor.matmul_mx(
+                    out=bank[:],
+                    lhsT=vc[n][:].bitcast(FP8X4),
+                    lhsT_scale=vs[n][:],
+                    rhs=up_sb[:, 1024 * h : 1024 * (h + 1)].bitcast(FP4X4),
+                    rhs_scale=up_sc[:, 512 * h : 512 * (h + 1)],
+                    start=True,
+                    stop=True,
+                )
+                s3_banks[n, h] = bank
+
+        def i_gate(n):
+            sig[n] = work.tile([P, D], F32, name="sig", bufs=3)
+            nc.scalar.activation(sig[n][:], gate_sb[n // 4][:, n % 4], SIGMOID)
+
+        o_tiles = {}
+
+        def j_out(n, h):
+            if h == 0:
+                o_tiles[n] = work.tile([P, D], F32, name="o", bufs=3)
+            cols = slice(512 * h, 512 * (h + 1))
+            if h == 1 and n in SG:
+                z = work.tile([P, 512], F32, name="z", bufs=2)
+                nc.scalar.copy(out=z[:], in_=s3_banks[n, h][:])
+                nc.gpsimd.tensor_tensor(out=o_tiles[n][:, cols], in0=z[:], in1=sig[n][:, cols], op=MULT)
+            else:
+                nc.vector.tensor_tensor(out=o_tiles[n][:, cols], in0=s3_banks[n, h][:], in1=sig[n][:, cols], op=MULT)
+
+        for n in range(BLOCKS + 1):
+            if n < BLOCKS:
+                stage2(n)
+            if n >= 1:
+                stage3(n - 1)
+            if n < BLOCKS:
+                i_gate(n)
+                f_v(n)
+            if n in (0, BLOCKS - 1) or n - 1 in SG:
+                if n < BLOCKS:
+                    h_v(n)
+                if n >= 1:
+                    j_out(n - 1, 0)
+            else:
+                j_out(n - 1, 0)
+                if n < BLOCKS:
+                    h_v(n)
+            if n >= 1:
+                j_out(n - 1, 1)
+                nc.sync.dma_start(out=out[P * (n - 1) : P * n, :], in_=o_tiles[n - 1][:])

@@ -18,12 +18,9 @@ MULT = mybir.AluOpType.mult
 SIGMOID = mybir.ActivationFunctionType.Sigmoid
 
 P = 128
-EARLY_W = {5: [(0, 0)], 6: [(0, 1), (0, 2)], 7: [(0, 3), (1, 0)], 8: [(1, 1), (1, 2)], 9: [(1, 3), (2, 0)], 10: [(2, 1), (2, 2), (2, 3), (3, 0), (3, 1), (3, 2), (3, 3)]}
-W_ON_VECTOR = {(2, 1), (2, 3), (3, 1)}
-SG = (1, 3, 5, 7, 9, 11, 13, 14)
-D_ON_SCALAR = {(0, 0), (1, 0), (2, 0), (3, 0)}
 GROUPS = T // 512
 BLOCKS = T // P
+STEPS = 2 * GROUPS
 
 
 def tile_low_rank_row_mixer_t2_kernel(
@@ -33,8 +30,12 @@ def tile_low_rank_row_mixer_t2_kernel(
     with ExitStack() as ctx:
         const = ctx.enter_context(tc.tile_pool(name="const", bufs=1))
         work = ctx.enter_context(tc.tile_pool(name="work", bufs=2))
-        psum = ctx.enter_context(tc.psum_pool(name="psum", bufs=2))
+        psum = ctx.enter_context(tc.psum_pool(name="psum", bufs=1))
         ctx.enter_context(tc.manual_schedule())
+
+        def psum_bank(index):
+            bank = psum.tile([P, 512], F32, name="bank%d" % index, tag="bank%d" % index)
+            return bank
 
         def scale_plane(width, name):
             plane = const.tile([P, width], U8, name=name, align_bytes=64)
@@ -47,93 +48,113 @@ def tile_low_rank_row_mixer_t2_kernel(
             for quad in range(4):
                 queue.dma_start(out=dst[32 * quad : 32 * quad + 4], in_=src[4 * quad : 4 * quad + 4])
 
+        x_rows = x.rearrange("(g p t) k -> g p t k", p=P, t=4)
+        pos_rows = pos.rearrange("(g p t) r -> g p t r", p=P, t=4)
+        gate_rows = gate.rearrange("(n p) c -> p n c", p=P)
+
         down_sc = scale_plane(2 * R, "down_sc")
-        load_scales(nc.sync, down_sc, down_scales, 2)
+        mix_sc = scale_plane(4 * T, "mix_sc")
+        up_sc = scale_plane(D, "up_sc")
         warm = const.tile([P, 1], F32, name="warm")
         nc.vector.memset(warm[:], 0.0)
         nc.scalar.activation(warm[:], warm[:], SIGMOID)
         ident = const.tile([P, P], F32, name="ident")
         make_identity(nc, ident[:])
 
-        mix_sc = scale_plane(4 * T, "mix_sc")
-        up_sc = scale_plane(D, "up_sc")
-
-        down_sb = const.tile([P, 2 * 2 * R], U8, name="down_sb", align_bytes=64)
-        mix_sb = const.tile([P, 4 * 2 * T], U8, name="mix_sb", align_bytes=64)
-        up_sb = const.tile([P, 2 * D], U8, name="up_sb", align_bytes=64)
-
-        x_rows = x.rearrange("(g p t) k -> g p t k", p=P, t=4)
-        pos_rows = pos.rearrange("(g p t) r -> g p t r", p=P, t=4)
-        gate_rows = gate.rearrange("(q b p) c -> q p b c", p=P, b=4)
-
-        x_sb = [work.tile([P, 4, D], BF16, name="x", bufs=3) for g in range(GROUPS)]
-        pos_sb = [const.tile([P, 4, R], BF16, name="pos%d" % g) for g in range(GROUPS)]
-        gate_sb = [const.tile([P, 4, D], BF16, name="gate%d" % q) for q in range(4)]
-
         keep_bf = const.tile([P, GROUPS, 4], BF16, name="keep_bf")
         nc.gpsimd.dma_start(out=keep_bf[:], in_=keep.rearrange("(g p t) -> p g t", p=P, t=4))
         keep_f = const.tile([P, GROUPS, 4], F32, name="keep_f")
         nc.gpsimd.tensor_copy(out=keep_f[:], in_=keep_bf[:])
 
-        for t in range(4):
-            nc.sync.dma_start(out=x_sb[0][:, t], in_=x_rows[0][:, t])
+        x_sb, pos_sb, gate_sb, mix_sb = {}, {}, {}, {}
+
+        def load_x(g, first, count):
+            rows = const.tile([P, count * D], BF16, name="x%d_%d" % (g, first))
+            nc.sync.dma_start(
+                out=rows[:].rearrange("p (t k) -> p t k", t=count), in_=x_rows[g][:, first : first + count]
+            )
+            for t in range(count):
+                x_sb[g, first + t] = rows[:, D * t : D * (t + 1)]
+
+        def load_pos(g):
+            pos_sb[g] = const.tile([P, 4, R], BF16, name="pos%d" % g)
+            nc.sync.dma_start(out=pos_sb[g][:], in_=pos_rows[g])
+
+        def load_gate(first, count):
+            rows = const.tile([P, count, D], BF16, name="gate%d" % first)
+            nc.sync.dma_start(out=rows[:], in_=gate_rows[:, first : first + count])
+            for n in range(count):
+                gate_sb[first + n] = rows[:, n]
+
+        def load_mix(half):
+            mix_sb[half] = const.tile([P, GROUPS * T], U8, name="mix%d" % half, align_bytes=64)
+            nc.sync.dma_start(
+                out=mix_sb[half][:].bitcast(I32).rearrange("p (g n) -> p g n", g=GROUPS),
+                in_=mix_words.bitcast(I32).rearrange("g p n -> p g n")[:, :, 512 * half : 512 * (half + 1)],
+            )
+
+        down_sb = const.tile([P, 2 * 2 * R], U8, name="down_sb", align_bytes=64)
+        up_sb = const.tile([P, 2 * D], U8, name="up_sb", align_bytes=64)
+
+        load_x(0, 0, 1)
+        load_x(0, 1, 1)
         nc.sync.dma_start(
             out=down_sb[:].bitcast(I32).rearrange("p (g n) -> p g n", g=2),
             in_=down_words.bitcast(I32).rearrange("g p n -> p g n"),
         )
-        nc.sync.dma_start(out=pos_sb[0][:], in_=pos_rows[0])
+        load_scales(nc.sync, down_sc, down_scales, 2)
+        load_x(0, 2, 2)
+        load_pos(0)
         for g in range(1, GROUPS):
-            for h in range(2):
-                nc.sync.dma_start(out=x_sb[g][:, 2 * h : 2 * h + 2], in_=x_rows[g][:, 2 * h : 2 * h + 2])
-            nc.sync.dma_start(out=pos_sb[g][:], in_=pos_rows[g])
-        mix_dst = mix_sb[:].bitcast(I32).rearrange("p (g n) -> p g n", g=4)
-        mix_src = mix_words.bitcast(I32).rearrange("g p n -> p g n")
-        for h in range(2):
-            nc.sync.dma_start(out=mix_dst[:, :, 512 * h : 512 * h + 512], in_=mix_src[:, :, 512 * h : 512 * h + 512])
-        nc.sync.dma_start(
-            out=up_sb[:].bitcast(I32),
-            in_=up_words.bitcast(I32).rearrange("g p n -> p (g n)"),
-        )
-        load_scales(nc.sync, mix_sc, mix_scales, 4)
-        load_scales(nc.sync, up_sc, up_scales, 1)
-        for q in range(4):
-            nc.sync.dma_start(out=gate_sb[q][:], in_=gate_rows[q])
+            load_x(g, 0, 2)
+            load_x(g, 2, 2)
+            load_pos(g)
+            if g == 2:
+                load_scales(nc.sync, mix_sc, mix_scales, 4)
+                load_scales(nc.sync, up_sc, up_scales, 1)
+        load_mix(0)
+        nc.sync.dma_start(out=up_sb[:].bitcast(I32), in_=up_words.bitcast(I32).rearrange("g p n -> p (g n)"))
+        load_gate(0, 2)
+        load_gate(2, 2)
+        load_mix(1)
+        for first in range(4, BLOCKS, 4):
+            load_gate(first, 4)
 
-        xt_banks, xg, xc, xs, s1_banks, u, w, ug, uc, us, w_t = {}, {}, {}, {}, {}, {}, {}, {}, {}, {}, {}
+        xt_banks, xc, xs, xg, s1_banks, u, ug, uc, us, w_t, wt_banks = {}, {}, {}, {}, {}, {}, {}, {}, {}, {}, {}
 
-        def t_x(j):
+        def turn_x(j):
             for tt in range(2):
-                words = x_sb[j // 2][:, 2 * (j % 2) + tt].bitcast(F32)
-                bank = psum.tile([P, 2, 2, P], F32, name="xt", tag="bank_a", bufs=3)
+                words = x_sb[j // 2, 2 * (j % 2) + tt].bitcast(F32)
+                bank = psum_bank(2 * (j % 2) + tt)
                 for kc in range(2):
                     for half in range(2):
-                        nc.tensor.transpose(bank[:, kc, half], words[:, 256 * kc + half : 256 * (kc + 1) : 2], ident[:])
+                        col = P * (2 * kc + half)
+                        nc.tensor.transpose(
+                            bank[:, col : col + P], words[:, 256 * kc + half : 256 * (kc + 1) : 2], ident[:]
+                        )
                 xt_banks[j, tt] = bank
 
-        def a_x(j):
-            xg[j] = work.tile([P, 2, 2 * P * 4], BF16, name="xg", bufs=3, align_bytes=64)
-            for tt in range(2):
-                nc.scalar.copy(
-                    out=xg[j][:, tt].bitcast(F32).rearrange("p (k r u) -> p k r u", k=2, u=2),
-                    in_=xt_banks[j, tt][:].rearrange("p k u r -> p k r u"),
-                )
-
-        def b_x(j):
-            xc[j] = work.tile([P, 512], U32, name="xc", bufs=3, align_bytes=64)
-            xs[j] = work.tile([P, 512], U8, name="xs", bufs=3, align_bytes=64)
-            nc.vector.quantize_mx(
-                out=xc[j][:].bitcast(FP8X4), scales=xs[j][:], in_=xg[j][:].rearrange("p a b -> p (a b)")
+        def copy_x(j, tt):
+            xg[j, tt] = work.tile([P, 2 * P * 4], BF16, name="xg", bufs=4, align_bytes=64)
+            nc.scalar.copy(
+                out=xg[j, tt][:].bitcast(F32).rearrange("p (k r h) -> p k r h", k=2, h=2),
+                in_=xt_banks[j, tt][:].rearrange("p (k h r) -> p k r h", k=2, h=2),
             )
+
+        def quant_x(j, tt):
+            xc[j, tt] = work.tile([P, 256], U32, name="xc", bufs=4, align_bytes=64)
+            xs[j, tt] = work.tile([P, 256], U8, name="xs", bufs=4, align_bytes=64)
+            nc.vector.quantize_mx(out=xc[j, tt][:].bitcast(FP8X4), scales=xs[j, tt][:], in_=xg[j, tt][:])
 
         def stage1(j):
             for tt in range(2):
-                bank = psum.tile([P, R], F32, name="s1", tag="bank_b", bufs=2)
+                bank = psum_bank(4 + 2 * (j % 2) + tt)
                 for kc in range(2):
-                    cols = slice(256 * tt + 128 * kc, 256 * tt + 128 * kc + 128)
+                    cols = slice(P * kc, P * (kc + 1))
                     nc.tensor.matmul_mx(
                         out=bank[:],
-                        lhsT=xc[j][:, cols].bitcast(FP8X4),
-                        lhsT_scale=xs[j][:, cols],
+                        lhsT=xc[j, tt][:, cols].bitcast(FP8X4),
+                        lhsT_scale=xs[j, tt][:, cols],
                         rhs=down_sb[:, 2 * R * kc : 2 * R * (kc + 1)].bitcast(FP4X4),
                         rhs_scale=down_sc[:, R * kc : R * (kc + 1)],
                         start=(kc == 0),
@@ -141,116 +162,136 @@ def tile_low_rank_row_mixer_t2_kernel(
                     )
                 s1_banks[j, tt] = bank
 
-        def c_u(j):
-            g = j // 2
-            if j % 2 == 0:
-                u[g] = work.tile([P, 4, R], F32, name="u", bufs=2)
-                w[g] = work.tile([P, 4, R], F32, name="w", bufs=2)
-            for tt in range(2):
-                t = 2 * (j % 2) + tt
-                nc.vector.tensor_tensor(
-                    out=u[g][:, t].rearrange("p (a m) -> p a m", a=4),
-                    in0=s1_banks[j, tt][:].rearrange("p (m a) -> p a m", a=4),
-                    in1=pos_sb[g][:, t].rearrange("p (m a) -> p a m", a=4),
-                    op=ADD,
-                )
-                if True:
-                    nc.gpsimd.tensor_scalar(
-                        out=w[g][:, t], in0=u[g][:, t], scalar1=keep_f[:, g, t : t + 1], scalar2=0.0, op0=MULT, op1=ADD
-                    )
+        def add_pos(j, tt):
+            g, t = j // 2, 2 * (j % 2) + tt
+            if t == 0:
+                u[g] = const.tile([P, 4, R], F32, name="u%d" % g)
+            nc.vector.tensor_tensor(
+                out=u[g][:, t].rearrange("p (a c i) -> p c a i", a=4, i=4),
+                in0=s1_banks[j, tt][:].rearrange("p (c i a) -> p c a i", a=4, i=4),
+                in1=pos_sb[g][:, t].rearrange("p (c i a) -> p c a i", a=4, i=4),
+                op=ADD,
+            )
 
-        def d_u(g):
-            ug[g] = work.tile([P, R, 4], BF16, name="ug", bufs=2, align_bytes=64)
-            src = u[g][:].rearrange("p t c -> p c t")
-            for h in range(2):
-                cols = slice(256 * h, 256 * h + 256)
-                if (g, h) in D_ON_SCALAR:
-                    nc.scalar.copy(out=ug[g][:, cols], in_=src[:, cols])
-                else:
-                    nc.vector.tensor_copy(out=ug[g][:, cols], in_=src[:, cols])
+        def round_u(g, a, on_vector):
+            ug[g, a] = work.tile([P, P, 4], BF16, name="ug", bufs=8, align_bytes=64)
+            src = u[g][:, :, P * a : P * (a + 1)].rearrange("p t c -> p c t")
+            copy = nc.vector.tensor_copy if on_vector else nc.scalar.copy
+            copy(out=ug[g, a][:], in_=src)
 
-        def e_u(g):
-            uc[g] = const.tile([P, R], U32, name="uc%d" % g, align_bytes=64)
-            us[g] = const.tile([P, R], U8, name="us%d" % g, align_bytes=64)
-            for h in (1, 0):
-                cols = slice(256 * h, 256 * h + 256)
-                nc.vector.quantize_mx(
-                    out=uc[g][:, cols].bitcast(FP8X4),
-                    scales=us[g][:, cols],
-                    in_=ug[g][:, cols].rearrange("p c t -> p (c t)"),
-                )
-
-        def w_turn(g, a):
+        def quant_u(g, a):
             if a == 0:
-                w_t[g] = work.tile([P, 4, 512], F32, name="w_t", bufs=4)
-            bank = psum.tile([P, 4, P], F32, name="wt", tag="bank_c", bufs=3)
+                uc[g] = const.tile([P, R], U32, name="uc%d" % g, align_bytes=64)
+                us[g] = const.tile([P, R], U8, name="us%d" % g, align_bytes=64)
+            cols = slice(P * a, P * (a + 1))
+            nc.vector.quantize_mx(
+                out=uc[g][:, cols].bitcast(FP8X4), scales=us[g][:, cols], in_=ug[g, a][:].rearrange("p c t -> p (c t)")
+            )
+
+        def scale_u(g):
             for t in range(4):
-                nc.tensor.transpose(bank[:, t], w[g][:, t, P * a : P * (a + 1)], ident[:])
-            copy = nc.vector.tensor_copy if (g, a) in W_ON_VECTOR else nc.scalar.copy
-            copy(out=w_t[g][:, a].rearrange("m (p t) -> m p t", t=4), in_=bank[:].rearrange("m t p -> m p t"))
+                nc.gpsimd.tensor_scalar(
+                    out=u[g][:, t], in0=u[g][:, t], scalar1=keep_f[:, g, t : t + 1], scalar2=0.0, op0=MULT, op1=ADD
+                )
 
-        def w_run(banks):
-            for g, a in banks:
-                w_turn(g, a)
+        def turn_w(g, t, index):
+            bank = psum_bank(index)
+            for a in range(4):
+                cols = slice(P * a, P * (a + 1))
+                nc.tensor.transpose(bank[:, cols], u[g][:, t, cols], ident[:])
+            wt_banks[g, t] = bank
 
-        for j in range(10):
-            g = (j - 3) // 2
-            if j < 8:
-                t_x(j)
-            if 1 <= j < 9:
+        def copy_w(g, t):
+            if t == 0:
+                w_t[g] = work.tile([P, 512 * 4], F32, name="w_t", bufs=2)
+            nc.scalar.copy(
+                out=w_t[g][:].rearrange("m (p t a) -> m t p a", t=4, a=4)[:, t],
+                in_=wt_banks[g, t][:].rearrange("m (a p) -> m p a", a=4),
+            )
+
+        last = GROUPS - 1
+        for j in range(STEPS + 1):
+            g, late = (j - 3) // 2, (j - 3) % 2
+            if j < STEPS:
+                turn_x(j)
+            if j >= 1:
                 stage1(j - 1)
-            if j < 8:
-                a_x(j)
-            if j % 2 == 1 and g >= 0:
-                d_u(g)
-            w_run(EARLY_W.get(j, []))
-            if j < 8:
-                b_x(j)
-            if 1 <= j < 9:
-                c_u(j - 1)
-            if j % 2 == 1 and g >= 0:
-                e_u(g)
-        w_run(EARLY_W[10])
+            if j < STEPS:
+                copy_x(j, 0)
+                copy_x(j, 1)
+            if j >= 2:
+                add_pos(j - 2, 0)
+                add_pos(j - 2, 1)
+            if j >= 3 and not late:
+                round_u(g, 0, False)
+                round_u(g, 1, False)
+            if j >= 3 and late:
+                round_u(g, 2, False)
+                round_u(g, 3, True)
+            if j < STEPS:
+                quant_x(j, 0)
+            if j >= 3 and late:
+                quant_u(g, 0)
+                quant_u(g, 1)
+            if j < STEPS:
+                quant_x(j, 1)
+            if j >= 3 and late:
+                scale_u(g)
+                quant_u(g, 3)
+                quant_u(g, 2)
+        for t in range(4):
+            turn_w(0, t, t)
+            copy_w(0, t)
+        add_pos(STEPS - 1, 0)
+        add_pos(STEPS - 1, 1)
+        round_u(last, 0, True)
+        round_u(last, 1, True)
+        quant_u(last, 0)
+        round_u(last, 2, True)
+        quant_u(last, 1)
+        round_u(last, 3, True)
+        quant_u(last, 2)
+        quant_u(last, 3)
+        scale_u(last)
 
-        s2_banks, vg, vc, vs, s3_banks, sig = {}, {}, {}, {}, {}, {}
+        s2_banks, vg, vc, vs, s3_banks, sig, o_tiles = {}, {}, {}, {}, {}, {}, {}
 
         def stage2(n):
-            bank = psum.tile([P, 4, P], F32, name="s2", tag="bank_a", bufs=3)
+            bank = psum_bank(4 + n % 2)
             for a in range(4):
+                cols = slice(P * a, P * (a + 1))
                 for g in range(GROUPS):
-                    cols = slice(P * a, P * (a + 1))
+                    word = (T // 2) * g + P * (n % 8)
                     first = T * g + P * n
                     nc.tensor.matmul_mx(
-                        out=bank[:, a],
+                        out=bank[:, cols],
                         lhsT=uc[g][:, cols].bitcast(FP8X4),
                         lhsT_scale=us[g][:, cols],
-                        rhs=mix_sb[:, 2 * first : 2 * (first + P)].bitcast(FP4X4),
+                        rhs=mix_sb[n // 8][:, 2 * word : 2 * (word + P)].bitcast(FP4X4),
                         rhs_scale=mix_sc[:, first : first + P],
                         start=(g == 0),
                         stop=(g == GROUPS - 1),
                     )
             s2_banks[n] = bank
 
-        def f_v(n):
-            vg[n] = work.tile([P, P, 4], BF16, name="vg", bufs=3, align_bytes=64)
-            col = P * (n % 4)
+        def add_w(n):
+            vg[n] = work.tile([P, P * 4], BF16, name="vg", bufs=3, align_bytes=64)
+            col = 4 * P * (n % 4)
             nc.vector.tensor_tensor(
-                out=vg[n][:],
-                in0=s2_banks[n][:].rearrange("m a n -> m n a"),
-                in1=w_t[n // 4][:, :, col : col + P].rearrange("m a n -> m n a"),
+                out=vg[n][:].rearrange("m (n a) -> m n a", a=4),
+                in0=s2_banks[n][:].rearrange("m (a n) -> m n a", a=4),
+                in1=w_t[n // 4][:, col : col + 4 * P].rearrange("m (n a) -> m n a", a=4),
                 op=ADD,
             )
 
-        def h_v(n):
+        def quant_v(n):
             vc[n] = work.tile([P, P], U32, name="vc", bufs=3, align_bytes=64)
             vs[n] = work.tile([P, P], U8, name="vs", bufs=3, align_bytes=64)
-            nc.vector.quantize_mx(
-                out=vc[n][:].bitcast(FP8X4), scales=vs[n][:], in_=vg[n][:].rearrange("m n a -> m (n a)")
-            )
+            nc.vector.quantize_mx(out=vc[n][:].bitcast(FP8X4), scales=vs[n][:], in_=vg[n][:])
 
         def stage3(n):
-            for h, tag, bufs in ((0, "bank_b", 2), (1, "bank_c", 3)):
-                bank = psum.tile([P, 512], F32, name="s3", tag=tag, bufs=bufs)
+            for h in range(2):
+                bank = psum_bank(2 * (n % 2) + h)
                 nc.tensor.matmul_mx(
                     out=bank[:],
                     lhsT=vc[n][:].bitcast(FP8X4),
@@ -262,40 +303,40 @@ def tile_low_rank_row_mixer_t2_kernel(
                 )
                 s3_banks[n, h] = bank
 
-        def i_gate(n):
-            sig[n] = work.tile([P, D], F32, name="sig", bufs=3)
-            nc.scalar.activation(sig[n][:], gate_sb[n // 4][:, n % 4], SIGMOID)
+        def sigmoid_gate(n):
+            sig[n] = work.tile([P, D], F32, name="sig", bufs=4)
+            nc.scalar.activation(sig[n][:], gate_sb[n], SIGMOID)
 
-        o_tiles = {}
-
-        def j_out(n, h):
+        def gate_out(n, h):
             if h == 0:
-                o_tiles[n] = work.tile([P, D], F32, name="o", bufs=3)
+                o_tiles[n] = work.tile([P, D], F32, name="o", bufs=4)
             cols = slice(512 * h, 512 * (h + 1))
-            if h == 1 and n in SG:
-                z = work.tile([P, 512], F32, name="z", bufs=2)
-                nc.scalar.copy(out=z[:], in_=s3_banks[n, h][:])
-                nc.gpsimd.tensor_tensor(out=o_tiles[n][:, cols], in0=z[:], in1=sig[n][:, cols], op=MULT)
-            else:
-                nc.vector.tensor_tensor(out=o_tiles[n][:, cols], in0=s3_banks[n, h][:], in1=sig[n][:, cols], op=MULT)
+            nc.vector.tensor_tensor(out=o_tiles[n][:, cols], in0=s3_banks[n, h][:], in1=sig[n][:, cols], op=MULT)
+            rows = slice(P * n, P * (n + 1))
+            if n == BLOCKS - 1:
+                nc.sync.dma_start(out=out[rows, cols], in_=o_tiles[n][:, cols])
+            elif h == 1:
+                nc.sync.dma_start(out=out[rows, :], in_=o_tiles[n][:])
 
-        for n in range(BLOCKS + 1):
+        for n in range(BLOCKS + 3):
+            g, phase = n // 4 + 1, n % 4
             if n < BLOCKS:
                 stage2(n)
-            if n >= 1:
-                stage3(n - 1)
-            if n < BLOCKS:
-                i_gate(n)
-                f_v(n)
-            if n in (0, BLOCKS - 1) or n - 1 in SG:
-                if n < BLOCKS:
-                    h_v(n)
-                if n >= 1:
-                    j_out(n - 1, 0)
-            else:
-                j_out(n - 1, 0)
-                if n < BLOCKS:
-                    h_v(n)
-            if n >= 1:
-                j_out(n - 1, 1)
-                nc.sync.dma_start(out=out[P * (n - 1) : P * n, :], in_=o_tiles[n - 1][:])
+            if 2 <= n < BLOCKS + 2:
+                stage3(n - 2)
+            if g < GROUPS and phase in (1, 2):
+                for i in range(2):
+                    turn_w(g, 2 * (phase - 1) + i, 6 + i)
+            if 1 <= n < BLOCKS + 1:
+                add_w(n - 1)
+            if g < GROUPS and phase in (1, 2):
+                for i in range(2):
+                    copy_w(g, 2 * (phase - 1) + i)
+            if 1 <= n < BLOCKS + 1:
+                sigmoid_gate(n - 1)
+            if n >= 3:
+                gate_out(n - 3, 0)
+            if 1 <= n < BLOCKS + 1:
+                quant_v(n - 1)
+            if n >= 3:
+                gate_out(n - 3, 1)

@@ -21,6 +21,8 @@ P = 128
 GROUPS = T // 512
 BLOCKS = T // P
 STEPS = 2 * GROUPS
+SHARED = ()
+CLOSE = 11
 
 
 def tile_low_rank_row_mixer_t2_kernel(
@@ -53,11 +55,10 @@ def tile_low_rank_row_mixer_t2_kernel(
         gate_rows = gate.rearrange("(n p) c -> p n c", p=P)
 
         down_sc = scale_plane(2 * R, "down_sc")
-        mix_sc = scale_plane(4 * T, "mix_sc")
-        up_sc = scale_plane(D, "up_sc")
         warm = const.tile([P, 1], F32, name="warm")
         nc.vector.memset(warm[:], 0.0)
-        nc.scalar.activation(warm[:], warm[:], SIGMOID)
+        mix_sc = scale_plane(4 * T, "mix_sc")
+        up_sc = scale_plane(D, "up_sc")
         ident = const.tile([P, P], F32, name="ident")
         make_identity(nc, ident[:])
 
@@ -96,14 +97,15 @@ def tile_low_rank_row_mixer_t2_kernel(
         down_sb = const.tile([P, 2 * 2 * R], U8, name="down_sb", align_bytes=64)
         up_sb = const.tile([P, 2 * D], U8, name="up_sb", align_bytes=64)
 
+        nc.scalar.activation(warm[:], warm[:], SIGMOID)
         load_x(0, 0, 1)
         load_x(0, 1, 1)
+        load_x(0, 2, 2)
         nc.sync.dma_start(
             out=down_sb[:].bitcast(I32).rearrange("p (g n) -> p g n", g=2),
             in_=down_words.bitcast(I32).rearrange("g p n -> p g n"),
         )
         load_scales(nc.sync, down_sc, down_scales, 2)
-        load_x(0, 2, 2)
         load_pos(0)
         for g in range(1, GROUPS):
             load_x(g, 0, 2)
@@ -173,26 +175,31 @@ def tile_low_rank_row_mixer_t2_kernel(
                 op=ADD,
             )
 
-        def round_u(g, a, on_vector):
-            ug[g, a] = work.tile([P, P, 4], BF16, name="ug", bufs=8, align_bytes=64)
-            src = u[g][:, :, P * a : P * (a + 1)].rearrange("p t c -> p c t")
-            copy = nc.vector.tensor_copy if on_vector else nc.scalar.copy
-            copy(out=ug[g, a][:], in_=src)
+        def round_u(g, a, engine):
+            if a == 0:
+                ug[g] = work.tile([P, 4 * R], BF16, name="ug", bufs=2, align_bytes=64)
+            dst = ug[g][:, 4 * P * a : 4 * P * (a + 1)].rearrange("p (c i t) -> p c t i", t=4, i=4)
+            src = u[g][:, :, P * a : P * (a + 1)].rearrange("p t (c i) -> p c t i", i=4)
+            if engine == "gpsimd":
+                nc.gpsimd.tensor_scalar(out=dst, in0=src, scalar1=1.0, scalar2=0.0, op0=MULT, op1=ADD)
+            elif engine == "vector":
+                nc.vector.tensor_copy(out=dst, in_=src)
+            else:
+                nc.scalar.copy(out=dst, in_=src)
 
-        def quant_u(g, a):
+        def quant_u(g, a, count):
             if a == 0:
                 uc[g] = const.tile([P, R], U32, name="uc%d" % g, align_bytes=64)
                 us[g] = const.tile([P, R], U8, name="us%d" % g, align_bytes=64)
-            cols = slice(P * a, P * (a + 1))
+            cols = slice(P * a, P * (a + count))
             nc.vector.quantize_mx(
-                out=uc[g][:, cols].bitcast(FP8X4), scales=us[g][:, cols], in_=ug[g, a][:].rearrange("p c t -> p (c t)")
+                out=uc[g][:, cols].bitcast(FP8X4), scales=us[g][:, cols], in_=ug[g][:, 4 * P * a : 4 * P * (a + count)]
             )
 
-        def scale_u(g):
-            for t in range(4):
-                nc.gpsimd.tensor_scalar(
-                    out=u[g][:, t], in0=u[g][:, t], scalar1=keep_f[:, g, t : t + 1], scalar2=0.0, op0=MULT, op1=ADD
-                )
+        def scale_u(g, t):
+            nc.vector.tensor_scalar(
+                out=u[g][:, t], in0=u[g][:, t], scalar1=keep_f[:, g, t : t + 1], scalar2=None, op0=MULT
+            )
 
         def turn_w(g, t, index):
             bank = psum_bank(index)
@@ -212,6 +219,7 @@ def tile_low_rank_row_mixer_t2_kernel(
         last = GROUPS - 1
         for j in range(STEPS + 1):
             g, late = (j - 3) // 2, (j - 3) % 2
+            ready = j >= 3
             if j < STEPS:
                 turn_x(j)
             if j >= 1:
@@ -219,40 +227,45 @@ def tile_low_rank_row_mixer_t2_kernel(
             if j < STEPS:
                 copy_x(j, 0)
                 copy_x(j, 1)
-            if j >= 2:
-                add_pos(j - 2, 0)
-                add_pos(j - 2, 1)
-            if j >= 3 and not late:
-                round_u(g, 0, False)
-                round_u(g, 1, False)
-            if j >= 3 and late:
-                round_u(g, 2, False)
-                round_u(g, 3, True)
             if j < STEPS:
                 quant_x(j, 0)
-            if j >= 3 and late:
-                quant_u(g, 0)
-                quant_u(g, 1)
+            if ready and not late:
+                round_u(g, 0, "vector" if g < last - 1 else "scalar")
+                round_u(g, 1, "scalar")
+                if g < last - 1:
+                    round_u(g, 2, "scalar")
+            if ready and late:
+                if g == last - 1:
+                    round_u(g, 2, "scalar")
+                round_u(g, 3, "scalar")
             if j < STEPS:
                 quant_x(j, 1)
-            if j >= 3 and late:
-                scale_u(g)
-                quant_u(g, 3)
-                quant_u(g, 2)
+            if ready and late:
+                quant_u(g, 0, 2)
+            if j >= 1:
+                add_pos(j - 1, 0)
+            if ready and late and g < last - 1:
+                quant_u(g, 2, 2)
+            if j in (5, 7):
+                scale_u(0, j - 5)
+                scale_u(0, j - 4)
+            if j >= 1:
+                add_pos(j - 1, 1)
+        quant_u(last - 1, 2, 2)
         for t in range(4):
             turn_w(0, t, t)
-            copy_w(0, t)
-        add_pos(STEPS - 1, 0)
-        add_pos(STEPS - 1, 1)
-        round_u(last, 0, True)
-        round_u(last, 1, True)
-        quant_u(last, 0)
-        round_u(last, 2, True)
-        quant_u(last, 1)
-        round_u(last, 3, True)
-        quant_u(last, 2)
-        quant_u(last, 3)
-        scale_u(last)
+        copy_w(0, 0)
+        copy_w(0, 1)
+        round_u(last, 0, "vector")
+        round_u(last, 2, "scalar")
+        round_u(last, 1, "vector")
+        quant_u(last, 0, 1)
+        round_u(last, 3, "vector")
+        quant_u(last, 1, 1)
+        quant_u(last, 2, 1)
+        quant_u(last, 3, 1)
+        copy_w(0, 2)
+        copy_w(0, 3)
 
         s2_banks, vg, vc, vs, s3_banks, sig, o_tiles = {}, {}, {}, {}, {}, {}, {}
 
@@ -304,39 +317,60 @@ def tile_low_rank_row_mixer_t2_kernel(
                 s3_banks[n, h] = bank
 
         def sigmoid_gate(n):
-            sig[n] = work.tile([P, D], F32, name="sig", bufs=4)
+            sig[n] = work.tile([P, D], F32, name="sig", bufs=5)
             nc.scalar.activation(sig[n][:], gate_sb[n], SIGMOID)
 
         def gate_out(n, h):
             if h == 0:
                 o_tiles[n] = work.tile([P, D], F32, name="o", bufs=4)
             cols = slice(512 * h, 512 * (h + 1))
-            nc.vector.tensor_tensor(out=o_tiles[n][:, cols], in0=s3_banks[n, h][:], in1=sig[n][:, cols], op=MULT)
+            if h == 1 and n in SHARED:
+                z = work.tile([P, 512], F32, name="z", bufs=2)
+                nc.scalar.copy(out=z[:], in_=s3_banks[n, h][:])
+                nc.gpsimd.tensor_tensor(out=o_tiles[n][:, cols], in0=z[:], in1=sig[n][:, cols], op=MULT)
+            else:
+                nc.vector.tensor_tensor(out=o_tiles[n][:, cols], in0=s3_banks[n, h][:], in1=sig[n][:, cols], op=MULT)
             rows = slice(P * n, P * (n + 1))
-            if n == BLOCKS - 1:
+            if n >= BLOCKS - 2:
                 nc.sync.dma_start(out=out[rows, cols], in_=o_tiles[n][:, cols])
             elif h == 1:
                 nc.sync.dma_start(out=out[rows, :], in_=o_tiles[n][:])
 
-        for n in range(BLOCKS + 3):
+        def vector_step(fresh, old):
+            if fresh is not None:
+                add_w(fresh)
+            if old is not None:
+                gate_out(old, 0)
+            if fresh is not None:
+                quant_v(fresh)
+            if old is not None:
+                gate_out(old, 1)
+
+        sigmoid_gate(0)
+        for n in range(BLOCKS + 1):
             g, phase = n // 4 + 1, n % 4
+            turns = [2 * (phase - 2), 2 * (phase - 2) + 1] if g < GROUPS and phase >= 2 else []
+            far = n <= CLOSE
+            third = n - 2 if far else n - 1
             if n < BLOCKS:
                 stage2(n)
-            if 2 <= n < BLOCKS + 2:
-                stage3(n - 2)
-            if g < GROUPS and phase in (1, 2):
-                for i in range(2):
-                    turn_w(g, 2 * (phase - 1) + i, 6 + i)
-            if 1 <= n < BLOCKS + 1:
-                add_w(n - 1)
-            if g < GROUPS and phase in (1, 2):
-                for i in range(2):
-                    copy_w(g, 2 * (phase - 1) + i)
-            if 1 <= n < BLOCKS + 1:
-                sigmoid_gate(n - 1)
-            if n >= 3:
-                gate_out(n - 3, 0)
-            if 1 <= n < BLOCKS + 1:
-                quant_v(n - 1)
-            if n >= 3:
-                gate_out(n - 3, 1)
+            if third >= 0:
+                stage3(third)
+            for i, t in enumerate(turns):
+                turn_w(g, t, 6 + i)
+                copy_w(g, t)
+            if n + 1 < BLOCKS:
+                sigmoid_gate(n + 1)
+            if far:
+                vector_step(n - 1 if n >= 1 else None, n - 3 if n >= 3 else None)
+            else:
+                vector_step(n if n < BLOCKS else None, n - 1)
+            if n < GROUPS - 1:
+                for t in range(4):
+                    scale_u(n + 1, t)
+            if n == CLOSE:
+                if n >= 1:
+                    stage3(n - 1)
+                vector_step(n, n - 2 if n >= 2 else None)
+                if n >= 1:
+                    vector_step(None, n - 1)

@@ -10,6 +10,7 @@ F32 = mybir.dt.float32
 BF16 = mybir.dt.bfloat16
 I32 = mybir.dt.int32
 U32 = mybir.dt.uint32
+U16 = mybir.dt.uint16
 U8 = mybir.dt.uint8
 FP8X4 = mybir.dt.float8_e4m3fn_x4
 FP4X4 = mybir.dt.float4_e2m1fn_x4
@@ -21,8 +22,8 @@ P = 128
 GROUPS = T // 512
 BLOCKS = T // P
 STEPS = 2 * GROUPS
-SHARED = ()
-CLOSE = 11
+SHARED = (2, 4, 6, 8, 10)
+EARLY = 4
 
 
 def tile_low_rank_row_mixer_t2_kernel(
@@ -52,12 +53,15 @@ def tile_low_rank_row_mixer_t2_kernel(
 
         x_rows = x.rearrange("(g p t) k -> g p t k", p=P, t=4)
         pos_rows = pos.rearrange("(g p t) r -> g p t r", p=P, t=4)
-        gate_rows = gate.rearrange("(n p) c -> p n c", p=P)
+        gate_rows = gate.rearrange("(g p t) c -> g p t c", p=P, t=4)
+        out_rows = out.rearrange("(g p t) c -> g t p c", p=P, t=4)
 
         down_sc = scale_plane(2 * R, "down_sc")
         warm = const.tile([P, 1], F32, name="warm")
         nc.vector.memset(warm[:], 0.0)
-        mix_sc = scale_plane(4 * T, "mix_sc")
+        packed_sc = scale_plane(T, "packed_sc")
+        mix_sc = scale_plane(3 * T, "mix_sc")
+        dealt_sc = const.tile([P, T], U8, name="dealt_sc", align_bytes=64)
         up_sc = scale_plane(D, "up_sc")
         ident = const.tile([P, P], F32, name="ident")
         make_identity(nc, ident[:])
@@ -67,10 +71,10 @@ def tile_low_rank_row_mixer_t2_kernel(
         keep_f = const.tile([P, GROUPS, 4], F32, name="keep_f")
         nc.gpsimd.tensor_copy(out=keep_f[:], in_=keep_bf[:])
 
-        x_sb, pos_sb, gate_sb, mix_sb = {}, {}, {}, {}
+        x_sb, pos_sb, gate_sb, mix_sb, mix_raw = {}, {}, {}, {}, {}
 
         def load_x(g, first, count):
-            rows = const.tile([P, count * D], BF16, name="x%d_%d" % (g, first))
+            rows = work.tile([P, count * D], BF16, name="x", tag="rows", bufs=9)
             nc.sync.dma_start(
                 out=rows[:].rearrange("p (t k) -> p t k", t=count), in_=x_rows[g][:, first : first + count]
             )
@@ -83,16 +87,48 @@ def tile_low_rank_row_mixer_t2_kernel(
 
         def load_gate(first, count):
             rows = const.tile([P, count, D], BF16, name="gate%d" % first)
-            nc.sync.dma_start(out=rows[:], in_=gate_rows[:, first : first + count])
+            nc.sync.dma_start(out=rows[:], in_=gate_rows[first // 4][:, first % 4 : first % 4 + count])
             for n in range(count):
                 gate_sb[first + n] = rows[:, n]
 
-        def load_mix(half):
-            mix_sb[half] = const.tile([P, GROUPS * T], U8, name="mix%d" % half, align_bytes=64)
+        def load_mix(g):
+            mix_raw[g] = work.tile([P, GROUPS * 1024], U8, name="mix_raw", bufs=3, align_bytes=64)
             nc.sync.dma_start(
-                out=mix_sb[half][:].bitcast(I32).rearrange("p (g n) -> p g n", g=GROUPS),
-                in_=mix_words.bitcast(I32).rearrange("g p n -> p g n")[:, :, 512 * half : 512 * (half + 1)],
+                out=mix_raw[g][:].bitcast(I32).rearrange("p (s n) -> p s n", s=GROUPS),
+                in_=mix_words.bitcast(I32).rearrange("s p n -> p s n")[:, :, 256 * g : 256 * (g + 1)],
             )
+
+        def deal_mix(g, s0, count):
+            if s0 == 0:
+                mix_sb[g] = const.tile([P, GROUPS * 1024], U8, name="mix%d" % g, align_bytes=64)
+            cols = slice(1024 * s0, 1024 * (s0 + count))
+            nc.vector.tensor_copy(
+                out=mix_sb[g][:, cols].bitcast(U16).rearrange("p (s t c i) -> p s c t i", s=count, t=4, i=8),
+                in_=mix_raw[g][:, cols].bitcast(U16).rearrange("p (s c i t) -> p s c t i", s=count, t=4, i=8),
+            )
+
+        def load_mix_scales():
+            src = mix_scales.bitcast(I32)
+            for quad in range(4):
+                nc.sync.dma_start(
+                    out=packed_sc[:].bitcast(I32)[32 * quad : 32 * quad + 16], in_=src[:, 4 * quad : 4 * quad + 4]
+                )
+
+        def deal_mix_scales(half):
+            cols = slice(1024 * half, 1024 * (half + 1))
+            nc.vector.tensor_copy(
+                out=dealt_sc[:, cols].rearrange("p (g t c i) -> p g c t i", g=2, t=4, i=16),
+                in_=packed_sc[:, cols].rearrange("p (g c i t) -> p g c t i", g=2, t=4, i=16),
+            )
+
+        def spread_mix_scales():
+            for s in range(1, GROUPS):
+                dst = mix_sc[:, T * (s - 1) : T * s].bitcast(I32)
+                for quad in range(4):
+                    row = 32 * quad
+                    nc.sync.dma_start(
+                        out=dst[row : row + 4], in_=dealt_sc[:].bitcast(I32)[row + 4 * s : row + 4 * s + 4]
+                    )
 
         down_sb = const.tile([P, 2 * 2 * R], U8, name="down_sb", align_bytes=64)
         up_sb = const.tile([P, 2 * D], U8, name="up_sb", align_bytes=64)
@@ -107,20 +143,30 @@ def tile_low_rank_row_mixer_t2_kernel(
         )
         load_scales(nc.sync, down_sc, down_scales, 2)
         load_pos(0)
-        for g in range(1, GROUPS):
-            load_x(g, 0, 2)
-            load_x(g, 2, 2)
-            load_pos(g)
-            if g == 2:
-                load_scales(nc.sync, mix_sc, mix_scales, 4)
-                load_scales(nc.sync, up_sc, up_scales, 1)
+        load_x(1, 0, 2)
+        load_x(1, 2, 2)
+        load_mix_scales()
+        load_pos(1)
+        load_x(2, 0, 2)
+        load_x(2, 2, 2)
         load_mix(0)
-        nc.sync.dma_start(out=up_sb[:].bitcast(I32), in_=up_words.bitcast(I32).rearrange("g p n -> p (g n)"))
-        load_gate(0, 2)
-        load_gate(2, 2)
-        load_mix(1)
-        for first in range(4, BLOCKS, 4):
-            load_gate(first, 4)
+        load_pos(2)
+        load_x(3, 0, 2)
+        load_x(3, 2, 2)
+        load_pos(3)
+
+        def later_loads():
+            spread_mix_scales()
+            load_scales(nc.sync, up_sc, up_scales, 1)
+            nc.sync.dma_start(out=up_sb[:].bitcast(I32), in_=up_words.bitcast(I32).rearrange("g p n -> p (g n)"))
+            load_gate(0, 2)
+            load_mix(1)
+            load_gate(2, 2)
+            load_mix(2)
+            load_gate(4, 4)
+            load_mix(3)
+            load_gate(8, 4)
+            load_gate(12, 4)
 
         xt_banks, xc, xs, xg, s1_banks, u, ug, uc, us, w_t, wt_banks = {}, {}, {}, {}, {}, {}, {}, {}, {}, {}, {}
 
@@ -169,9 +215,9 @@ def tile_low_rank_row_mixer_t2_kernel(
             if t == 0:
                 u[g] = const.tile([P, 4, R], F32, name="u%d" % g)
             nc.vector.tensor_tensor(
-                out=u[g][:, t].rearrange("p (a c i) -> p c a i", a=4, i=4),
-                in0=s1_banks[j, tt][:].rearrange("p (c i a) -> p c a i", a=4, i=4),
-                in1=pos_sb[g][:, t].rearrange("p (c i a) -> p c a i", a=4, i=4),
+                out=u[g][:, t].rearrange("p (h m e) -> p m h e", h=2, e=2),
+                in0=s1_banks[j, tt][:].rearrange("p (m h e) -> p m h e", h=2, e=2),
+                in1=pos_sb[g][:, t].rearrange("p (m h e) -> p m h e", h=2, e=2),
                 op=ADD,
             )
 
@@ -196,26 +242,6 @@ def tile_low_rank_row_mixer_t2_kernel(
                 out=uc[g][:, cols].bitcast(FP8X4), scales=us[g][:, cols], in_=ug[g][:, 4 * P * a : 4 * P * (a + count)]
             )
 
-        def scale_u(g, t):
-            nc.vector.tensor_scalar(
-                out=u[g][:, t], in0=u[g][:, t], scalar1=keep_f[:, g, t : t + 1], scalar2=None, op0=MULT
-            )
-
-        def turn_w(g, t, index):
-            bank = psum_bank(index)
-            for a in range(4):
-                cols = slice(P * a, P * (a + 1))
-                nc.tensor.transpose(bank[:, cols], u[g][:, t, cols], ident[:])
-            wt_banks[g, t] = bank
-
-        def copy_w(g, t):
-            if t == 0:
-                w_t[g] = work.tile([P, 512 * 4], F32, name="w_t", bufs=2)
-            nc.scalar.copy(
-                out=w_t[g][:].rearrange("m (p t a) -> m t p a", t=4, a=4)[:, t],
-                in_=wt_banks[g, t][:].rearrange("m (a p) -> m p a", a=4),
-            )
-
         last = GROUPS - 1
         for j in range(STEPS + 1):
             g, late = (j - 3) // 2, (j - 3) % 2
@@ -227,79 +253,80 @@ def tile_low_rank_row_mixer_t2_kernel(
             if j < STEPS:
                 copy_x(j, 0)
                 copy_x(j, 1)
+            if ready:
+                round_u(g, 2 * late, "scalar")
+                round_u(g, 2 * late + 1, "scalar")
+            if j >= 5 and not late:
+                quant_u(g - 1, 2, 2)
             if j < STEPS:
                 quant_x(j, 0)
-            if ready and not late:
-                round_u(g, 0, "vector" if g < last - 1 else "scalar")
-                round_u(g, 1, "scalar")
-                if g < last - 1:
-                    round_u(g, 2, "scalar")
-            if ready and late:
-                if g == last - 1:
-                    round_u(g, 2, "scalar")
-                round_u(g, 3, "scalar")
-            if j < STEPS:
-                quant_x(j, 1)
             if ready and late:
                 quant_u(g, 0, 2)
+            if j < STEPS:
+                quant_x(j, 1)
+            if j in (2, 3):
+                deal_mix_scales(j - 2)
+            if j == 3:
+                later_loads()
+            if j in (4, 5):
+                deal_mix(0, 2 * (j - 4), 2)
             if j >= 1:
                 add_pos(j - 1, 0)
-            if ready and late and g < last - 1:
-                quant_u(g, 2, 2)
-            if j in (5, 7):
-                scale_u(0, j - 5)
-                scale_u(0, j - 4)
-            if j >= 1:
                 add_pos(j - 1, 1)
         quant_u(last - 1, 2, 2)
-        for t in range(4):
-            turn_w(0, t, t)
-        copy_w(0, 0)
-        copy_w(0, 1)
         round_u(last, 0, "vector")
         round_u(last, 2, "scalar")
         round_u(last, 1, "vector")
-        quant_u(last, 0, 1)
-        round_u(last, 3, "vector")
-        quant_u(last, 1, 1)
-        quant_u(last, 2, 1)
-        quant_u(last, 3, 1)
-        copy_w(0, 2)
-        copy_w(0, 3)
+        round_u(last, 3, "scalar")
+        quant_u(last, 0, 2)
+        quant_u(last, 2, 2)
 
-        s2_banks, vg, vc, vs, s3_banks, sig, o_tiles = {}, {}, {}, {}, {}, {}, {}
+        s2_banks, vb, vt_banks, vg, vc, vs, s3_banks, sig, o_tiles = {}, {}, [], {}, {}, {}, {}, {}, {}
 
-        def stage2(n):
-            bank = psum_bank(4 + n % 2)
-            for a in range(4):
-                cols = slice(P * a, P * (a + 1))
-                for g in range(GROUPS):
-                    word = (T // 2) * g + P * (n % 8)
-                    first = T * g + P * n
-                    nc.tensor.matmul_mx(
-                        out=bank[:, cols],
-                        lhsT=uc[g][:, cols].bitcast(FP8X4),
-                        lhsT_scale=us[g][:, cols],
-                        rhs=mix_sb[n // 8][:, 2 * word : 2 * (word + P)].bitcast(FP4X4),
-                        rhs_scale=mix_sc[:, first : first + P],
-                        start=(g == 0),
-                        stop=(g == GROUPS - 1),
-                    )
-            s2_banks[n] = bank
+        def stage2(n, sources):
+            g, t = divmod(n, 4)
+            if sources[0] == 0:
+                s2_banks[n] = psum_bank(n if n < EARLY else 4 + n % 2)
+            for s in sources:
+                word = 512 * s + P * t
+                plane = dealt_sc[:] if s == 0 else mix_sc[:, T * (s - 1) : T * s]
+                nc.tensor.matmul_mx(
+                    out=s2_banks[n][:],
+                    lhsT=mix_sb[g][:, 2 * word : 2 * (word + P)].bitcast(FP4X4),
+                    lhsT_scale=plane[:, P * n : P * (n + 1)],
+                    rhs=uc[s][:].bitcast(FP8X4),
+                    rhs_scale=us[s][:],
+                    start=(s == 0),
+                    stop=(s == GROUPS - 1),
+                )
 
-        def add_w(n):
-            vg[n] = work.tile([P, P * 4], BF16, name="vg", bufs=3, align_bytes=64)
-            col = 4 * P * (n % 4)
-            nc.vector.tensor_tensor(
-                out=vg[n][:].rearrange("m (n a) -> m n a", a=4),
-                in0=s2_banks[n][:].rearrange("m (a n) -> m n a", a=4),
-                in1=w_t[n // 4][:, col : col + 4 * P].rearrange("m (n a) -> m n a", a=4),
-                op=ADD,
+        def add_u(n):
+            g, t = divmod(n, 4)
+            vb[n] = work.tile([P, R], BF16, name="vb", bufs=4)
+            nc.vector.scalar_tensor_tensor(
+                out=vb[n][:], in0=u[g][:, t], scalar=keep_f[:, g, t : t + 1], in1=s2_banks[n][:], op0=MULT, op1=ADD
             )
 
+        def turn_v(tiles):
+            bank = psum_bank(6 + len(vt_banks) % 2)
+            vt_banks.append(bank)
+            for i, n in enumerate(tiles):
+                words = vb[n][:].bitcast(F32)
+                for h in range(2):
+                    col = P * (2 * i + h)
+                    nc.tensor.transpose(bank[:, col : col + P], words[:, P * h : P * (h + 1)], ident[:])
+
+        def copy_v(tiles):
+            for i, n in enumerate(tiles):
+                vg[n] = work.tile([P, P * 4], BF16, name="vg", bufs=4, align_bytes=64)
+                nc.scalar.copy(
+                    out=vg[n][:].bitcast(F32).rearrange("m (n h) -> m n h", h=2),
+                    in_=vt_banks[-1][:, 2 * P * i : 2 * P * (i + 1)].rearrange("m (h n) -> m n h", h=2),
+                )
+
         def quant_v(n):
-            vc[n] = work.tile([P, P], U32, name="vc", bufs=3, align_bytes=64)
-            vs[n] = work.tile([P, P], U8, name="vs", bufs=3, align_bytes=64)
+            vc[n] = work.tile([P, P], U32, name="vc", bufs=4, align_bytes=64)
+            vs[n] = work.tile([P, P], U8, name="vs", bufs=4, align_bytes=64)
             nc.vector.quantize_mx(out=vc[n][:].bitcast(FP8X4), scales=vs[n][:], in_=vg[n][:])
 
         def stage3(n):
@@ -317,60 +344,99 @@ def tile_low_rank_row_mixer_t2_kernel(
                 s3_banks[n, h] = bank
 
         def sigmoid_gate(n):
-            sig[n] = work.tile([P, D], F32, name="sig", bufs=5)
+            sig[n] = work.tile([P, D], F32, name="sig", bufs=6)
             nc.scalar.activation(sig[n][:], gate_sb[n], SIGMOID)
 
         def gate_out(n, h):
             if h == 0:
-                o_tiles[n] = work.tile([P, D], F32, name="o", bufs=4)
+                o_tiles[n] = work.tile([P, D], F32, name="o", tag="rows", bufs=9)
             cols = slice(512 * h, 512 * (h + 1))
-            if h == 1 and n in SHARED:
+            if h == 0 and n in SHARED:
                 z = work.tile([P, 512], F32, name="z", bufs=2)
                 nc.scalar.copy(out=z[:], in_=s3_banks[n, h][:])
                 nc.gpsimd.tensor_tensor(out=o_tiles[n][:, cols], in0=z[:], in1=sig[n][:, cols], op=MULT)
             else:
                 nc.vector.tensor_tensor(out=o_tiles[n][:, cols], in0=s3_banks[n, h][:], in1=sig[n][:, cols], op=MULT)
-            rows = slice(P * n, P * (n + 1))
-            if n >= BLOCKS - 2:
-                nc.sync.dma_start(out=out[rows, cols], in_=o_tiles[n][:, cols])
+            rows = out_rows[n // 4][n % 4]
+            if n >= BLOCKS - 4:
+                nc.sync.dma_start(out=rows[:, cols], in_=o_tiles[n][:, cols])
             elif h == 1:
-                nc.sync.dma_start(out=out[rows, :], in_=o_tiles[n][:])
+                nc.sync.dma_start(out=rows, in_=o_tiles[n][:])
 
-        def vector_step(fresh, old):
-            if fresh is not None:
-                add_w(fresh)
-            if old is not None:
-                gate_out(old, 0)
-            if fresh is not None:
-                quant_v(fresh)
-            if old is not None:
-                gate_out(old, 1)
-
+        every = list(range(GROUPS))
+        for s in range(GROUPS - 1):
+            for n in range(EARLY):
+                stage2(n, [s])
         sigmoid_gate(0)
-        for n in range(BLOCKS + 1):
-            g, phase = n // 4 + 1, n % 4
-            turns = [2 * (phase - 2), 2 * (phase - 2) + 1] if g < GROUPS and phase >= 2 else []
-            far = n <= CLOSE
-            third = n - 2 if far else n - 1
-            if n < BLOCKS:
-                stage2(n)
-            if third >= 0:
-                stage3(third)
-            for i, t in enumerate(turns):
-                turn_w(g, t, 6 + i)
-                copy_w(g, t)
-            if n + 1 < BLOCKS:
-                sigmoid_gate(n + 1)
-            if far:
-                vector_step(n - 1 if n >= 1 else None, n - 3 if n >= 3 else None)
-            else:
-                vector_step(n if n < BLOCKS else None, n - 1)
-            if n < GROUPS - 1:
-                for t in range(4):
-                    scale_u(n + 1, t)
-            if n == CLOSE:
-                if n >= 1:
-                    stage3(n - 1)
-                vector_step(n, n - 2 if n >= 2 else None)
-                if n >= 1:
-                    vector_step(None, n - 1)
+        sigmoid_gate(1)
+        sigmoid_gate(2)
+        deal_mix(1, 0, 2)
+        deal_mix(1, 2, 2)
+        for n in range(EARLY):
+            stage2(n, [last])
+        stage2(4, every)
+        add_u(0)
+        add_u(1)
+        turn_v([0, 1])
+        copy_v([0, 1])
+        sigmoid_gate(3)
+        stage2(5, every)
+        add_u(2)
+        add_u(3)
+        deal_mix(2, 0, 2)
+        quant_v(0)
+        quant_v(1)
+        turn_v([2, 3])
+        copy_v([2, 3])
+        sigmoid_gate(4)
+        stage3(0)
+        stage3(1)
+        add_u(4)
+        deal_mix(2, 2, 2)
+        quant_v(2)
+        gate_out(0, 0)
+        quant_v(3)
+        gate_out(0, 1)
+        stage3(2)
+        gate_out(1, 0)
+        gate_out(1, 1)
+        sigmoid_gate(5)
+        for n in range(6, BLOCKS, 2):
+            stage2(n, every)
+            add_u(n - 1)
+            gate_out(n - 4, 0)
+            gate_out(n - 4, 1)
+            sigmoid_gate(n)
+            turn_v([n - 2, n - 1])
+            copy_v([n - 2, n - 1])
+            stage3(n - 3)
+            stage2(n + 1, every)
+            add_u(n)
+            quant_v(n - 2)
+            gate_out(n - 3, 0)
+            quant_v(n - 1)
+            gate_out(n - 3, 1)
+            sigmoid_gate(n + 1)
+            if n in (6, 8):
+                deal_mix(3, n - 6, 2)
+            if n + 2 < BLOCKS:
+                stage3(n - 2)
+        n = BLOCKS
+        turn_v([n - 2])
+        copy_v([n - 2])
+        stage3(n - 4)
+        add_u(n - 1)
+        stage3(n - 3)
+        quant_v(n - 2)
+        gate_out(n - 4, 0)
+        turn_v([n - 1])
+        copy_v([n - 1])
+        gate_out(n - 4, 1)
+        stage3(n - 2)
+        quant_v(n - 1)
+        gate_out(n - 3, 0)
+        gate_out(n - 3, 1)
+        stage3(n - 1)
+        for m in (n - 2, n - 1):
+            gate_out(m, 0)
+            gate_out(m, 1)

@@ -121,14 +121,11 @@ def tile_low_rank_row_mixer_t2_kernel(
                 in_=packed_sc[:, cols].rearrange("p (g c i t) -> p g c t i", g=2, t=4, i=16),
             )
 
-        def spread_mix_scales():
-            for s in range(1, GROUPS):
-                dst = mix_sc[:, T * (s - 1) : T * s].bitcast(I32)
-                for quad in range(4):
-                    row = 32 * quad
-                    nc.sync.dma_start(
-                        out=dst[row : row + 4], in_=dealt_sc[:].bitcast(I32)[row + 4 * s : row + 4 * s + 4]
-                    )
+        def spread_mix_scales(s):
+            dst = mix_sc[:, T * (s - 1) : T * s].bitcast(I32)
+            for quad in range(4):
+                row = 32 * quad
+                nc.sync.dma_start(out=dst[row : row + 4], in_=dealt_sc[:].bitcast(I32)[row + 4 * s : row + 4 * s + 4])
 
         down_sb = const.tile([P, 2 * 2 * R], U8, name="down_sb", align_bytes=64)
         up_sb = const.tile([P, 2 * D], U8, name="up_sb", align_bytes=64)
@@ -142,27 +139,29 @@ def tile_low_rank_row_mixer_t2_kernel(
             in_=down_words.bitcast(I32).rearrange("g p n -> p g n"),
         )
         load_scales(nc.sync, down_sc, down_scales, 2)
-        load_pos(0)
         load_x(1, 0, 2)
+        load_pos(0)
         load_x(1, 2, 2)
+        load_x(2, 0, 2)
         load_mix_scales()
         load_pos(1)
-        load_x(2, 0, 2)
         load_x(2, 2, 2)
         load_mix(0)
-        load_pos(2)
         load_x(3, 0, 2)
+        load_pos(2)
         load_x(3, 2, 2)
-        load_pos(3)
 
         def later_loads():
-            spread_mix_scales()
-            load_scales(nc.sync, up_sc, up_scales, 1)
-            nc.sync.dma_start(out=up_sb[:].bitcast(I32), in_=up_words.bitcast(I32).rearrange("g p n -> p (g n)"))
-            load_gate(0, 2)
+            spread_mix_scales(1)
+            load_pos(3)
             load_mix(1)
-            load_gate(2, 2)
+            spread_mix_scales(2)
+            load_gate(0, 2)
             load_mix(2)
+            spread_mix_scales(3)
+            nc.sync.dma_start(out=up_sb[:].bitcast(I32), in_=up_words.bitcast(I32).rearrange("g p n -> p (g n)"))
+            load_gate(2, 2)
+            load_scales(nc.sync, up_sc, up_scales, 1)
             load_gate(4, 4)
             load_mix(3)
             load_gate(8, 4)
@@ -264,15 +263,16 @@ def tile_low_rank_row_mixer_t2_kernel(
                 quant_u(g, 0, 2)
             if j < STEPS:
                 quant_x(j, 1)
-            if j in (2, 3):
-                deal_mix_scales(j - 2)
-            if j == 3:
-                later_loads()
             if j in (4, 5):
                 deal_mix(0, 2 * (j - 4), 2)
+            if j == 3:
+                deal_mix_scales(1)
+                later_loads()
             if j >= 1:
                 add_pos(j - 1, 0)
                 add_pos(j - 1, 1)
+            if j == 2:
+                deal_mix_scales(0)
         quant_u(last - 1, 2, 2)
         round_u(last, 0, "vector")
         round_u(last, 2, "scalar")

@@ -98,11 +98,14 @@ def tile_low_rank_row_mixer_t2_kernel(
                 in_=mix_words.bitcast(I32).rearrange("s p n -> p s n")[:, :, 256 * g : 256 * (g + 1)],
             )
 
+        DEALERS = [nc.gpsimd.tensor_copy, nc.vector.tensor_copy, nc.scalar.copy, nc.vector.tensor_copy]
+
         def deal_mix(g, s0, count):
             if s0 == 0:
                 mix_sb[g] = const.tile([P, GROUPS * 1024], U8, name="mix%d" % g, align_bytes=64)
             cols = slice(1024 * s0, 1024 * (s0 + count))
-            nc.vector.tensor_copy(
+            copy = DEALERS[g]
+            copy(
                 out=mix_sb[g][:, cols].bitcast(U16).rearrange("p (s t c i) -> p s c t i", s=count, t=4, i=8),
                 in_=mix_raw[g][:, cols].bitcast(U16).rearrange("p (s c i t) -> p s c t i", s=count, t=4, i=8),
             )
@@ -167,7 +170,15 @@ def tile_low_rank_row_mixer_t2_kernel(
             load_gate(8, 4)
             load_gate(12, 4)
 
+        sorted_x = {}
         xt_banks, xc, xs, xg, s1_banks, u, ug, uc, us, w_t, wt_banks = {}, {}, {}, {}, {}, {}, {}, {}, {}, {}, {}
+
+        def sort_x(j, tt):
+            sorted_x[j, tt] = work.tile([P, 512], F32, name="sorted_x", bufs=4)
+            nc.vector.tensor_copy(
+                out=sorted_x[j, tt][:].rearrange("p (k h c i) -> p k c h i", k=2, h=2, i=4),
+                in_=x_sb[j // 2, 2 * (j % 2) + tt].bitcast(F32).rearrange("p (k c i h) -> p k c h i", k=2, h=2, i=4),
+            )
 
         def turn_x(j):
             for tt in range(2):
@@ -176,9 +187,11 @@ def tile_low_rank_row_mixer_t2_kernel(
                 for kc in range(2):
                     for half in range(2):
                         col = P * (2 * kc + half)
-                        nc.tensor.transpose(
-                            bank[:, col : col + P], words[:, 256 * kc + half : 256 * (kc + 1) : 2], ident[:]
-                        )
+                        if (j, tt) in sorted_x:
+                            src = sorted_x[j, tt][:, col : col + P]
+                        else:
+                            src = words[:, 256 * kc + half : 256 * (kc + 1) : 2]
+                        nc.tensor.transpose(bank[:, col : col + P], src, ident[:])
                 xt_banks[j, tt] = bank
 
         def copy_x(j, tt):
@@ -259,18 +272,26 @@ def tile_low_rank_row_mixer_t2_kernel(
                 quant_u(g - 1, 2, 2)
             if j < STEPS:
                 quant_x(j, 0)
+            if j == 1:
+                sort_x(2, 0)
+                sort_x(2, 1)
             if ready and late:
                 quant_u(g, 0, 2)
             if j < STEPS:
                 quant_x(j, 1)
-            if j in (4, 5):
-                deal_mix(0, 2 * (j - 4), 2)
+            if j == 4:
+                for s in range(GROUPS):
+                    deal_mix(0, s, 1)
             if j == 3:
                 deal_mix_scales(1)
                 later_loads()
             if j >= 1:
                 add_pos(j - 1, 0)
+                if j == 1:
+                    sort_x(3, 0)
                 add_pos(j - 1, 1)
+                if j == 1:
+                    sort_x(3, 1)
             if j == 2:
                 deal_mix_scales(0)
         quant_u(last - 1, 2, 2)
@@ -344,7 +365,7 @@ def tile_low_rank_row_mixer_t2_kernel(
                 s3_banks[n, h] = bank
 
         def sigmoid_gate(n):
-            sig[n] = work.tile([P, D], F32, name="sig", bufs=6)
+            sig[n] = work.tile([P, D], F32, name="sig", bufs=5)
             nc.scalar.activation(sig[n][:], gate_sb[n], SIGMOID)
 
         def gate_out(n, h):
@@ -369,7 +390,7 @@ def tile_low_rank_row_mixer_t2_kernel(
                 stage2(n, [s])
         sigmoid_gate(0)
         sigmoid_gate(1)
-        sigmoid_gate(2)
+        deal_mix(2, 0, 2)
         deal_mix(1, 0, 2)
         deal_mix(1, 2, 2)
         for n in range(EARLY):
@@ -379,34 +400,33 @@ def tile_low_rank_row_mixer_t2_kernel(
         add_u(1)
         turn_v([0, 1])
         copy_v([0, 1])
-        sigmoid_gate(3)
+        sigmoid_gate(2)
         stage2(5, every)
         add_u(2)
         add_u(3)
-        deal_mix(2, 0, 2)
         quant_v(0)
         quant_v(1)
         turn_v([2, 3])
         copy_v([2, 3])
-        sigmoid_gate(4)
+        sigmoid_gate(3)
+        deal_mix(2, 2, 2)
         stage3(0)
         stage3(1)
         add_u(4)
-        deal_mix(2, 2, 2)
         quant_v(2)
         gate_out(0, 0)
         quant_v(3)
         gate_out(0, 1)
-        stage3(2)
-        gate_out(1, 0)
-        gate_out(1, 1)
-        sigmoid_gate(5)
         for n in range(6, BLOCKS, 2):
             stage2(n, every)
             add_u(n - 1)
+            if n == 6:
+                stage3(2)
+                gate_out(1, 0)
+                gate_out(1, 1)
             gate_out(n - 4, 0)
             gate_out(n - 4, 1)
-            sigmoid_gate(n)
+            sigmoid_gate(n - 2)
             turn_v([n - 2, n - 1])
             copy_v([n - 2, n - 1])
             stage3(n - 3)
@@ -416,7 +436,7 @@ def tile_low_rank_row_mixer_t2_kernel(
             gate_out(n - 3, 0)
             quant_v(n - 1)
             gate_out(n - 3, 1)
-            sigmoid_gate(n + 1)
+            sigmoid_gate(n - 1)
             if n in (6, 8):
                 deal_mix(3, n - 6, 2)
             if n + 2 < BLOCKS:
@@ -424,6 +444,7 @@ def tile_low_rank_row_mixer_t2_kernel(
         n = BLOCKS
         turn_v([n - 2])
         copy_v([n - 2])
+        sigmoid_gate(n - 2)
         stage3(n - 4)
         add_u(n - 1)
         stage3(n - 3)
@@ -431,6 +452,7 @@ def tile_low_rank_row_mixer_t2_kernel(
         gate_out(n - 4, 0)
         turn_v([n - 1])
         copy_v([n - 1])
+        sigmoid_gate(n - 1)
         gate_out(n - 4, 1)
         stage3(n - 2)
         quant_v(n - 1)

@@ -20,10 +20,13 @@ SIGMOID = mybir.ActivationFunctionType.Sigmoid
 
 P = 128
 GROUPS = T // 512
-BLOCKS = T // P
-STEPS = 2 * GROUPS
-SHARED = (2, 4, 6, 8, 10)
+TILES = T // P
+STEPS = TILES // 2
+LAST = GROUPS - 1
+BANK = 512
 EARLY = 4
+SHARED = range(2, TILES - 4, 2)
+HALVED = range(TILES - 4, TILES)
 
 
 def tile_low_rank_row_mixer_t2_kernel(
@@ -37,7 +40,7 @@ def tile_low_rank_row_mixer_t2_kernel(
         ctx.enter_context(tc.manual_schedule())
 
         def psum_bank(index):
-            bank = psum.tile([P, 512], F32, name="bank%d" % index, tag="bank%d" % index)
+            bank = psum.tile([P, BANK], F32, name="bank%d" % index, tag="bank%d" % index)
             return bank
 
         def scale_plane(width, name):
@@ -45,11 +48,11 @@ def tile_low_rank_row_mixer_t2_kernel(
             nc.vector.memset(plane[:].bitcast(I32), 0)
             return plane
 
-        def load_scales(queue, plane, scales, groups):
-            src = scales.bitcast(I32).rearrange("g q n -> q g n")
-            dst = plane[:].bitcast(I32).rearrange("p (g n) -> p g n", g=groups)
+        def load_scales(plane, scales, passes):
+            src = scales.bitcast(I32).rearrange("s q n -> q s n")
+            dst = plane[:].bitcast(I32).rearrange("p (s n) -> p s n", s=passes)
             for quad in range(4):
-                queue.dma_start(out=dst[32 * quad : 32 * quad + 4], in_=src[4 * quad : 4 * quad + 4])
+                nc.sync.dma_start(out=dst[32 * quad : 32 * quad + 4], in_=src[4 * quad : 4 * quad + 4])
 
         x_rows = x.rearrange("(g p t) k -> g p t k", p=P, t=4)
         pos_rows = pos.rearrange("(g p t) r -> g p t r", p=P, t=4)
@@ -60,7 +63,7 @@ def tile_low_rank_row_mixer_t2_kernel(
         warm = const.tile([P, 1], F32, name="warm")
         nc.vector.memset(warm[:], 0.0)
         packed_sc = scale_plane(T, "packed_sc")
-        mix_sc = scale_plane(3 * T, "mix_sc")
+        mix_sc = scale_plane(LAST * T, "mix_sc")
         dealt_sc = const.tile([P, T], U8, name="dealt_sc", align_bytes=64)
         up_sc = scale_plane(D, "up_sc")
         ident = const.tile([P, P], F32, name="ident")
@@ -73,13 +76,12 @@ def tile_low_rank_row_mixer_t2_kernel(
 
         x_sb, pos_sb, gate_sb, mix_sb, mix_raw = {}, {}, {}, {}, {}
 
-        def load_x(g, first, count):
+        def load_x(first, count):
             rows = work.tile([P, count * D], BF16, name="x", tag="rows", bufs=9)
-            nc.sync.dma_start(
-                out=rows[:].rearrange("p (t k) -> p t k", t=count), in_=x_rows[g][:, first : first + count]
-            )
-            for t in range(count):
-                x_sb[g, first + t] = rows[:, D * t : D * (t + 1)]
+            g, t = divmod(first, 4)
+            nc.sync.dma_start(out=rows[:].rearrange("p (t k) -> p t k", t=count), in_=x_rows[g][:, t : t + count])
+            for i in range(count):
+                x_sb[first + i] = rows[:, D * i : D * (i + 1)]
 
         def load_pos(g):
             pos_sb[g] = const.tile([P, 4, R], BF16, name="pos%d" % g)
@@ -87,9 +89,10 @@ def tile_low_rank_row_mixer_t2_kernel(
 
         def load_gate(first, count):
             rows = const.tile([P, count, D], BF16, name="gate%d" % first)
-            nc.sync.dma_start(out=rows[:], in_=gate_rows[first // 4][:, first % 4 : first % 4 + count])
-            for n in range(count):
-                gate_sb[first + n] = rows[:, n]
+            g, t = divmod(first, 4)
+            nc.sync.dma_start(out=rows[:], in_=gate_rows[g][:, t : t + count])
+            for i in range(count):
+                gate_sb[first + i] = rows[:, i]
 
         def load_mix(g):
             mix_raw[g] = work.tile([P, GROUPS * 1024], U8, name="mix_raw", bufs=3, align_bytes=64)
@@ -98,13 +101,10 @@ def tile_low_rank_row_mixer_t2_kernel(
                 in_=mix_words.bitcast(I32).rearrange("s p n -> p s n")[:, :, 256 * g : 256 * (g + 1)],
             )
 
-        DEALERS = [nc.gpsimd.tensor_copy, nc.vector.tensor_copy, nc.scalar.copy, nc.vector.tensor_copy]
-
-        def deal_mix(g, s0, count):
-            if s0 == 0:
+        def deal_mix(copy, g, first, count):
+            if first == 0:
                 mix_sb[g] = const.tile([P, GROUPS * 1024], U8, name="mix%d" % g, align_bytes=64)
-            cols = slice(1024 * s0, 1024 * (s0 + count))
-            copy = DEALERS[g]
+            cols = slice(1024 * first, 1024 * (first + count))
             copy(
                 out=mix_sb[g][:, cols].bitcast(U16).rearrange("p (s t c i) -> p s c t i", s=count, t=4, i=8),
                 in_=mix_raw[g][:, cols].bitcast(U16).rearrange("p (s c i t) -> p s c t i", s=count, t=4, i=8),
@@ -134,25 +134,26 @@ def tile_low_rank_row_mixer_t2_kernel(
         up_sb = const.tile([P, 2 * D], U8, name="up_sb", align_bytes=64)
 
         nc.scalar.activation(warm[:], warm[:], SIGMOID)
-        load_x(0, 0, 1)
-        load_x(0, 1, 1)
-        load_x(0, 2, 2)
+
+        load_x(0, 1)
+        load_x(1, 1)
+        load_x(2, 2)
         nc.sync.dma_start(
-            out=down_sb[:].bitcast(I32).rearrange("p (g n) -> p g n", g=2),
-            in_=down_words.bitcast(I32).rearrange("g p n -> p g n"),
+            out=down_sb[:].bitcast(I32).rearrange("p (s n) -> p s n", s=2),
+            in_=down_words.bitcast(I32).rearrange("s p n -> p s n"),
         )
-        load_scales(nc.sync, down_sc, down_scales, 2)
-        load_x(1, 0, 2)
+        load_scales(down_sc, down_scales, 2)
+        load_x(4, 2)
         load_pos(0)
-        load_x(1, 2, 2)
-        load_x(2, 0, 2)
+        load_x(6, 2)
+        load_x(8, 2)
         load_mix_scales()
         load_pos(1)
-        load_x(2, 2, 2)
+        load_x(10, 2)
         load_mix(0)
-        load_x(3, 0, 2)
+        load_x(12, 2)
         load_pos(2)
-        load_x(3, 2, 2)
+        load_x(14, 2)
 
         def later_loads():
             spread_mix_scales(1)
@@ -162,153 +163,96 @@ def tile_low_rank_row_mixer_t2_kernel(
             load_gate(0, 2)
             load_mix(2)
             spread_mix_scales(3)
-            nc.sync.dma_start(out=up_sb[:].bitcast(I32), in_=up_words.bitcast(I32).rearrange("g p n -> p (g n)"))
+            nc.sync.dma_start(out=up_sb[:].bitcast(I32), in_=up_words.bitcast(I32).rearrange("s p n -> p (s n)"))
             load_gate(2, 2)
-            load_scales(nc.sync, up_sc, up_scales, 1)
+            load_scales(up_sc, up_scales, 1)
             load_gate(4, 4)
             load_mix(3)
             load_gate(8, 4)
             load_gate(12, 4)
 
-        sorted_x = {}
-        xt_banks, xc, xs, xg, s1_banks, u, ug, uc, us, w_t, wt_banks = {}, {}, {}, {}, {}, {}, {}, {}, {}, {}, {}
+        sorted_x, xt_banks, xg, xc, xs, s1_banks, u, ug, uc, us = {}, {}, {}, {}, {}, {}, {}, {}, {}, {}
 
-        def sort_x(j, tt):
-            sorted_x[j, tt] = work.tile([P, 512], F32, name="sorted_x", bufs=4)
+        def sort_x(n):
+            sorted_x[n] = work.tile([P, 512], F32, name="sorted_x", bufs=5)
             nc.vector.tensor_copy(
-                out=sorted_x[j, tt][:].rearrange("p (k h c i) -> p k c h i", k=2, h=2, i=4),
-                in_=x_sb[j // 2, 2 * (j % 2) + tt].bitcast(F32).rearrange("p (k c i h) -> p k c h i", k=2, h=2, i=4),
+                out=sorted_x[n][:].rearrange("p (k h c i) -> p k c h i", k=2, h=2, i=4),
+                in_=x_sb[n].bitcast(F32).rearrange("p (k c i h) -> p k c h i", k=2, h=2, i=4),
             )
 
-        def turn_x(j):
-            for tt in range(2):
-                words = x_sb[j // 2, 2 * (j % 2) + tt].bitcast(F32)
-                bank = psum_bank(2 * (j % 2) + tt)
-                for kc in range(2):
-                    for half in range(2):
-                        col = P * (2 * kc + half)
-                        if (j, tt) in sorted_x:
-                            src = sorted_x[j, tt][:, col : col + P]
-                        else:
-                            src = words[:, 256 * kc + half : 256 * (kc + 1) : 2]
-                        nc.tensor.transpose(bank[:, col : col + P], src, ident[:])
-                xt_banks[j, tt] = bank
+        def turn_x(n):
+            words = x_sb[n].bitcast(F32)
+            xt_banks[n] = psum_bank(n % 4)
+            for k in range(2):
+                for h in range(2):
+                    col = P * (2 * k + h)
+                    if n in sorted_x:
+                        src = sorted_x[n][:, col : col + P]
+                    else:
+                        src = words[:, 256 * k + h : 256 * (k + 1) : 2]
+                    nc.tensor.transpose(xt_banks[n][:, col : col + P], src, ident[:])
 
-        def copy_x(j, tt):
-            xg[j, tt] = work.tile([P, 2 * P * 4], BF16, name="xg", bufs=4, align_bytes=64)
+        def copy_x(n):
+            xg[n] = work.tile([P, D], BF16, name="xg", bufs=4, align_bytes=64)
             nc.scalar.copy(
-                out=xg[j, tt][:].bitcast(F32).rearrange("p (k r h) -> p k r h", k=2, h=2),
-                in_=xt_banks[j, tt][:].rearrange("p (k h r) -> p k r h", k=2, h=2),
+                out=xg[n][:].bitcast(F32).rearrange("p (k r h) -> p k r h", k=2, h=2),
+                in_=xt_banks[n][:].rearrange("p (k h r) -> p k r h", k=2, h=2),
             )
 
-        def quant_x(j, tt):
-            xc[j, tt] = work.tile([P, 256], U32, name="xc", bufs=4, align_bytes=64)
-            xs[j, tt] = work.tile([P, 256], U8, name="xs", bufs=4, align_bytes=64)
-            nc.vector.quantize_mx(out=xc[j, tt][:].bitcast(FP8X4), scales=xs[j, tt][:], in_=xg[j, tt][:])
+        def quant_x(n):
+            xc[n] = work.tile([P, 2 * P], U32, name="xc", bufs=4, align_bytes=64)
+            xs[n] = work.tile([P, 2 * P], U8, name="xs", bufs=4, align_bytes=64)
+            nc.vector.quantize_mx(out=xc[n][:].bitcast(FP8X4), scales=xs[n][:], in_=xg[n][:])
 
-        def stage1(j):
-            for tt in range(2):
-                bank = psum_bank(4 + 2 * (j % 2) + tt)
-                for kc in range(2):
-                    cols = slice(P * kc, P * (kc + 1))
-                    nc.tensor.matmul_mx(
-                        out=bank[:],
-                        lhsT=xc[j, tt][:, cols].bitcast(FP8X4),
-                        lhsT_scale=xs[j, tt][:, cols],
-                        rhs=down_sb[:, 2 * R * kc : 2 * R * (kc + 1)].bitcast(FP4X4),
-                        rhs_scale=down_sc[:, R * kc : R * (kc + 1)],
-                        start=(kc == 0),
-                        stop=(kc == 1),
-                    )
-                s1_banks[j, tt] = bank
+        def stage1(n):
+            s1_banks[n] = psum_bank(4 + n % 4)
+            for k in range(2):
+                cols = slice(P * k, P * (k + 1))
+                nc.tensor.matmul_mx(
+                    out=s1_banks[n][:],
+                    lhsT=xc[n][:, cols].bitcast(FP8X4),
+                    lhsT_scale=xs[n][:, cols],
+                    rhs=down_sb[:, 2 * R * k : 2 * R * (k + 1)].bitcast(FP4X4),
+                    rhs_scale=down_sc[:, R * k : R * (k + 1)],
+                    start=(k == 0),
+                    stop=(k == 1),
+                )
 
-        def add_pos(j, tt):
-            g, t = j // 2, 2 * (j % 2) + tt
+        def add_pos(n):
+            g, t = divmod(n, 4)
             if t == 0:
                 u[g] = const.tile([P, 4, R], F32, name="u%d" % g)
             nc.vector.tensor_tensor(
                 out=u[g][:, t].rearrange("p (h m e) -> p m h e", h=2, e=2),
-                in0=s1_banks[j, tt][:].rearrange("p (m h e) -> p m h e", h=2, e=2),
+                in0=s1_banks[n][:].rearrange("p (m h e) -> p m h e", h=2, e=2),
                 in1=pos_sb[g][:, t].rearrange("p (m h e) -> p m h e", h=2, e=2),
                 op=ADD,
             )
 
-        def round_u(g, a, engine):
-            if a == 0:
+        def round_u(copy, g, quarter):
+            if quarter == 0:
                 ug[g] = work.tile([P, 4 * R], BF16, name="ug", bufs=2, align_bytes=64)
-            dst = ug[g][:, 4 * P * a : 4 * P * (a + 1)].rearrange("p (c i t) -> p c t i", t=4, i=4)
-            src = u[g][:, :, P * a : P * (a + 1)].rearrange("p t (c i) -> p c t i", i=4)
-            if engine == "gpsimd":
-                nc.gpsimd.tensor_scalar(out=dst, in0=src, scalar1=1.0, scalar2=0.0, op0=MULT, op1=ADD)
-            elif engine == "vector":
-                nc.vector.tensor_copy(out=dst, in_=src)
-            else:
-                nc.scalar.copy(out=dst, in_=src)
-
-        def quant_u(g, a, count):
-            if a == 0:
-                uc[g] = const.tile([P, R], U32, name="uc%d" % g, align_bytes=64)
-                us[g] = const.tile([P, R], U8, name="us%d" % g, align_bytes=64)
-            cols = slice(P * a, P * (a + count))
-            nc.vector.quantize_mx(
-                out=uc[g][:, cols].bitcast(FP8X4), scales=us[g][:, cols], in_=ug[g][:, 4 * P * a : 4 * P * (a + count)]
+            copy(
+                out=ug[g][:, R * quarter : R * (quarter + 1)].rearrange("p (c i t) -> p c t i", t=4, i=4),
+                in_=u[g][:, :, P * quarter : P * (quarter + 1)].rearrange("p t (c i) -> p c t i", i=4),
             )
 
-        last = GROUPS - 1
-        for j in range(STEPS + 1):
-            g, late = (j - 3) // 2, (j - 3) % 2
-            ready = j >= 3
-            if j < STEPS:
-                turn_x(j)
-            if j >= 1:
-                stage1(j - 1)
-            if j < STEPS:
-                copy_x(j, 0)
-                copy_x(j, 1)
-            if ready:
-                round_u(g, 2 * late, "scalar")
-                round_u(g, 2 * late + 1, "scalar")
-            if j >= 5 and not late:
-                quant_u(g - 1, 2, 2)
-            if j < STEPS:
-                quant_x(j, 0)
-            if j == 1:
-                sort_x(2, 0)
-                sort_x(2, 1)
-            if ready and late:
-                quant_u(g, 0, 2)
-            if j < STEPS:
-                quant_x(j, 1)
-            if j == 4:
-                for s in range(GROUPS):
-                    deal_mix(0, s, 1)
-            if j == 3:
-                deal_mix_scales(1)
-                later_loads()
-            if j >= 1:
-                add_pos(j - 1, 0)
-                if j == 1:
-                    sort_x(3, 0)
-                add_pos(j - 1, 1)
-                if j == 1:
-                    sort_x(3, 1)
-            if j == 2:
-                deal_mix_scales(0)
-        quant_u(last - 1, 2, 2)
-        round_u(last, 0, "vector")
-        round_u(last, 2, "scalar")
-        round_u(last, 1, "vector")
-        round_u(last, 3, "scalar")
-        quant_u(last, 0, 2)
-        quant_u(last, 2, 2)
+        def quant_u(g, half):
+            if half == 0:
+                uc[g] = const.tile([P, R], U32, name="uc%d" % g, align_bytes=64)
+                us[g] = const.tile([P, R], U8, name="us%d" % g, align_bytes=64)
+            cols = slice(256 * half, 256 * (half + 1))
+            nc.vector.quantize_mx(
+                out=uc[g][:, cols].bitcast(FP8X4), scales=us[g][:, cols], in_=ug[g][:, 1024 * half : 1024 * (half + 1)]
+            )
 
         s2_banks, vb, vt_banks, vg, vc, vs, s3_banks, sig, o_tiles = {}, {}, [], {}, {}, {}, {}, {}, {}
 
-        def stage2(n, sources):
+        def stage2(n, passes):
             g, t = divmod(n, 4)
-            if sources[0] == 0:
+            if passes[0] == 0:
                 s2_banks[n] = psum_bank(n if n < EARLY else 4 + n % 2)
-            for s in sources:
+            for s in passes:
                 word = 512 * s + P * t
                 plane = dealt_sc[:] if s == 0 else mix_sc[:, T * (s - 1) : T * s]
                 nc.tensor.matmul_mx(
@@ -318,7 +262,7 @@ def tile_low_rank_row_mixer_t2_kernel(
                     rhs=uc[s][:].bitcast(FP8X4),
                     rhs_scale=us[s][:],
                     start=(s == 0),
-                    stop=(s == GROUPS - 1),
+                    stop=(s == LAST),
                 )
 
         def add_u(n):
@@ -336,13 +280,11 @@ def tile_low_rank_row_mixer_t2_kernel(
                 for h in range(2):
                     col = P * (2 * i + h)
                     nc.tensor.transpose(bank[:, col : col + P], words[:, P * h : P * (h + 1)], ident[:])
-
-        def copy_v(tiles):
             for i, n in enumerate(tiles):
-                vg[n] = work.tile([P, P * 4], BF16, name="vg", bufs=4, align_bytes=64)
+                vg[n] = work.tile([P, R], BF16, name="vg", bufs=4, align_bytes=64)
                 nc.scalar.copy(
-                    out=vg[n][:].bitcast(F32).rearrange("m (n h) -> m n h", h=2),
-                    in_=vt_banks[-1][:, 2 * P * i : 2 * P * (i + 1)].rearrange("m (h n) -> m n h", h=2),
+                    out=vg[n][:].bitcast(F32).rearrange("m (p h) -> m p h", h=2),
+                    in_=bank[:, 2 * P * i : 2 * P * (i + 1)].rearrange("m (h p) -> m p h", h=2),
                 )
 
         def quant_v(n):
@@ -351,84 +293,134 @@ def tile_low_rank_row_mixer_t2_kernel(
             nc.vector.quantize_mx(out=vc[n][:].bitcast(FP8X4), scales=vs[n][:], in_=vg[n][:])
 
         def stage3(n):
-            for h in range(2):
-                bank = psum_bank(2 * (n % 2) + h)
+            for half in range(2):
+                s3_banks[n, half] = psum_bank(2 * (n % 2) + half)
                 nc.tensor.matmul_mx(
-                    out=bank[:],
+                    out=s3_banks[n, half][:],
                     lhsT=vc[n][:].bitcast(FP8X4),
                     lhsT_scale=vs[n][:],
-                    rhs=up_sb[:, 1024 * h : 1024 * (h + 1)].bitcast(FP4X4),
-                    rhs_scale=up_sc[:, 512 * h : 512 * (h + 1)],
+                    rhs=up_sb[:, 2 * BANK * half : 2 * BANK * (half + 1)].bitcast(FP4X4),
+                    rhs_scale=up_sc[:, BANK * half : BANK * (half + 1)],
                     start=True,
                     stop=True,
                 )
-                s3_banks[n, h] = bank
 
         def sigmoid_gate(n):
             sig[n] = work.tile([P, D], F32, name="sig", bufs=5)
             nc.scalar.activation(sig[n][:], gate_sb[n], SIGMOID)
 
-        def gate_out(n, h):
-            if h == 0:
+        def gate_out(n, half):
+            if half == 0:
                 o_tiles[n] = work.tile([P, D], F32, name="o", tag="rows", bufs=9)
-            cols = slice(512 * h, 512 * (h + 1))
-            if h == 0 and n in SHARED:
-                z = work.tile([P, 512], F32, name="z", bufs=2)
-                nc.scalar.copy(out=z[:], in_=s3_banks[n, h][:])
+            cols = slice(BANK * half, BANK * (half + 1))
+            bank = s3_banks[n, half]
+            if half == 0 and n in SHARED:
+                z = work.tile([P, BANK], F32, name="z", bufs=2)
+                nc.scalar.copy(out=z[:], in_=bank[:])
                 nc.gpsimd.tensor_tensor(out=o_tiles[n][:, cols], in0=z[:], in1=sig[n][:, cols], op=MULT)
             else:
-                nc.vector.tensor_tensor(out=o_tiles[n][:, cols], in0=s3_banks[n, h][:], in1=sig[n][:, cols], op=MULT)
+                nc.vector.tensor_tensor(out=o_tiles[n][:, cols], in0=bank[:], in1=sig[n][:, cols], op=MULT)
             rows = out_rows[n // 4][n % 4]
-            if n >= BLOCKS - 4:
+            if n in HALVED:
                 nc.sync.dma_start(out=rows[:, cols], in_=o_tiles[n][:, cols])
-            elif h == 1:
+            elif half == 1:
                 nc.sync.dma_start(out=rows, in_=o_tiles[n][:])
 
+        sort_x(1)
+        for j in range(STEPS + 1):
+            fresh = [2 * j, 2 * j + 1] if j < STEPS else []
+            before = [2 * j - 2, 2 * j - 1] if j >= 1 else []
+            rounding, quantising = divmod(j - 3, 2), divmod(j - 4, 2)
+            for n in fresh:
+                turn_x(n)
+            for n in before:
+                stage1(n)
+            for n in fresh:
+                copy_x(n)
+            if j >= 3:
+                g, half = rounding
+                round_u(nc.scalar.copy, g, 2 * half)
+                round_u(nc.scalar.copy, g, 2 * half + 1)
+            if j >= 4 and quantising[1] == 1:
+                quant_u(*quantising)
+            if j == 0:
+                sort_x(3)
+            for n in fresh[:1]:
+                quant_x(n)
+            if j == 1:
+                sort_x(4)
+                sort_x(5)
+            if j >= 4 and quantising[1] == 0:
+                quant_u(*quantising)
+            for n in fresh[1:]:
+                quant_x(n)
+            if j == 3:
+                deal_mix_scales(1)
+                later_loads()
+            if j == 4:
+                for s in range(GROUPS):
+                    deal_mix(nc.gpsimd.tensor_copy, 0, s, 1)
+            for n in before:
+                add_pos(n)
+                if j == 1:
+                    sort_x(6 + n)
+            if j == 2:
+                deal_mix_scales(0)
+
+        quant_u(LAST - 1, 1)
+        round_u(nc.vector.tensor_copy, LAST, 0)
+        round_u(nc.scalar.copy, LAST, 2)
+        round_u(nc.vector.tensor_copy, LAST, 1)
+        round_u(nc.scalar.copy, LAST, 3)
+        quant_u(LAST, 0)
+        quant_u(LAST, 1)
+
         every = list(range(GROUPS))
-        for s in range(GROUPS - 1):
+        for s in range(LAST):
             for n in range(EARLY):
                 stage2(n, [s])
         sigmoid_gate(0)
         sigmoid_gate(1)
-        deal_mix(2, 0, 2)
-        deal_mix(1, 0, 2)
-        deal_mix(1, 2, 2)
+        deal_mix(nc.scalar.copy, 2, 0, 2)
+        deal_mix(nc.vector.tensor_copy, 1, 0, 2)
+        deal_mix(nc.vector.tensor_copy, 1, 2, 2)
         for n in range(EARLY):
-            stage2(n, [last])
+            stage2(n, [LAST])
         stage2(4, every)
         add_u(0)
         add_u(1)
         turn_v([0, 1])
-        copy_v([0, 1])
         sigmoid_gate(2)
         stage2(5, every)
         add_u(2)
         add_u(3)
+        deal_mix(nc.vector.tensor_copy, 3, 0, 2)
         quant_v(0)
         quant_v(1)
         turn_v([2, 3])
-        copy_v([2, 3])
         sigmoid_gate(3)
-        deal_mix(2, 2, 2)
+        deal_mix(nc.scalar.copy, 2, 2, 2)
         stage3(0)
         stage3(1)
         add_u(4)
+        deal_mix(nc.vector.tensor_copy, 3, 2, 2)
         quant_v(2)
         gate_out(0, 0)
         quant_v(3)
         gate_out(0, 1)
-        for n in range(6, BLOCKS, 2):
+
+        first_round, last_round = EARLY + 2, TILES - 2
+        for n in range(first_round, TILES, 2):
             stage2(n, every)
             add_u(n - 1)
-            if n == 6:
-                stage3(2)
-                gate_out(1, 0)
-                gate_out(1, 1)
+            if n == first_round:
+                stage3(n - 4)
+                gate_out(n - 5, 0)
+                gate_out(n - 5, 1)
             gate_out(n - 4, 0)
             gate_out(n - 4, 1)
             sigmoid_gate(n - 2)
             turn_v([n - 2, n - 1])
-            copy_v([n - 2, n - 1])
             stage3(n - 3)
             stage2(n + 1, every)
             add_u(n)
@@ -437,13 +429,11 @@ def tile_low_rank_row_mixer_t2_kernel(
             quant_v(n - 1)
             gate_out(n - 3, 1)
             sigmoid_gate(n - 1)
-            if n in (6, 8):
-                deal_mix(3, n - 6, 2)
-            if n + 2 < BLOCKS:
+            if n < last_round:
                 stage3(n - 2)
-        n = BLOCKS
+
+        n = TILES
         turn_v([n - 2])
-        copy_v([n - 2])
         sigmoid_gate(n - 2)
         stage3(n - 4)
         add_u(n - 1)
@@ -451,7 +441,6 @@ def tile_low_rank_row_mixer_t2_kernel(
         quant_v(n - 2)
         gate_out(n - 4, 0)
         turn_v([n - 1])
-        copy_v([n - 1])
         sigmoid_gate(n - 1)
         gate_out(n - 4, 1)
         stage3(n - 2)
@@ -459,6 +448,6 @@ def tile_low_rank_row_mixer_t2_kernel(
         gate_out(n - 3, 0)
         gate_out(n - 3, 1)
         stage3(n - 1)
-        for m in (n - 2, n - 1):
-            gate_out(m, 0)
-            gate_out(m, 1)
+        for last_two in (n - 2, n - 1):
+            gate_out(last_two, 0)
+            gate_out(last_two, 1)

@@ -25,7 +25,7 @@ STEPS = TILES // 2
 LAST = GROUPS - 1
 BANK = 512
 EARLY = 4
-SHARED = range(2, TILES - 4, 2)
+SHARED = range(2, 6, 2)
 HALVED = range(TILES - 4, TILES)
 
 

@@ -69,10 +69,7 @@ def tile_low_rank_row_mixer_t2_kernel(
         ident = const.tile([P, P], F32, name="ident")
         make_identity(nc, ident[:])
 
-        keep_bf = const.tile([P, GROUPS, 4], BF16, name="keep_bf")
-        nc.gpsimd.dma_start(out=keep_bf[:], in_=keep.rearrange("(g p t) -> p g t", p=P, t=4))
-        keep_f = const.tile([P, GROUPS, 4], F32, name="keep_f")
-        nc.gpsimd.tensor_copy(out=keep_f[:], in_=keep_bf[:])
+        keep_sb = const.tile([P, GROUPS, 4], BF16, name="keep_sb")
 
         x_sb, pos_sb, gate_sb, mix_sb, mix_raw = {}, {}, {}, {}, {}
 
@@ -137,17 +134,18 @@ def tile_low_rank_row_mixer_t2_kernel(
 
         load_x(0, 1)
         load_x(1, 1)
+        load_scales(down_sc, down_scales, 2)
         load_x(2, 2)
         nc.sync.dma_start(
             out=down_sb[:].bitcast(I32).rearrange("p (s n) -> p s n", s=2),
             in_=down_words.bitcast(I32).rearrange("s p n -> p s n"),
         )
-        load_scales(down_sc, down_scales, 2)
         load_x(4, 2)
         load_pos(0)
         load_x(6, 2)
         load_x(8, 2)
         load_mix_scales()
+        nc.sync.dma_start(out=keep_sb[:], in_=keep.rearrange("(g p t) -> p g t", p=P, t=4))
         load_pos(1)
         load_x(10, 2)
         load_mix(0)
@@ -269,7 +267,7 @@ def tile_low_rank_row_mixer_t2_kernel(
             g, t = divmod(n, 4)
             vb[n] = work.tile([P, R], BF16, name="vb", bufs=4)
             nc.vector.scalar_tensor_tensor(
-                out=vb[n][:], in0=u[g][:, t], scalar=keep_f[:, g, t : t + 1], in1=s2_banks[n][:], op0=MULT, op1=ADD
+                out=vb[n][:], in0=u[g][:, t], scalar=keep_sb[:, g, t : t + 1], in1=s2_banks[n][:], op0=MULT, op1=ADD
             )
 
         def turn_v(tiles):

@@ -51,8 +51,8 @@ def tile_low_rank_row_mixer_t2_kernel(
         def load_scales(plane, scales, passes):
             src = scales.bitcast(I32).rearrange("s q n -> q s n")
             dst = plane[:].bitcast(I32).rearrange("p (s n) -> p s n", s=passes)
-            for quad in range(4):
-                nc.sync.dma_start(out=dst[32 * quad : 32 * quad + 4], in_=src[4 * quad : 4 * quad + 4])
+            for r in range(4):
+                nc.sync.dma_start(out=dst[r:P:32], in_=src[r:16:4])
 
         x_rows = x.rearrange("(g p t) k -> g p t k", p=P, t=4)
         pos_rows = pos.rearrange("(g p t) r -> g p t r", p=P, t=4)
@@ -109,7 +109,7 @@ def tile_low_rank_row_mixer_t2_kernel(
 
         def load_mix_scales():
             src = mix_scales.bitcast(I32)
-            for quad in range(4):
+            for quad in (0, 2, 1, 3):
                 nc.sync.dma_start(
                     out=packed_sc[:].bitcast(I32)[32 * quad : 32 * quad + 16], in_=src[:, 4 * quad : 4 * quad + 4]
                 )
@@ -123,9 +123,8 @@ def tile_low_rank_row_mixer_t2_kernel(
 
         def spread_mix_scales(s):
             dst = mix_sc[:, T * (s - 1) : T * s].bitcast(I32)
-            for quad in range(4):
-                row = 32 * quad
-                nc.sync.dma_start(out=dst[row : row + 4], in_=dealt_sc[:].bitcast(I32)[row + 4 * s : row + 4 * s + 4])
+            for r in range(4):
+                nc.sync.dma_start(out=dst[r:P:32], in_=dealt_sc[:].bitcast(I32)[4 * s + r : P : 32])
 
         down_sb = const.tile([P, 2 * 2 * R], U8, name="down_sb", align_bytes=64)
         up_sb = const.tile([P, 2 * D], U8, name="up_sb", align_bytes=64)
@@ -162,10 +161,10 @@ def tile_low_rank_row_mixer_t2_kernel(
             load_mix(2)
             spread_mix_scales(3)
             nc.sync.dma_start(out=up_sb[:].bitcast(I32), in_=up_words.bitcast(I32).rearrange("s p n -> p (s n)"))
-            load_gate(2, 2)
             load_scales(up_sc, up_scales, 1)
-            load_gate(4, 4)
             load_mix(3)
+            load_gate(2, 2)
+            load_gate(4, 4)
             load_gate(8, 4)
             load_gate(12, 4)
 

@@ -25,8 +25,11 @@ STEPS = TILES // 2
 LAST = GROUPS - 1
 BANK = 512
 EARLY = 4
-SHARED = range(2, 6, 2)
-HALVED = range(TILES - 4, TILES)
+SHARE = False
+HALVED = range(TILES - 5, TILES)
+SORTED = (7, 9, 11, 13)
+SIG_FIRST = 1
+RING = (0, 1, 2, 3, 4, 5, 7)
 
 
 def tile_low_rank_row_mixer_t2_kernel(
@@ -81,7 +84,7 @@ def tile_low_rank_row_mixer_t2_kernel(
                 x_sb[first + i] = rows[:, D * i : D * (i + 1)]
 
         def load_pos(g):
-            pos_sb[g] = const.tile([P, 4, R], BF16, name="pos%d" % g)
+            pos_sb[g] = work.tile([P, 4, R], BF16, name="pos", tag="wide", bufs=7)
             nc.sync.dma_start(out=pos_sb[g][:], in_=pos_rows[g])
 
         def load_gate(first, count):
@@ -98,13 +101,14 @@ def tile_low_rank_row_mixer_t2_kernel(
                 in_=mix_words.bitcast(I32).rearrange("s p n -> p s n")[:, :, 256 * g : 256 * (g + 1)],
             )
 
-        def deal_mix(copy, g, first, count):
-            if first == 0:
-                mix_sb[g] = const.tile([P, GROUPS * 1024], U8, name="mix%d" % g, align_bytes=64)
-            cols = slice(1024 * first, 1024 * (first + count))
+        def deal_mix(copy, first, count, tag=None):
+            dealt = const.tile([P, count * 1024], U8, name="mix", tag=tag or "mix%d" % first, align_bytes=64)
+            g, t = divmod(first, 4)
+            for i in range(count):
+                mix_sb[first + i] = dealt[:, 1024 * i : 1024 * (i + 1)]
             copy(
-                out=mix_sb[g][:, cols].bitcast(U16).rearrange("p (s t c i) -> p s c t i", s=count, t=4, i=8),
-                in_=mix_raw[g][:, cols].bitcast(U16).rearrange("p (s c i t) -> p s c t i", s=count, t=4, i=8),
+                out=dealt[:].bitcast(U16).rearrange("p (t c i) -> p c t i", t=count, i=8),
+                in_=mix_raw[g][:].bitcast(U16).rearrange("p (c i t) -> p c t i", t=4, i=8)[:, :, t : t + count],
             )
 
         def load_mix_scales():
@@ -141,9 +145,9 @@ def tile_low_rank_row_mixer_t2_kernel(
         )
         load_x(4, 2)
         load_pos(0)
+        load_mix_scales()
         load_x(6, 2)
         load_x(8, 2)
-        load_mix_scales()
         nc.sync.dma_start(out=keep_sb[:], in_=keep.rearrange("(g p t) -> p g t", p=P, t=4))
         load_pos(1)
         load_x(10, 2)
@@ -162,16 +166,16 @@ def tile_low_rank_row_mixer_t2_kernel(
             spread_mix_scales(3)
             nc.sync.dma_start(out=up_sb[:].bitcast(I32), in_=up_words.bitcast(I32).rearrange("s p n -> p (s n)"))
             load_scales(up_sc, up_scales, 1)
-            load_mix(3)
             load_gate(2, 2)
             load_gate(4, 4)
+            load_mix(3)
             load_gate(8, 4)
             load_gate(12, 4)
 
         sorted_x, xt_banks, xg, xc, xs, s1_banks, u, ug, uc, us = {}, {}, {}, {}, {}, {}, {}, {}, {}, {}
 
         def sort_x(n):
-            sorted_x[n] = work.tile([P, 512], F32, name="sorted_x", bufs=5)
+            sorted_x[n] = work.tile([P, 512], F32, name="sorted_x", bufs=4)
             nc.vector.tensor_copy(
                 out=sorted_x[n][:].rearrange("p (k h c i) -> p k c h i", k=2, h=2, i=4),
                 in_=x_sb[n].bitcast(F32).rearrange("p (k c i h) -> p k c h i", k=2, h=2, i=4),
@@ -190,7 +194,10 @@ def tile_low_rank_row_mixer_t2_kernel(
                     nc.tensor.transpose(xt_banks[n][:, col : col + P], src, ident[:])
 
         def copy_x(n):
-            xg[n] = work.tile([P, D], BF16, name="xg", bufs=4, align_bytes=64)
+            if n > 8 and n % 2:
+                xg[n] = const.tile([P, D], BF16, name="xg", tag="late%d" % ((n - 9) // 2), align_bytes=64)
+            else:
+                xg[n] = work.tile([P, D], BF16, name="xg", bufs=3, align_bytes=64)
             nc.scalar.copy(
                 out=xg[n][:].bitcast(F32).rearrange("p (k r h) -> p k r h", k=2, h=2),
                 in_=xt_banks[n][:].rearrange("p (k h r) -> p k r h", k=2, h=2),
@@ -245,16 +252,21 @@ def tile_low_rank_row_mixer_t2_kernel(
 
         s2_banks, vb, vt_banks, vg, vc, vs, s3_banks, sig, o_tiles = {}, {}, [], {}, {}, {}, {}, {}, {}
 
+        ring, moved = [], {}
+
+        def ring_bank():
+            ring.append(psum_bank(RING[len(ring) % len(RING)]))
+            return ring[-1]
+
         def stage2(n, passes):
             g, t = divmod(n, 4)
             if passes[0] == 0:
-                s2_banks[n] = psum_bank(n if n < EARLY else 4 + n % 2)
+                s2_banks[n] = ring_bank()
             for s in passes:
-                word = 512 * s + P * t
                 plane = dealt_sc[:] if s == 0 else mix_sc[:, T * (s - 1) : T * s]
                 nc.tensor.matmul_mx(
                     out=s2_banks[n][:],
-                    lhsT=mix_sb[g][:, 2 * word : 2 * (word + P)].bitcast(FP4X4),
+                    lhsT=mix_sb[n][:, 2 * P * s : 2 * P * (s + 1)].bitcast(FP4X4),
                     lhsT_scale=plane[:, P * n : P * (n + 1)],
                     rhs=uc[s][:].bitcast(FP8X4),
                     rhs_scale=us[s][:],
@@ -264,13 +276,13 @@ def tile_low_rank_row_mixer_t2_kernel(
 
         def add_u(n):
             g, t = divmod(n, 4)
-            vb[n] = work.tile([P, R], BF16, name="vb", bufs=4)
+            vb[n] = work.tile([P, R], BF16, name="vb", bufs=6)
             nc.vector.scalar_tensor_tensor(
                 out=vb[n][:], in0=u[g][:, t], scalar=keep_sb[:, g, t : t + 1], in1=s2_banks[n][:], op0=MULT, op1=ADD
             )
 
         def turn_v(tiles):
-            bank = psum_bank(6 + len(vt_banks) % 2)
+            bank = psum_bank(6)
             vt_banks.append(bank)
             for i, n in enumerate(tiles):
                 words = vb[n][:].bitcast(F32)
@@ -278,7 +290,10 @@ def tile_low_rank_row_mixer_t2_kernel(
                     col = P * (2 * i + h)
                     nc.tensor.transpose(bank[:, col : col + P], words[:, P * h : P * (h + 1)], ident[:])
             for i, n in enumerate(tiles):
-                vg[n] = work.tile([P, R], BF16, name="vg", bufs=4, align_bytes=64)
+                if n in (5, 7, 9):
+                    vg[n] = const.tile([P, R], BF16, name="vg", tag="later%d" % n, align_bytes=64)
+                else:
+                    vg[n] = work.tile([P, R], BF16, name="vg", bufs=3, align_bytes=64)
                 nc.scalar.copy(
                     out=vg[n][:].bitcast(F32).rearrange("m (p h) -> m p h", h=2),
                     in_=bank[:, 2 * P * i : 2 * P * (i + 1)].rearrange("m (h p) -> m p h", h=2),
@@ -291,7 +306,7 @@ def tile_low_rank_row_mixer_t2_kernel(
 
         def stage3(n):
             for half in range(2):
-                s3_banks[n, half] = psum_bank(2 * (n % 2) + half)
+                s3_banks[n, half] = ring_bank()
                 nc.tensor.matmul_mx(
                     out=s3_banks[n, half][:],
                     lhsT=vc[n][:].bitcast(FP8X4),
@@ -303,18 +318,20 @@ def tile_low_rank_row_mixer_t2_kernel(
                 )
 
         def sigmoid_gate(n):
-            sig[n] = work.tile([P, D], F32, name="sig", bufs=5)
+            sig[n] = work.tile([P, D], F32, name="sig", tag="wide", bufs=7)
             nc.scalar.activation(sig[n][:], gate_sb[n], SIGMOID)
 
+        def move_out(n, half):
+            moved[n, half] = work.tile([P, BANK], F32, name="z", bufs=1)
+            nc.scalar.copy(out=moved[n, half][:], in_=s3_banks[n, half][:])
+
         def gate_out(n, half):
-            if half == 0:
+            if n not in o_tiles:
                 o_tiles[n] = work.tile([P, D], F32, name="o", tag="rows", bufs=9)
             cols = slice(BANK * half, BANK * (half + 1))
             bank = s3_banks[n, half]
-            if half == 0 and n in SHARED:
-                z = work.tile([P, BANK], F32, name="z", bufs=2)
-                nc.scalar.copy(out=z[:], in_=bank[:])
-                nc.gpsimd.tensor_tensor(out=o_tiles[n][:, cols], in0=z[:], in1=sig[n][:, cols], op=MULT)
+            if (n, half) in moved:
+                nc.gpsimd.tensor_tensor(out=o_tiles[n][:, cols], in0=moved[n, half][:], in1=sig[n][:, cols], op=MULT)
             else:
                 nc.vector.tensor_tensor(out=o_tiles[n][:, cols], in0=bank[:], in1=sig[n][:, cols], op=MULT)
             rows = out_rows[n // 4][n % 4]
@@ -323,8 +340,9 @@ def tile_low_rank_row_mixer_t2_kernel(
             elif half == 1:
                 nc.sync.dma_start(out=rows, in_=o_tiles[n][:])
 
+        vec, act, pool = nc.vector.tensor_copy, nc.scalar.copy, nc.gpsimd.tensor_copy
         sort_x(1)
-        for j in range(STEPS + 1):
+        for j in range(STEPS):
             fresh = [2 * j, 2 * j + 1] if j < STEPS else []
             before = [2 * j - 2, 2 * j - 1] if j >= 1 else []
             rounding, quantising = divmod(j - 3, 2), divmod(j - 4, 2)
@@ -342,6 +360,8 @@ def tile_low_rank_row_mixer_t2_kernel(
                 quant_u(*quantising)
             if j == 0:
                 sort_x(3)
+            if j >= 2 and 2 * j + 3 in SORTED:
+                sort_x(2 * j + 3)
             for n in fresh[:1]:
                 quant_x(n)
             if j == 1:
@@ -349,101 +369,139 @@ def tile_low_rank_row_mixer_t2_kernel(
                 sort_x(5)
             if j >= 4 and quantising[1] == 0:
                 quant_u(*quantising)
+            if j == STEPS - 1:
+                add_pos(before.pop(0))
             for n in fresh[1:]:
                 quant_x(n)
-            if j == 3:
-                deal_mix_scales(1)
-                later_loads()
-            if j == 4:
-                for s in range(GROUPS):
-                    deal_mix(nc.gpsimd.tensor_copy, 0, s, 1)
+            if 4 <= j:
+                deal_mix(pool, j - 4, 1, "late%d" % (j - 4))
             for n in before:
                 add_pos(n)
-                if j == 1:
-                    sort_x(6 + n)
-            if j == 2:
+            if j == 1:
                 deal_mix_scales(0)
+            if j == 2:
+                deal_mix_scales(1)
+                later_loads()
 
+        stage2(0, [0])
+        stage2(1, [0])
+        stage1(14)
+        stage1(15)
+        round_u(act, LAST - 1, 2)
+        round_u(act, LAST - 1, 3)
+        deal_mix(act, 4, 1)
+        add_pos(14)
+        quant_u(LAST - 1, 0)
+        add_pos(15)
         quant_u(LAST - 1, 1)
-        round_u(nc.vector.tensor_copy, LAST, 0)
-        round_u(nc.scalar.copy, LAST, 2)
-        round_u(nc.vector.tensor_copy, LAST, 1)
-        round_u(nc.scalar.copy, LAST, 3)
+        round_u(vec, LAST, 0)
+        round_u(act, LAST, 3)
+        round_u(vec, LAST, 1)
+        round_u(vec, LAST, 2)
         quant_u(LAST, 0)
         quant_u(LAST, 1)
 
         every = list(range(GROUPS))
-        for s in range(LAST):
-            for n in range(EARLY):
-                stage2(n, [s])
+        stage2(2, [0])
+        for n in range(3):
+            stage2(n, [1])
+        stage2(3, [0, 1])
+        stage2(4, [0, 1])
+        for n in range(EARLY + 1):
+            stage2(n, [2])
         sigmoid_gate(0)
         sigmoid_gate(1)
-        deal_mix(nc.scalar.copy, 2, 0, 2)
-        deal_mix(nc.vector.tensor_copy, 1, 0, 2)
-        deal_mix(nc.vector.tensor_copy, 1, 2, 2)
-        for n in range(EARLY):
+        deal_mix(act, 8, 2)
+        sigmoid_gate(2)
+        deal_mix(vec, 5, 1)
+        deal_mix(vec, 6, 2)
+        for n in range(EARLY + 1):
             stage2(n, [LAST])
-        stage2(4, every)
+        stage2(5, every)
         add_u(0)
         add_u(1)
         turn_v([0, 1])
-        sigmoid_gate(2)
-        stage2(5, every)
+        sigmoid_gate(3)
+        stage2(6, every)
         add_u(2)
         add_u(3)
-        deal_mix(nc.vector.tensor_copy, 3, 0, 2)
+        add_u(4)
+        add_u(5)
         quant_v(0)
         quant_v(1)
         turn_v([2, 3])
-        sigmoid_gate(3)
-        deal_mix(nc.scalar.copy, 2, 2, 2)
+        sigmoid_gate(4)
         stage3(0)
         stage3(1)
-        add_u(4)
-        deal_mix(nc.vector.tensor_copy, 3, 2, 2)
-        quant_v(2)
+        add_u(6)
         gate_out(0, 0)
-        quant_v(3)
+        quant_v(2)
+        turn_v([4, 5])
+        stage3(2)
         gate_out(0, 1)
+        quant_v(3)
+        sigmoid_gate(5)
+        sigmoid_gate(6)
+        sigmoid_gate(7)
+        stage2(7, every)
+        stage3(3)
+        gate_out(1, 0)
+        gate_out(1, 1)
+        quant_v(4)
+        quant_v(5)
+        deal_mix(pool, 10, 2, "later5")
+        stage3(4)
+        gate_out(2, 0)
+        gate_out(2, 1)
 
-        first_round, last_round = EARLY + 2, TILES - 2
+        first_round, last_round = 8, TILES - 2
         for n in range(first_round, TILES, 2):
             stage2(n, every)
             add_u(n - 1)
             if n == first_round:
-                stage3(n - 4)
                 gate_out(n - 5, 0)
                 gate_out(n - 5, 1)
             gate_out(n - 4, 0)
             gate_out(n - 4, 1)
-            sigmoid_gate(n - 2)
             turn_v([n - 2, n - 1])
             stage3(n - 3)
-            stage2(n + 1, every)
-            add_u(n)
-            quant_v(n - 2)
+            if n == last_round and SHARE:
+                move_out(n - 3, 1)
+            sigmoid_gate(n)
+            sigmoid_gate(n + 1)
+            if n < last_round:
+                stage2(n + 1, every)
+            else:
+                stage2(n + 1, every[:LAST])
+            if n == first_round:
+                quant_v(n - 2)
+                add_u(n)
+            else:
+                add_u(n)
+                quant_v(n - 2)
             gate_out(n - 3, 0)
             quant_v(n - 1)
-            gate_out(n - 3, 1)
-            sigmoid_gate(n - 1)
-            if n < last_round:
-                stage3(n - 2)
+            if n <= 10:
+                deal_mix(pool, n + 4, 2, "later%d" % (n - 1))
+            if n < last_round or not SHARE:
+                gate_out(n - 3, 1)
+            stage3(n - 2)
 
         n = TILES
+        stage2(n - 1, [LAST])
         turn_v([n - 2])
-        sigmoid_gate(n - 2)
-        stage3(n - 4)
+        gate_out(n - 4, 0)
+        if SHARE:
+            gate_out(n - 5, 1)
         add_u(n - 1)
         stage3(n - 3)
-        quant_v(n - 2)
-        gate_out(n - 4, 0)
-        turn_v([n - 1])
-        sigmoid_gate(n - 1)
         gate_out(n - 4, 1)
-        stage3(n - 2)
-        quant_v(n - 1)
+        quant_v(n - 2)
+        turn_v([n - 1])
         gate_out(n - 3, 0)
         gate_out(n - 3, 1)
+        stage3(n - 2)
+        quant_v(n - 1)
         stage3(n - 1)
         for last_two in (n - 2, n - 1):
             gate_out(last_two, 0)

@@ -25,9 +25,11 @@ STEPS = TILES // 2
 LAST = GROUPS - 1
 BANK = 512
 EARLY = 4
-SHARE = False
+SHARE = (8, 10, 12, 14)
+SH2 = 1
 HALVED = range(TILES - 5, TILES)
-SORTED = (7, 9, 11, 13)
+SORTED = (9, 11, 13)
+S7 = 1
 SIG_FIRST = 1
 RING = (0, 1, 2, 3, 4, 5, 7)
 
@@ -67,13 +69,13 @@ def tile_low_rank_row_mixer_t2_kernel(
         nc.vector.memset(warm[:], 0.0)
         packed_sc = scale_plane(T, "packed_sc")
         mix_sc = scale_plane(LAST * T, "mix_sc")
-        dealt_sc = const.tile([P, T], U8, name="dealt_sc", align_bytes=64)
         up_sc = scale_plane(D, "up_sc")
         ident = const.tile([P, P], F32, name="ident")
         make_identity(nc, ident[:])
 
         keep_sb = const.tile([P, GROUPS, 4], BF16, name="keep_sb")
 
+        planes = []
         x_sb, pos_sb, gate_sb, mix_sb, mix_raw = {}, {}, {}, {}, {}
 
         def load_x(first, count):
@@ -83,9 +85,12 @@ def tile_low_rank_row_mixer_t2_kernel(
             for i in range(count):
                 x_sb[first + i] = rows[:, D * i : D * (i + 1)]
 
-        def load_pos(g):
-            pos_sb[g] = work.tile([P, 4, R], BF16, name="pos", tag="wide", bufs=7)
-            nc.sync.dma_start(out=pos_sb[g][:], in_=pos_rows[g])
+        def load_pos(first, count):
+            rows = work.tile([P, count, R], BF16, name="pos", tag="wide", bufs=8)
+            g, t = divmod(first, 4)
+            nc.sync.dma_start(out=rows[:], in_=pos_rows[g][:, t : t + count])
+            for i in range(count):
+                pos_sb[first + i] = rows[:, i]
 
         def load_gate(first, count):
             rows = const.tile([P, count, D], BF16, name="gate%d" % first)
@@ -120,6 +125,9 @@ def tile_low_rank_row_mixer_t2_kernel(
 
         def deal_mix_scales(half):
             cols = slice(1024 * half, 1024 * (half + 1))
+            if half == 0:
+                planes.append(const.tile([P, T], U8, name="dealt_sc", align_bytes=64))
+            dealt_sc = planes[0]
             nc.vector.tensor_copy(
                 out=dealt_sc[:, cols].rearrange("p (g t c i) -> p g c t i", g=2, t=4, i=16),
                 in_=packed_sc[:, cols].rearrange("p (g c i t) -> p g c t i", g=2, t=4, i=16),
@@ -128,7 +136,7 @@ def tile_low_rank_row_mixer_t2_kernel(
         def spread_mix_scales(s):
             dst = mix_sc[:, T * (s - 1) : T * s].bitcast(I32)
             for r in range(4):
-                nc.sync.dma_start(out=dst[r:P:32], in_=dealt_sc[:].bitcast(I32)[4 * s + r : P : 32])
+                nc.sync.dma_start(out=dst[r:P:32], in_=planes[0][:].bitcast(I32)[4 * s + r : P : 32])
 
         down_sb = const.tile([P, 2 * 2 * R], U8, name="down_sb", align_bytes=64)
         up_sb = const.tile([P, 2 * D], U8, name="up_sb", align_bytes=64)
@@ -144,21 +152,22 @@ def tile_low_rank_row_mixer_t2_kernel(
             in_=down_words.bitcast(I32).rearrange("s p n -> p s n"),
         )
         load_x(4, 2)
-        load_pos(0)
+        load_pos(0, 2)
         load_mix_scales()
         load_x(6, 2)
+        load_pos(2, 2)
         load_x(8, 2)
         nc.sync.dma_start(out=keep_sb[:], in_=keep.rearrange("(g p t) -> p g t", p=P, t=4))
-        load_pos(1)
+        load_pos(4, 4)
         load_x(10, 2)
         load_mix(0)
         load_x(12, 2)
-        load_pos(2)
+        load_pos(8, 4)
         load_x(14, 2)
 
         def later_loads():
             spread_mix_scales(1)
-            load_pos(3)
+            load_pos(12, 4)
             load_mix(1)
             spread_mix_scales(2)
             load_gate(0, 2)
@@ -174,9 +183,9 @@ def tile_low_rank_row_mixer_t2_kernel(
 
         sorted_x, xt_banks, xg, xc, xs, s1_banks, u, ug, uc, us = {}, {}, {}, {}, {}, {}, {}, {}, {}, {}
 
-        def sort_x(n):
+        def sort_x(n, copy):
             sorted_x[n] = work.tile([P, 512], F32, name="sorted_x", bufs=4)
-            nc.vector.tensor_copy(
+            copy(
                 out=sorted_x[n][:].rearrange("p (k h c i) -> p k c h i", k=2, h=2, i=4),
                 in_=x_sb[n].bitcast(F32).rearrange("p (k c i h) -> p k c h i", k=2, h=2, i=4),
             )
@@ -229,7 +238,7 @@ def tile_low_rank_row_mixer_t2_kernel(
             nc.vector.tensor_tensor(
                 out=u[g][:, t].rearrange("p (h m e) -> p m h e", h=2, e=2),
                 in0=s1_banks[n][:].rearrange("p (m h e) -> p m h e", h=2, e=2),
-                in1=pos_sb[g][:, t].rearrange("p (m h e) -> p m h e", h=2, e=2),
+                in1=pos_sb[n].rearrange("p (m h e) -> p m h e", h=2, e=2),
                 op=ADD,
             )
 
@@ -263,7 +272,7 @@ def tile_low_rank_row_mixer_t2_kernel(
             if passes[0] == 0:
                 s2_banks[n] = ring_bank()
             for s in passes:
-                plane = dealt_sc[:] if s == 0 else mix_sc[:, T * (s - 1) : T * s]
+                plane = planes[0][:] if s == 0 else mix_sc[:, T * (s - 1) : T * s]
                 nc.tensor.matmul_mx(
                     out=s2_banks[n][:],
                     lhsT=mix_sb[n][:, 2 * P * s : 2 * P * (s + 1)].bitcast(FP4X4),
@@ -290,7 +299,7 @@ def tile_low_rank_row_mixer_t2_kernel(
                     col = P * (2 * i + h)
                     nc.tensor.transpose(bank[:, col : col + P], words[:, P * h : P * (h + 1)], ident[:])
             for i, n in enumerate(tiles):
-                if n in (5, 7, 9):
+                if n in (5, 7, 9, 11, 13):
                     vg[n] = const.tile([P, R], BF16, name="vg", tag="later%d" % n, align_bytes=64)
                 else:
                     vg[n] = work.tile([P, R], BF16, name="vg", bufs=3, align_bytes=64)
@@ -318,30 +327,35 @@ def tile_low_rank_row_mixer_t2_kernel(
                 )
 
         def sigmoid_gate(n):
-            sig[n] = work.tile([P, D], F32, name="sig", tag="wide", bufs=7)
+            sig[n] = work.tile([P, D], F32, name="sig", tag="wide", bufs=8)
             nc.scalar.activation(sig[n][:], gate_sb[n], SIGMOID)
 
         def move_out(n, half):
-            moved[n, half] = work.tile([P, BANK], F32, name="z", bufs=1)
+            moved[n, half] = work.tile([P, BANK], F32, name="z", bufs=2)
             nc.scalar.copy(out=moved[n, half][:], in_=s3_banks[n, half][:])
 
         def gate_out(n, half):
+            cols = slice(BANK * half, BANK * (half + 1))
+            rows = out_rows[n // 4][n % 4]
+            if (n, half) in moved and n > 7:
+                own = const.tile([P, BANK], F32, name="o", tag="later%d" % (n + 2), align_bytes=64)
+                nc.gpsimd.tensor_tensor(out=own[:], in0=moved[n, half][:], in1=sig[n][:, cols], op=MULT)
+                nc.sync.dma_start(out=rows[:, cols], in_=own[:])
+                return
             if n not in o_tiles:
                 o_tiles[n] = work.tile([P, D], F32, name="o", tag="rows", bufs=9)
-            cols = slice(BANK * half, BANK * (half + 1))
             bank = s3_banks[n, half]
             if (n, half) in moved:
                 nc.gpsimd.tensor_tensor(out=o_tiles[n][:, cols], in0=moved[n, half][:], in1=sig[n][:, cols], op=MULT)
             else:
                 nc.vector.tensor_tensor(out=o_tiles[n][:, cols], in0=bank[:], in1=sig[n][:, cols], op=MULT)
-            rows = out_rows[n // 4][n % 4]
-            if n in HALVED:
+            if n in HALVED or (n, 1) in moved and n > 7:
                 nc.sync.dma_start(out=rows[:, cols], in_=o_tiles[n][:, cols])
             elif half == 1:
                 nc.sync.dma_start(out=rows, in_=o_tiles[n][:])
 
         vec, act, pool = nc.vector.tensor_copy, nc.scalar.copy, nc.gpsimd.tensor_copy
-        sort_x(1)
+        sort_x(1, vec)
         for j in range(STEPS):
             fresh = [2 * j, 2 * j + 1] if j < STEPS else []
             before = [2 * j - 2, 2 * j - 1] if j >= 1 else []
@@ -352,6 +366,11 @@ def tile_low_rank_row_mixer_t2_kernel(
                 stage1(n)
             for n in fresh:
                 copy_x(n)
+            if j == 1:
+                sort_x(4, act)
+                sort_x(5, act)
+            if j == 2 and S7:
+                sort_x(7, act)
             if j >= 3:
                 g, half = rounding
                 round_u(nc.scalar.copy, g, 2 * half)
@@ -359,14 +378,11 @@ def tile_low_rank_row_mixer_t2_kernel(
             if j >= 4 and quantising[1] == 1:
                 quant_u(*quantising)
             if j == 0:
-                sort_x(3)
+                sort_x(3, vec)
             if j >= 2 and 2 * j + 3 in SORTED:
-                sort_x(2 * j + 3)
+                sort_x(2 * j + 3, vec)
             for n in fresh[:1]:
                 quant_x(n)
-            if j == 1:
-                sort_x(4)
-                sort_x(5)
             if j >= 4 and quantising[1] == 0:
                 quant_u(*quantising)
             if j == STEPS - 1:
@@ -377,15 +393,15 @@ def tile_low_rank_row_mixer_t2_kernel(
                 deal_mix(pool, j - 4, 1, "late%d" % (j - 4))
             for n in before:
                 add_pos(n)
+                if j == 1:
+                    deal_mix_scales(n)
             if j == 1:
-                deal_mix_scales(0)
-            if j == 2:
-                deal_mix_scales(1)
                 later_loads()
 
         stage2(0, [0])
         stage2(1, [0])
         stage1(14)
+        stage2(2, [0])
         stage1(15)
         round_u(act, LAST - 1, 2)
         round_u(act, LAST - 1, 3)
@@ -402,7 +418,6 @@ def tile_low_rank_row_mixer_t2_kernel(
         quant_u(LAST, 1)
 
         every = list(range(GROUPS))
-        stage2(2, [0])
         for n in range(3):
             stage2(n, [1])
         stage2(3, [0, 1])
@@ -437,13 +452,15 @@ def tile_low_rank_row_mixer_t2_kernel(
         gate_out(0, 0)
         quant_v(2)
         turn_v([4, 5])
+        stage2(7, every)
         stage3(2)
         gate_out(0, 1)
         quant_v(3)
         sigmoid_gate(5)
+        if SH2:
+            move_out(2, 1)
         sigmoid_gate(6)
         sigmoid_gate(7)
-        stage2(7, every)
         stage3(3)
         gate_out(1, 0)
         gate_out(1, 1)
@@ -451,24 +468,24 @@ def tile_low_rank_row_mixer_t2_kernel(
         quant_v(5)
         deal_mix(pool, 10, 2, "later5")
         stage3(4)
+        add_u(7)
         gate_out(2, 0)
         gate_out(2, 1)
 
         first_round, last_round = 8, TILES - 2
         for n in range(first_round, TILES, 2):
             stage2(n, every)
-            add_u(n - 1)
-            if n == first_round:
+            if n > first_round:
+                add_u(n - 1)
+            else:
                 gate_out(n - 5, 0)
                 gate_out(n - 5, 1)
             gate_out(n - 4, 0)
             gate_out(n - 4, 1)
             turn_v([n - 2, n - 1])
             stage3(n - 3)
-            if n == last_round and SHARE:
+            if n in SHARE:
                 move_out(n - 3, 1)
-            sigmoid_gate(n)
-            sigmoid_gate(n + 1)
             if n < last_round:
                 stage2(n + 1, every)
             else:
@@ -481,17 +498,21 @@ def tile_low_rank_row_mixer_t2_kernel(
                 quant_v(n - 2)
             gate_out(n - 3, 0)
             quant_v(n - 1)
+            sigmoid_gate(n)
+            if n < last_round:
+                sigmoid_gate(n + 1)
             if n <= 10:
                 deal_mix(pool, n + 4, 2, "later%d" % (n - 1))
-            if n < last_round or not SHARE:
+            if n < last_round or n not in SHARE:
                 gate_out(n - 3, 1)
             stage3(n - 2)
 
         n = TILES
         stage2(n - 1, [LAST])
         turn_v([n - 2])
+        sigmoid_gate(n - 1)
         gate_out(n - 4, 0)
-        if SHARE:
+        if last_round in SHARE:
             gate_out(n - 5, 1)
         add_u(n - 1)
         stage3(n - 3)

@@ -30,6 +30,9 @@ SH2 = 1
 HALVED = range(TILES - 5, TILES)
 SORTED = (9, 11, 13)
 S7 = 1
+FQ = 1
+QUART = 0
+OWN = {1: 5, 9: 11, 11: 13}
 SIG_FIRST = 1
 RING = (0, 1, 2, 3, 4, 5, 7)
 
@@ -86,7 +89,7 @@ def tile_low_rank_row_mixer_t2_kernel(
                 x_sb[first + i] = rows[:, D * i : D * (i + 1)]
 
         def load_pos(first, count):
-            rows = work.tile([P, count, R], BF16, name="pos", tag="wide", bufs=8)
+            rows = work.tile([P, count, R], BF16, name="pos", tag="wide", bufs=7)
             g, t = divmod(first, 4)
             nc.sync.dma_start(out=rows[:], in_=pos_rows[g][:, t : t + count])
             for i in range(count):
@@ -291,26 +294,25 @@ def tile_low_rank_row_mixer_t2_kernel(
             )
 
         def turn_v(tiles):
-            bank = psum_bank(6)
-            vt_banks.append(bank)
+            banks = [psum_bank(6)] + ([ring_bank()] if len(tiles) > 2 else [])
             for i, n in enumerate(tiles):
                 words = vb[n][:].bitcast(F32)
                 for h in range(2):
-                    col = P * (2 * i + h)
-                    nc.tensor.transpose(bank[:, col : col + P], words[:, P * h : P * (h + 1)], ident[:])
+                    col = P * (2 * (i % 2) + h)
+                    nc.tensor.transpose(banks[i // 2][:, col : col + P], words[:, P * h : P * (h + 1)], ident[:])
             for i, n in enumerate(tiles):
-                if n in (5, 7, 9, 11, 13):
+                if n in (5, 9, 11, 13):
                     vg[n] = const.tile([P, R], BF16, name="vg", tag="later%d" % n, align_bytes=64)
                 else:
-                    vg[n] = work.tile([P, R], BF16, name="vg", bufs=3, align_bytes=64)
+                    vg[n] = work.tile([P, R], BF16, name="vg", bufs=4, align_bytes=64)
                 nc.scalar.copy(
                     out=vg[n][:].bitcast(F32).rearrange("m (p h) -> m p h", h=2),
-                    in_=bank[:, 2 * P * i : 2 * P * (i + 1)].rearrange("m (h p) -> m p h", h=2),
+                    in_=banks[i // 2][:, 2 * P * (i % 2) : 2 * P * (i % 2 + 1)].rearrange("m (h p) -> m p h", h=2),
                 )
 
         def quant_v(n):
-            vc[n] = work.tile([P, P], U32, name="vc", bufs=4, align_bytes=64)
-            vs[n] = work.tile([P, P], U8, name="vs", bufs=4, align_bytes=64)
+            vc[n] = work.tile([P, P], U32, name="vc", bufs=6, align_bytes=64)
+            vs[n] = work.tile([P, P], U8, name="vs", bufs=6, align_bytes=64)
             nc.vector.quantize_mx(out=vc[n][:].bitcast(FP8X4), scales=vs[n][:], in_=vg[n][:])
 
         def stage3(n):
@@ -327,7 +329,7 @@ def tile_low_rank_row_mixer_t2_kernel(
                 )
 
         def sigmoid_gate(n):
-            sig[n] = work.tile([P, D], F32, name="sig", tag="wide", bufs=8)
+            sig[n] = work.tile([P, D], F32, name="sig", tag="wide", bufs=7)
             nc.scalar.activation(sig[n][:], gate_sb[n], SIGMOID)
 
         def move_out(n, half):
@@ -337,10 +339,18 @@ def tile_low_rank_row_mixer_t2_kernel(
         def gate_out(n, half):
             cols = slice(BANK * half, BANK * (half + 1))
             rows = out_rows[n // 4][n % 4]
-            if (n, half) in moved and n > 7:
-                own = const.tile([P, BANK], F32, name="o", tag="later%d" % (n + 2), align_bytes=64)
+            if (n, half) in moved and n in OWN:
+                own = const.tile([P, BANK], F32, name="o", tag="later%d" % OWN[n], align_bytes=64)
                 nc.gpsimd.tensor_tensor(out=own[:], in0=moved[n, half][:], in1=sig[n][:, cols], op=MULT)
                 nc.sync.dma_start(out=rows[:, cols], in_=own[:])
+                return
+            if QUART and (n, half) == (TILES - 1, 1):
+                for q in range(2):
+                    part = slice(BANK + 256 * q, BANK + 256 * (q + 1))
+                    nc.vector.tensor_tensor(
+                        out=o_tiles[n][:, part], in0=s3_banks[n, half][:, 256 * q : 256 * (q + 1)], in1=sig[n][:, part], op=MULT
+                    )
+                    nc.sync.dma_start(out=rows[:, part], in_=o_tiles[n][:, part])
                 return
             if n not in o_tiles:
                 o_tiles[n] = work.tile([P, D], F32, name="o", tag="rows", bufs=9)
@@ -349,7 +359,7 @@ def tile_low_rank_row_mixer_t2_kernel(
                 nc.gpsimd.tensor_tensor(out=o_tiles[n][:, cols], in0=moved[n, half][:], in1=sig[n][:, cols], op=MULT)
             else:
                 nc.vector.tensor_tensor(out=o_tiles[n][:, cols], in0=bank[:], in1=sig[n][:, cols], op=MULT)
-            if n in HALVED or (n, 1) in moved and n > 7:
+            if n in HALVED or n in OWN:
                 nc.sync.dma_start(out=rows[:, cols], in_=o_tiles[n][:, cols])
             elif half == 1:
                 nc.sync.dma_start(out=rows, in_=o_tiles[n][:])
@@ -444,42 +454,71 @@ def tile_low_rank_row_mixer_t2_kernel(
         add_u(5)
         quant_v(0)
         quant_v(1)
-        turn_v([2, 3])
-        sigmoid_gate(4)
+        turn_v([2, 3, 4, 5])
         stage3(0)
         stage3(1)
+        move_out(1, 1)
+        sigmoid_gate(4)
         add_u(6)
         gate_out(0, 0)
         quant_v(2)
-        turn_v([4, 5])
         stage2(7, every)
         stage3(2)
         gate_out(0, 1)
         quant_v(3)
+        move_out(2, 1)
         sigmoid_gate(5)
-        if SH2:
-            move_out(2, 1)
         sigmoid_gate(6)
-        sigmoid_gate(7)
         stage3(3)
         gate_out(1, 0)
-        gate_out(1, 1)
         quant_v(4)
         quant_v(5)
-        deal_mix(pool, 10, 2, "later5")
+        gate_out(1, 1)
+        deal_mix(pool, 10, 2)
         stage3(4)
         add_u(7)
         gate_out(2, 0)
         gate_out(2, 1)
+        deal_mix(pool, 12, 2)
+        sigmoid_gate(7)
+        sigmoid_gate(8)
 
-        first_round, last_round = 8, TILES - 2
+        stage2(8, every)
+        stage3(5)
+        gate_out(3, 0)
+        gate_out(3, 1)
+        gate_out(4, 0)
+        gate_out(4, 1)
+        add_u(8)
+        stage2(9, every)
+        add_u(9)
+        stage2(10, every)
+        gate_out(5, 0)
+        gate_out(5, 1)
+        turn_v([6, 7, 8, 9])
+        sigmoid_gate(9)
+        add_u(10)
+        stage2(11, every)
+        for n in (6, 7, 8, 9):
+            quant_v(n)
+        deal_mix(pool, 14, 2, "later9")
+        stage3(6)
+        stage3(7)
+        sigmoid_gate(10)
+        move_out(7, 1)
+        sigmoid_gate(11)
+        add_u(11)
+        gate_out(6, 0)
+        gate_out(6, 1)
+        gate_out(7, 0)
+        gate_out(7, 1)
+        stage3(8)
+
+        first_round, last_round = 12, TILES - 2
         for n in range(first_round, TILES, 2):
             stage2(n, every)
             if n > first_round:
                 add_u(n - 1)
-            else:
-                gate_out(n - 5, 0)
-                gate_out(n - 5, 1)
             gate_out(n - 4, 0)
             gate_out(n - 4, 1)
             turn_v([n - 2, n - 1])
@@ -490,12 +529,8 @@ def tile_low_rank_row_mixer_t2_kernel(
                 stage2(n + 1, every)
             else:
                 stage2(n + 1, every[:LAST])
-            if n == first_round:
-                quant_v(n - 2)
-                add_u(n)
-            else:
-                add_u(n)
-                quant_v(n - 2)
+            add_u(n)
+            quant_v(n - 2)
             gate_out(n - 3, 0)
             quant_v(n - 1)
             sigmoid_gate(n)

@@ -52,7 +52,7 @@ def tile_low_rank_row_mixer_t2_kernel(
             return bank
 
         def scale_plane(width, name):
-            plane = const.tile([P, width], U8, name=name, align_bytes=64)
+            plane = const.tile([P, width], U8, name=name, align_bytes=256)
             nc.vector.memset(plane[:].bitcast(I32), 0)
             return plane
 
@@ -82,14 +82,14 @@ def tile_low_rank_row_mixer_t2_kernel(
         x_sb, pos_sb, gate_sb, mix_sb, mix_raw = {}, {}, {}, {}, {}
 
         def load_x(first, count):
-            rows = work.tile([P, count * D], BF16, name="x", tag="rows", bufs=9)
+            rows = work.tile([P, count * D], BF16, name="x", tag="rows", bufs=8)
             g, t = divmod(first, 4)
             nc.sync.dma_start(out=rows[:].rearrange("p (t k) -> p t k", t=count), in_=x_rows[g][:, t : t + count])
             for i in range(count):
                 x_sb[first + i] = rows[:, D * i : D * (i + 1)]
 
         def load_pos(first, count):
-            rows = work.tile([P, count, R], BF16, name="pos", tag="wide", bufs=7)
+            rows = work.tile([P, count, R], BF16, name="pos", tag="wide", bufs=6)
             g, t = divmod(first, 4)
             nc.sync.dma_start(out=rows[:], in_=pos_rows[g][:, t : t + count])
             for i in range(count):
@@ -103,14 +103,14 @@ def tile_low_rank_row_mixer_t2_kernel(
                 gate_sb[first + i] = rows[:, i]
 
         def load_mix(g):
-            mix_raw[g] = work.tile([P, GROUPS * 1024], U8, name="mix_raw", bufs=3, align_bytes=64)
+            mix_raw[g] = work.tile([P, GROUPS * 1024], U8, name="mix_raw", bufs=3, align_bytes=256)
             nc.sync.dma_start(
                 out=mix_raw[g][:].bitcast(I32).rearrange("p (s n) -> p s n", s=GROUPS),
                 in_=mix_words.bitcast(I32).rearrange("s p n -> p s n")[:, :, 256 * g : 256 * (g + 1)],
             )
 
         def deal_mix(copy, first, count, tag=None):
-            dealt = const.tile([P, count * 1024], U8, name="mix", tag=tag or "mix%d" % first, align_bytes=64)
+            dealt = const.tile([P, count * 1024], U8, name="mix", tag=tag or "mix%d" % first, align_bytes=256)
             g, t = divmod(first, 4)
             for i in range(count):
                 mix_sb[first + i] = dealt[:, 1024 * i : 1024 * (i + 1)]
@@ -129,7 +129,7 @@ def tile_low_rank_row_mixer_t2_kernel(
         def deal_mix_scales(half):
             cols = slice(1024 * half, 1024 * (half + 1))
             if half == 0:
-                planes.append(const.tile([P, T], U8, name="dealt_sc", align_bytes=64))
+                planes.append(const.tile([P, T], U8, name="dealt_sc", align_bytes=256))
             dealt_sc = planes[0]
             nc.vector.tensor_copy(
                 out=dealt_sc[:, cols].rearrange("p (g t c i) -> p g c t i", g=2, t=4, i=16),
@@ -141,8 +141,8 @@ def tile_low_rank_row_mixer_t2_kernel(
             for r in range(4):
                 nc.sync.dma_start(out=dst[r:P:32], in_=planes[0][:].bitcast(I32)[4 * s + r : P : 32])
 
-        down_sb = const.tile([P, 2 * 2 * R], U8, name="down_sb", align_bytes=64)
-        up_sb = const.tile([P, 2 * D], U8, name="up_sb", align_bytes=64)
+        down_sb = const.tile([P, 2 * 2 * R], U8, name="down_sb", align_bytes=256)
+        up_sb = const.tile([P, 2 * D], U8, name="up_sb", align_bytes=256)
 
         nc.scalar.activation(warm[:], warm[:], SIGMOID)
 
@@ -207,17 +207,17 @@ def tile_low_rank_row_mixer_t2_kernel(
 
         def copy_x(n):
             if n > 8 and n % 2:
-                xg[n] = const.tile([P, D], BF16, name="xg", tag="late%d" % ((n - 9) // 2), align_bytes=64)
+                xg[n] = const.tile([P, D], BF16, name="xg", tag="late%d" % ((n - 9) // 2), align_bytes=256)
             else:
-                xg[n] = work.tile([P, D], BF16, name="xg", bufs=3, align_bytes=64)
+                xg[n] = work.tile([P, D], BF16, name="xg", bufs=3, align_bytes=256)
             nc.scalar.copy(
                 out=xg[n][:].bitcast(F32).rearrange("p (k r h) -> p k r h", k=2, h=2),
                 in_=xt_banks[n][:].rearrange("p (k h r) -> p k r h", k=2, h=2),
             )
 
         def quant_x(n):
-            xc[n] = work.tile([P, 2 * P], U32, name="xc", bufs=4, align_bytes=64)
-            xs[n] = work.tile([P, 2 * P], U8, name="xs", bufs=4, align_bytes=64)
+            xc[n] = work.tile([P, 2 * P], U32, name="xc", bufs=4, align_bytes=256)
+            xs[n] = work.tile([P, 2 * P], U8, name="xs", bufs=4, align_bytes=256)
             nc.vector.quantize_mx(out=xc[n][:].bitcast(FP8X4), scales=xs[n][:], in_=xg[n][:])
 
         def stage1(n):
@@ -247,7 +247,7 @@ def tile_low_rank_row_mixer_t2_kernel(
 
         def round_u(copy, g, quarter):
             if quarter == 0:
-                ug[g] = work.tile([P, 4 * R], BF16, name="ug", bufs=2, align_bytes=64)
+                ug[g] = work.tile([P, 4 * R], BF16, name="ug", bufs=2, align_bytes=256)
             copy(
                 out=ug[g][:, R * quarter : R * (quarter + 1)].rearrange("p (c i t) -> p c t i", t=4, i=4),
                 in_=u[g][:, :, P * quarter : P * (quarter + 1)].rearrange("p t (c i) -> p c t i", i=4),
@@ -255,8 +255,8 @@ def tile_low_rank_row_mixer_t2_kernel(
 
         def quant_u(g, half):
             if half == 0:
-                uc[g] = const.tile([P, R], U32, name="uc%d" % g, align_bytes=64)
-                us[g] = const.tile([P, R], U8, name="us%d" % g, align_bytes=64)
+                uc[g] = const.tile([P, R], U32, name="uc%d" % g, align_bytes=256)
+                us[g] = const.tile([P, R], U8, name="us%d" % g, align_bytes=256)
             cols = slice(256 * half, 256 * (half + 1))
             nc.vector.quantize_mx(
                 out=uc[g][:, cols].bitcast(FP8X4), scales=us[g][:, cols], in_=ug[g][:, 1024 * half : 1024 * (half + 1)]
@@ -302,17 +302,17 @@ def tile_low_rank_row_mixer_t2_kernel(
                     nc.tensor.transpose(banks[i // 2][:, col : col + P], words[:, P * h : P * (h + 1)], ident[:])
             for i, n in enumerate(tiles):
                 if n in (5, 9, 11, 13):
-                    vg[n] = const.tile([P, R], BF16, name="vg", tag="later%d" % n, align_bytes=64)
+                    vg[n] = const.tile([P, R], BF16, name="vg", tag="later%d" % n, align_bytes=256)
                 else:
-                    vg[n] = work.tile([P, R], BF16, name="vg", bufs=4, align_bytes=64)
+                    vg[n] = work.tile([P, R], BF16, name="vg", bufs=4, align_bytes=256)
                 nc.scalar.copy(
                     out=vg[n][:].bitcast(F32).rearrange("m (p h) -> m p h", h=2),
                     in_=banks[i // 2][:, 2 * P * (i % 2) : 2 * P * (i % 2 + 1)].rearrange("m (h p) -> m p h", h=2),
                 )
 
         def quant_v(n):
-            vc[n] = work.tile([P, P], U32, name="vc", bufs=6, align_bytes=64)
-            vs[n] = work.tile([P, P], U8, name="vs", bufs=6, align_bytes=64)
+            vc[n] = work.tile([P, P], U32, name="vc", bufs=6, align_bytes=256)
+            vs[n] = work.tile([P, P], U8, name="vs", bufs=6, align_bytes=256)
             nc.vector.quantize_mx(out=vc[n][:].bitcast(FP8X4), scales=vs[n][:], in_=vg[n][:])
 
         def stage3(n):
@@ -329,7 +329,7 @@ def tile_low_rank_row_mixer_t2_kernel(
                 )
 
         def sigmoid_gate(n):
-            sig[n] = work.tile([P, D], F32, name="sig", tag="wide", bufs=7)
+            sig[n] = work.tile([P, D], F32, name="sig", tag="wide", bufs=6)
             nc.scalar.activation(sig[n][:], gate_sb[n], SIGMOID)
 
         def move_out(n, half):
@@ -340,7 +340,7 @@ def tile_low_rank_row_mixer_t2_kernel(
             cols = slice(BANK * half, BANK * (half + 1))
             rows = out_rows[n // 4][n % 4]
             if (n, half) in moved and n in OWN:
-                own = const.tile([P, BANK], F32, name="o", tag="later%d" % OWN[n], align_bytes=64)
+                own = const.tile([P, BANK], F32, name="o", tag="later%d" % OWN[n], align_bytes=256)
                 nc.gpsimd.tensor_tensor(out=own[:], in0=moved[n, half][:], in1=sig[n][:, cols], op=MULT)
                 nc.sync.dma_start(out=rows[:, cols], in_=own[:])
                 return
@@ -353,7 +353,7 @@ def tile_low_rank_row_mixer_t2_kernel(
                     nc.sync.dma_start(out=rows[:, part], in_=o_tiles[n][:, part])
                 return
             if n not in o_tiles:
-                o_tiles[n] = work.tile([P, D], F32, name="o", tag="rows", bufs=9)
+                o_tiles[n] = work.tile([P, D], F32, name="o", tag="rows", bufs=8)
             bank = s3_banks[n, half]
             if (n, half) in moved:
                 nc.gpsimd.tensor_tensor(out=o_tiles[n][:, cols], in0=moved[n, half][:], in1=sig[n][:, cols], op=MULT)

@@ -68,35 +68,35 @@ def tile_low_rank_row_mixer_t2_kernel(
         out_rows = out.rearrange("(g p t) c -> g t p c", p=P, t=4)
 
         down_sc = scale_plane(2 * R, "down_sc")
-        warm = const.tile([P, 1], F32, name="warm")
+        warm = const.tile([P, 1], F32, name="warm", align_bytes=256)
         nc.vector.memset(warm[:], 0.0)
         packed_sc = scale_plane(T, "packed_sc")
         mix_sc = scale_plane(LAST * T, "mix_sc")
         up_sc = scale_plane(D, "up_sc")
-        ident = const.tile([P, P], F32, name="ident")
+        ident = const.tile([P, P], F32, name="ident", align_bytes=256)
         make_identity(nc, ident[:])
 
-        keep_sb = const.tile([P, GROUPS, 4], BF16, name="keep_sb")
+        keep_sb = const.tile([P, GROUPS, 4], BF16, name="keep_sb", align_bytes=256)
 
         planes = []
         x_sb, pos_sb, gate_sb, mix_sb, mix_raw = {}, {}, {}, {}, {}
 
         def load_x(first, count):
-            rows = work.tile([P, count * D], BF16, name="x", tag="rows", bufs=8)
+            rows = work.tile([P, count * D], BF16, name="x", tag="rows", bufs=8, align_bytes=256)
             g, t = divmod(first, 4)
             nc.sync.dma_start(out=rows[:].rearrange("p (t k) -> p t k", t=count), in_=x_rows[g][:, t : t + count])
             for i in range(count):
                 x_sb[first + i] = rows[:, D * i : D * (i + 1)]
 
         def load_pos(first, count):
-            rows = work.tile([P, count, R], BF16, name="pos", tag="wide", bufs=6)
+            rows = work.tile([P, count, R], BF16, name="pos", tag="wide", bufs=6, align_bytes=256)
             g, t = divmod(first, 4)
             nc.sync.dma_start(out=rows[:], in_=pos_rows[g][:, t : t + count])
             for i in range(count):
                 pos_sb[first + i] = rows[:, i]
 
         def load_gate(first, count):
-            rows = const.tile([P, count, D], BF16, name="gate%d" % first)
+            rows = const.tile([P, count, D], BF16, name="gate%d" % first, align_bytes=256)
             g, t = divmod(first, 4)
             nc.sync.dma_start(out=rows[:], in_=gate_rows[g][:, t : t + count])
             for i in range(count):
@@ -187,7 +187,7 @@ def tile_low_rank_row_mixer_t2_kernel(
         sorted_x, xt_banks, xg, xc, xs, s1_banks, u, ug, uc, us = {}, {}, {}, {}, {}, {}, {}, {}, {}, {}
 
         def sort_x(n, copy):
-            sorted_x[n] = work.tile([P, 512], F32, name="sorted_x", bufs=4)
+            sorted_x[n] = work.tile([P, 512], F32, name="sorted_x", bufs=3, align_bytes=256)
             copy(
                 out=sorted_x[n][:].rearrange("p (k h c i) -> p k c h i", k=2, h=2, i=4),
                 in_=x_sb[n].bitcast(F32).rearrange("p (k c i h) -> p k c h i", k=2, h=2, i=4),
@@ -237,7 +237,7 @@ def tile_low_rank_row_mixer_t2_kernel(
         def add_pos(n):
             g, t = divmod(n, 4)
             if t == 0:
-                u[g] = const.tile([P, 4, R], F32, name="u%d" % g)
+                u[g] = const.tile([P, 4, R], F32, name="u%d" % g, align_bytes=256)
             nc.vector.tensor_tensor(
                 out=u[g][:, t].rearrange("p (h m e) -> p m h e", h=2, e=2),
                 in0=s1_banks[n][:].rearrange("p (m h e) -> p m h e", h=2, e=2),
@@ -288,7 +288,7 @@ def tile_low_rank_row_mixer_t2_kernel(
 
         def add_u(n):
             g, t = divmod(n, 4)
-            vb[n] = work.tile([P, R], BF16, name="vb", bufs=6)
+            vb[n] = work.tile([P, R], BF16, name="vb", bufs=5, align_bytes=256)
             nc.vector.scalar_tensor_tensor(
                 out=vb[n][:], in0=u[g][:, t], scalar=keep_sb[:, g, t : t + 1], in1=s2_banks[n][:], op0=MULT, op1=ADD
             )
@@ -329,11 +329,11 @@ def tile_low_rank_row_mixer_t2_kernel(
                 )
 
         def sigmoid_gate(n):
-            sig[n] = work.tile([P, D], F32, name="sig", tag="wide", bufs=6)
+            sig[n] = work.tile([P, D], F32, name="sig", tag="wide", bufs=6, align_bytes=256)
             nc.scalar.activation(sig[n][:], gate_sb[n], SIGMOID)
 
         def move_out(n, half):
-            moved[n, half] = work.tile([P, BANK], F32, name="z", bufs=2)
+            moved[n, half] = work.tile([P, BANK], F32, name="z", bufs=2, align_bytes=256)
             nc.scalar.copy(out=moved[n, half][:], in_=s3_banks[n, half][:])
 
         def gate_out(n, half):
@@ -353,7 +353,7 @@ def tile_low_rank_row_mixer_t2_kernel(
                     nc.sync.dma_start(out=rows[:, part], in_=o_tiles[n][:, part])
                 return
             if n not in o_tiles:
-                o_tiles[n] = work.tile([P, D], F32, name="o", tag="rows", bufs=8)
+                o_tiles[n] = work.tile([P, D], F32, name="o", tag="rows", bufs=8, align_bytes=256)
             bank = s3_banks[n, half]
             if (n, half) in moved:
                 nc.gpsimd.tensor_tensor(out=o_tiles[n][:, cols], in0=moved[n, half][:], in1=sig[n][:, cols], op=MULT)

@@ -24,17 +24,13 @@ TILES = T // P
 STEPS = TILES // 2
 LAST = GROUPS - 1
 BANK = 512
-EARLY = 4
-SHARE = (8, 10, 12, 14)
-SH2 = 1
-HALVED = range(TILES - 5, TILES)
-SORTED = (9, 11, 13)
-S7 = 1
-FQ = 1
-QUART = 0
-OWN = {1: 5, 9: 11, 11: 13}
-SIG_FIRST = 1
+ALIGN = 256
+EARLY = 5
 RING = (0, 1, 2, 3, 4, 5, 7)
+X_OPENS = (9, 11, 13, 15)
+V_OPENS = (5, 9, 11, 13)
+OWN_BUFFER = {1: 5, 9: 11, 11: 13}
+HALVED = range(TILES - 5, TILES)
 
 
 def tile_low_rank_row_mixer_t2_kernel(
@@ -46,13 +42,14 @@ def tile_low_rank_row_mixer_t2_kernel(
         work = ctx.enter_context(tc.tile_pool(name="work", bufs=2))
         psum = ctx.enter_context(tc.psum_pool(name="psum", bufs=1))
         ctx.enter_context(tc.manual_schedule())
+        on_vector, on_scalar, on_gpsimd = nc.vector.tensor_copy, nc.scalar.copy, nc.gpsimd.tensor_copy
 
         def psum_bank(index):
             bank = psum.tile([P, BANK], F32, name="bank%d" % index, tag="bank%d" % index)
             return bank
 
         def scale_plane(width, name):
-            plane = const.tile([P, width], U8, name=name, align_bytes=256)
+            plane = const.tile([P, width], U8, name=name, align_bytes=ALIGN)
             nc.vector.memset(plane[:].bitcast(I32), 0)
             return plane
 
@@ -68,49 +65,50 @@ def tile_low_rank_row_mixer_t2_kernel(
         out_rows = out.rearrange("(g p t) c -> g t p c", p=P, t=4)
 
         down_sc = scale_plane(2 * R, "down_sc")
-        warm = const.tile([P, 1], F32, name="warm", align_bytes=256)
+        warm = const.tile([P, 1], F32, name="warm", align_bytes=ALIGN)
         nc.vector.memset(warm[:], 0.0)
         packed_sc = scale_plane(T, "packed_sc")
         mix_sc = scale_plane(LAST * T, "mix_sc")
         up_sc = scale_plane(D, "up_sc")
-        ident = const.tile([P, P], F32, name="ident", align_bytes=256)
+        dealt_sc = const.tile([P, T], U8, name="dealt_sc", align_bytes=ALIGN)
+        ident = const.tile([P, P], F32, name="ident", align_bytes=ALIGN)
         make_identity(nc, ident[:])
 
-        keep_sb = const.tile([P, GROUPS, 4], BF16, name="keep_sb", align_bytes=256)
-
-        planes = []
-        x_sb, pos_sb, gate_sb, mix_sb, mix_raw = {}, {}, {}, {}, {}
+        keep_sb = const.tile([P, GROUPS, 4], BF16, name="keep_sb", align_bytes=ALIGN)
+        down_sb = const.tile([P, 2 * 2 * R], U8, name="down_sb", align_bytes=ALIGN)
+        up_sb = const.tile([P, 2 * D], U8, name="up_sb", align_bytes=ALIGN)
+        x_sb, pos_sb, gate_sb, mix_raw, mix_sb = {}, {}, {}, {}, {}
 
         def load_x(first, count):
-            rows = work.tile([P, count * D], BF16, name="x", tag="rows", bufs=8, align_bytes=256)
+            rows = work.tile([P, count * D], BF16, name="x", tag="rows", bufs=8, align_bytes=ALIGN)
             g, t = divmod(first, 4)
             nc.sync.dma_start(out=rows[:].rearrange("p (t k) -> p t k", t=count), in_=x_rows[g][:, t : t + count])
             for i in range(count):
                 x_sb[first + i] = rows[:, D * i : D * (i + 1)]
 
         def load_pos(first, count):
-            rows = work.tile([P, count, R], BF16, name="pos", tag="wide", bufs=6, align_bytes=256)
+            rows = work.tile([P, count, R], BF16, name="pos", tag="wide", bufs=6, align_bytes=ALIGN)
             g, t = divmod(first, 4)
             nc.sync.dma_start(out=rows[:], in_=pos_rows[g][:, t : t + count])
             for i in range(count):
                 pos_sb[first + i] = rows[:, i]
 
         def load_gate(first, count):
-            rows = const.tile([P, count, D], BF16, name="gate%d" % first, align_bytes=256)
+            rows = const.tile([P, count, D], BF16, name="gate%d" % first, align_bytes=ALIGN)
             g, t = divmod(first, 4)
             nc.sync.dma_start(out=rows[:], in_=gate_rows[g][:, t : t + count])
             for i in range(count):
                 gate_sb[first + i] = rows[:, i]
 
         def load_mix(g):
-            mix_raw[g] = work.tile([P, GROUPS * 1024], U8, name="mix_raw", bufs=3, align_bytes=256)
+            mix_raw[g] = work.tile([P, GROUPS * 1024], U8, name="mix_raw", bufs=3, align_bytes=ALIGN)
             nc.sync.dma_start(
                 out=mix_raw[g][:].bitcast(I32).rearrange("p (s n) -> p s n", s=GROUPS),
                 in_=mix_words.bitcast(I32).rearrange("s p n -> p s n")[:, :, 256 * g : 256 * (g + 1)],
             )
 
         def deal_mix(copy, first, count, tag=None):
-            dealt = const.tile([P, count * 1024], U8, name="mix", tag=tag or "mix%d" % first, align_bytes=256)
+            dealt = const.tile([P, count * 1024], U8, name="mix", tag=tag or "mix%d" % first, align_bytes=ALIGN)
             g, t = divmod(first, 4)
             for i in range(count):
                 mix_sb[first + i] = dealt[:, 1024 * i : 1024 * (i + 1)]
@@ -128,10 +126,7 @@ def tile_low_rank_row_mixer_t2_kernel(
 
         def deal_mix_scales(half):
             cols = slice(1024 * half, 1024 * (half + 1))
-            if half == 0:
-                planes.append(const.tile([P, T], U8, name="dealt_sc", align_bytes=256))
-            dealt_sc = planes[0]
-            nc.vector.tensor_copy(
+            on_vector(
                 out=dealt_sc[:, cols].rearrange("p (g t c i) -> p g c t i", g=2, t=4, i=16),
                 in_=packed_sc[:, cols].rearrange("p (g c i t) -> p g c t i", g=2, t=4, i=16),
             )
@@ -139,10 +134,7 @@ def tile_low_rank_row_mixer_t2_kernel(
         def spread_mix_scales(s):
             dst = mix_sc[:, T * (s - 1) : T * s].bitcast(I32)
             for r in range(4):
-                nc.sync.dma_start(out=dst[r:P:32], in_=planes[0][:].bitcast(I32)[4 * s + r : P : 32])
-
-        down_sb = const.tile([P, 2 * 2 * R], U8, name="down_sb", align_bytes=256)
-        up_sb = const.tile([P, 2 * D], U8, name="up_sb", align_bytes=256)
+                nc.sync.dma_start(out=dst[r:P:32], in_=dealt_sc[:].bitcast(I32)[4 * s + r : P : 32])
 
         nc.scalar.activation(warm[:], warm[:], SIGMOID)
 
@@ -186,8 +178,8 @@ def tile_low_rank_row_mixer_t2_kernel(
 
         sorted_x, xt_banks, xg, xc, xs, s1_banks, u, ug, uc, us = {}, {}, {}, {}, {}, {}, {}, {}, {}, {}
 
-        def sort_x(n, copy):
-            sorted_x[n] = work.tile([P, 512], F32, name="sorted_x", bufs=3, align_bytes=256)
+        def sort_x(copy, n):
+            sorted_x[n] = work.tile([P, 512], F32, name="sorted_x", bufs=3, align_bytes=ALIGN)
             copy(
                 out=sorted_x[n][:].rearrange("p (k h c i) -> p k c h i", k=2, h=2, i=4),
                 in_=x_sb[n].bitcast(F32).rearrange("p (k c i h) -> p k c h i", k=2, h=2, i=4),
@@ -206,18 +198,18 @@ def tile_low_rank_row_mixer_t2_kernel(
                     nc.tensor.transpose(xt_banks[n][:, col : col + P], src, ident[:])
 
         def copy_x(n):
-            if n > 8 and n % 2:
-                xg[n] = const.tile([P, D], BF16, name="xg", tag="late%d" % ((n - 9) // 2), align_bytes=256)
+            if n in X_OPENS:
+                xg[n] = const.tile([P, D], BF16, name="xg", tag="after_x%d" % n, align_bytes=ALIGN)
             else:
-                xg[n] = work.tile([P, D], BF16, name="xg", bufs=3, align_bytes=256)
-            nc.scalar.copy(
+                xg[n] = work.tile([P, D], BF16, name="xg", bufs=3, align_bytes=ALIGN)
+            on_scalar(
                 out=xg[n][:].bitcast(F32).rearrange("p (k r h) -> p k r h", k=2, h=2),
                 in_=xt_banks[n][:].rearrange("p (k h r) -> p k r h", k=2, h=2),
             )
 
         def quant_x(n):
-            xc[n] = work.tile([P, 2 * P], U32, name="xc", bufs=4, align_bytes=256)
-            xs[n] = work.tile([P, 2 * P], U8, name="xs", bufs=4, align_bytes=256)
+            xc[n] = work.tile([P, 2 * P], U32, name="xc", bufs=4, align_bytes=ALIGN)
+            xs[n] = work.tile([P, 2 * P], U8, name="xs", bufs=4, align_bytes=ALIGN)
             nc.vector.quantize_mx(out=xc[n][:].bitcast(FP8X4), scales=xs[n][:], in_=xg[n][:])
 
         def stage1(n):
@@ -237,7 +229,7 @@ def tile_low_rank_row_mixer_t2_kernel(
         def add_pos(n):
             g, t = divmod(n, 4)
             if t == 0:
-                u[g] = const.tile([P, 4, R], F32, name="u%d" % g, align_bytes=256)
+                u[g] = const.tile([P, 4, R], F32, name="u%d" % g, align_bytes=ALIGN)
             nc.vector.tensor_tensor(
                 out=u[g][:, t].rearrange("p (h m e) -> p m h e", h=2, e=2),
                 in0=s1_banks[n][:].rearrange("p (m h e) -> p m h e", h=2, e=2),
@@ -247,7 +239,7 @@ def tile_low_rank_row_mixer_t2_kernel(
 
         def round_u(copy, g, quarter):
             if quarter == 0:
-                ug[g] = work.tile([P, 4 * R], BF16, name="ug", bufs=2, align_bytes=256)
+                ug[g] = work.tile([P, 4 * R], BF16, name="ug", bufs=2, align_bytes=ALIGN)
             copy(
                 out=ug[g][:, R * quarter : R * (quarter + 1)].rearrange("p (c i t) -> p c t i", t=4, i=4),
                 in_=u[g][:, :, P * quarter : P * (quarter + 1)].rearrange("p t (c i) -> p c t i", i=4),
@@ -255,27 +247,24 @@ def tile_low_rank_row_mixer_t2_kernel(
 
         def quant_u(g, half):
             if half == 0:
-                uc[g] = const.tile([P, R], U32, name="uc%d" % g, align_bytes=256)
-                us[g] = const.tile([P, R], U8, name="us%d" % g, align_bytes=256)
+                uc[g] = const.tile([P, R], U32, name="uc%d" % g, align_bytes=ALIGN)
+                us[g] = const.tile([P, R], U8, name="us%d" % g, align_bytes=ALIGN)
             cols = slice(256 * half, 256 * (half + 1))
             nc.vector.quantize_mx(
                 out=uc[g][:, cols].bitcast(FP8X4), scales=us[g][:, cols], in_=ug[g][:, 1024 * half : 1024 * (half + 1)]
             )
 
-        s2_banks, vb, vt_banks, vg, vc, vs, s3_banks, sig, o_tiles = {}, {}, [], {}, {}, {}, {}, {}, {}
-
-        ring, moved = [], {}
+        ring, s2_banks, vb, vg, vc, vs, s3_banks, sig, moved, o_tiles = [], {}, {}, {}, {}, {}, {}, {}, {}, {}
 
         def ring_bank():
             ring.append(psum_bank(RING[len(ring) % len(RING)]))
             return ring[-1]
 
         def stage2(n, passes):
-            g, t = divmod(n, 4)
             if passes[0] == 0:
                 s2_banks[n] = ring_bank()
             for s in passes:
-                plane = planes[0][:] if s == 0 else mix_sc[:, T * (s - 1) : T * s]
+                plane = dealt_sc[:] if s == 0 else mix_sc[:, T * (s - 1) : T * s]
                 nc.tensor.matmul_mx(
                     out=s2_banks[n][:],
                     lhsT=mix_sb[n][:, 2 * P * s : 2 * P * (s + 1)].bitcast(FP4X4),
@@ -288,7 +277,7 @@ def tile_low_rank_row_mixer_t2_kernel(
 
         def add_u(n):
             g, t = divmod(n, 4)
-            vb[n] = work.tile([P, R], BF16, name="vb", bufs=5, align_bytes=256)
+            vb[n] = work.tile([P, R], BF16, name="vb", bufs=5, align_bytes=ALIGN)
             nc.vector.scalar_tensor_tensor(
                 out=vb[n][:], in0=u[g][:, t], scalar=keep_sb[:, g, t : t + 1], in1=s2_banks[n][:], op0=MULT, op1=ADD
             )
@@ -301,18 +290,19 @@ def tile_low_rank_row_mixer_t2_kernel(
                     col = P * (2 * (i % 2) + h)
                     nc.tensor.transpose(banks[i // 2][:, col : col + P], words[:, P * h : P * (h + 1)], ident[:])
             for i, n in enumerate(tiles):
-                if n in (5, 9, 11, 13):
-                    vg[n] = const.tile([P, R], BF16, name="vg", tag="later%d" % n, align_bytes=256)
+                if n in V_OPENS:
+                    vg[n] = const.tile([P, R], BF16, name="vg", tag="after_v%d" % n, align_bytes=ALIGN)
                 else:
-                    vg[n] = work.tile([P, R], BF16, name="vg", bufs=4, align_bytes=256)
-                nc.scalar.copy(
+                    vg[n] = work.tile([P, R], BF16, name="vg", bufs=4, align_bytes=ALIGN)
+                col = 2 * P * (i % 2)
+                on_scalar(
                     out=vg[n][:].bitcast(F32).rearrange("m (p h) -> m p h", h=2),
-                    in_=banks[i // 2][:, 2 * P * (i % 2) : 2 * P * (i % 2 + 1)].rearrange("m (h p) -> m p h", h=2),
+                    in_=banks[i // 2][:, col : col + 2 * P].rearrange("m (h p) -> m p h", h=2),
                 )
 
         def quant_v(n):
-            vc[n] = work.tile([P, P], U32, name="vc", bufs=6, align_bytes=256)
-            vs[n] = work.tile([P, P], U8, name="vs", bufs=6, align_bytes=256)
+            vc[n] = work.tile([P, P], U32, name="vc", bufs=6, align_bytes=ALIGN)
+            vs[n] = work.tile([P, P], U8, name="vs", bufs=6, align_bytes=ALIGN)
             nc.vector.quantize_mx(out=vc[n][:].bitcast(FP8X4), scales=vs[n][:], in_=vg[n][:])
 
         def stage3(n):
@@ -329,47 +319,39 @@ def tile_low_rank_row_mixer_t2_kernel(
                 )
 
         def sigmoid_gate(n):
-            sig[n] = work.tile([P, D], F32, name="sig", tag="wide", bufs=6, align_bytes=256)
+            sig[n] = work.tile([P, D], F32, name="sig", tag="wide", bufs=6, align_bytes=ALIGN)
             nc.scalar.activation(sig[n][:], gate_sb[n], SIGMOID)
 
-        def move_out(n, half):
-            moved[n, half] = work.tile([P, BANK], F32, name="z", bufs=2, align_bytes=256)
-            nc.scalar.copy(out=moved[n, half][:], in_=s3_banks[n, half][:])
+        def move_right_half(n):
+            moved[n] = work.tile([P, BANK], F32, name="moved", bufs=2, align_bytes=ALIGN)
+            on_scalar(out=moved[n][:], in_=s3_banks[n, 1][:])
 
         def gate_out(n, half):
             cols = slice(BANK * half, BANK * (half + 1))
             rows = out_rows[n // 4][n % 4]
-            if (n, half) in moved and n in OWN:
-                own = const.tile([P, BANK], F32, name="o", tag="later%d" % OWN[n], align_bytes=256)
-                nc.gpsimd.tensor_tensor(out=own[:], in0=moved[n, half][:], in1=sig[n][:, cols], op=MULT)
-                nc.sync.dma_start(out=rows[:, cols], in_=own[:])
-                return
-            if QUART and (n, half) == (TILES - 1, 1):
-                for q in range(2):
-                    part = slice(BANK + 256 * q, BANK + 256 * (q + 1))
-                    nc.vector.tensor_tensor(
-                        out=o_tiles[n][:, part], in0=s3_banks[n, half][:, 256 * q : 256 * (q + 1)], in1=sig[n][:, part], op=MULT
-                    )
-                    nc.sync.dma_start(out=rows[:, part], in_=o_tiles[n][:, part])
-                return
-            if n not in o_tiles:
-                o_tiles[n] = work.tile([P, D], F32, name="o", tag="rows", bufs=8, align_bytes=256)
-            bank = s3_banks[n, half]
-            if (n, half) in moved:
-                nc.gpsimd.tensor_tensor(out=o_tiles[n][:, cols], in0=moved[n, half][:], in1=sig[n][:, cols], op=MULT)
+            if half == 0:
+                o_tiles[n] = work.tile([P, D], F32, name="o", tag="rows", bufs=8, align_bytes=ALIGN)
+            product = o_tiles[n][:, cols]
+            if half == 1 and n in OWN_BUFFER:
+                own = const.tile([P, BANK], F32, name="o", tag="after_v%d" % OWN_BUFFER[n], align_bytes=ALIGN)
+                product = own[:]
+            if half == 1 and n in moved:
+                nc.gpsimd.tensor_tensor(out=product, in0=moved[n][:], in1=sig[n][:, cols], op=MULT)
             else:
-                nc.vector.tensor_tensor(out=o_tiles[n][:, cols], in0=bank[:], in1=sig[n][:, cols], op=MULT)
-            if n in HALVED or n in OWN:
-                nc.sync.dma_start(out=rows[:, cols], in_=o_tiles[n][:, cols])
+                nc.vector.tensor_tensor(out=product, in0=s3_banks[n, half][:], in1=sig[n][:, cols], op=MULT)
+            if n in HALVED or n in OWN_BUFFER:
+                nc.sync.dma_start(out=rows[:, cols], in_=product)
             elif half == 1:
                 nc.sync.dma_start(out=rows, in_=o_tiles[n][:])
 
-        vec, act, pool = nc.vector.tensor_copy, nc.scalar.copy, nc.gpsimd.tensor_copy
-        sort_x(1, vec)
+        def gate_both(n):
+            gate_out(n, 0)
+            gate_out(n, 1)
+
+        sort_x(on_vector, 1)
         for j in range(STEPS):
-            fresh = [2 * j, 2 * j + 1] if j < STEPS else []
+            fresh = [2 * j, 2 * j + 1]
             before = [2 * j - 2, 2 * j - 1] if j >= 1 else []
-            rounding, quantising = divmod(j - 3, 2), divmod(j - 4, 2)
             for n in fresh:
                 turn_x(n)
             for n in before:
@@ -377,87 +359,81 @@ def tile_low_rank_row_mixer_t2_kernel(
             for n in fresh:
                 copy_x(n)
             if j == 1:
-                sort_x(4, act)
-                sort_x(5, act)
-            if j == 2 and S7:
-                sort_x(7, act)
+                sort_x(on_scalar, 5)
             if j >= 3:
-                g, half = rounding
-                round_u(nc.scalar.copy, g, 2 * half)
-                round_u(nc.scalar.copy, g, 2 * half + 1)
-            if j >= 4 and quantising[1] == 1:
-                quant_u(*quantising)
+                g, half = divmod(j - 3, 2)
+                round_u(on_scalar, g, 2 * half)
+                round_u(on_scalar, g, 2 * half + 1)
+            if j >= 5 and j % 2:
+                quant_u((j - 4) // 2, 1)
             if j == 0:
-                sort_x(3, vec)
-            if j >= 2 and 2 * j + 3 in SORTED:
-                sort_x(2 * j + 3, vec)
-            for n in fresh[:1]:
-                quant_x(n)
-            if j >= 4 and quantising[1] == 0:
-                quant_u(*quantising)
+                sort_x(on_vector, 3)
+            if j == 4:
+                sort_x(on_vector, 11)
+            quant_x(fresh[0])
+            if j >= 4 and j % 2 == 0:
+                quant_u((j - 4) // 2, 0)
             if j == STEPS - 1:
                 add_pos(before.pop(0))
-            for n in fresh[1:]:
-                quant_x(n)
-            if 4 <= j:
-                deal_mix(pool, j - 4, 1, "late%d" % (j - 4))
+            quant_x(fresh[1])
+            if fresh[1] in X_OPENS:
+                deal_mix(on_gpsimd, X_OPENS.index(fresh[1]), 1, "after_x%d" % fresh[1])
             for n in before:
                 add_pos(n)
-                if j == 1:
-                    deal_mix_scales(n)
-            if j == 1:
+            if j in (1, 2):
+                deal_mix_scales(j - 1)
+            if j == 2:
                 later_loads()
 
         stage2(0, [0])
         stage2(1, [0])
-        stage1(14)
+        stage1(TILES - 2)
         stage2(2, [0])
-        stage1(15)
-        round_u(act, LAST - 1, 2)
-        round_u(act, LAST - 1, 3)
-        deal_mix(act, 4, 1)
-        add_pos(14)
+        stage1(TILES - 1)
+        round_u(on_scalar, LAST - 1, 2)
+        round_u(on_scalar, LAST - 1, 3)
+        deal_mix(on_scalar, 4, 1)
+        add_pos(TILES - 2)
         quant_u(LAST - 1, 0)
-        add_pos(15)
+        add_pos(TILES - 1)
         quant_u(LAST - 1, 1)
-        round_u(vec, LAST, 0)
-        round_u(act, LAST, 3)
-        round_u(vec, LAST, 1)
-        round_u(vec, LAST, 2)
+        round_u(on_vector, LAST, 0)
+        round_u(on_scalar, LAST, 3)
+        round_u(on_vector, LAST, 1)
+        round_u(on_vector, LAST, 2)
         quant_u(LAST, 0)
         quant_u(LAST, 1)
 
         every = list(range(GROUPS))
         for n in range(3):
             stage2(n, [1])
-        stage2(3, [0, 1])
-        stage2(4, [0, 1])
-        for n in range(EARLY + 1):
+        for n in range(3, EARLY):
+            stage2(n, [0, 1])
+        for n in range(EARLY):
             stage2(n, [2])
         sigmoid_gate(0)
         sigmoid_gate(1)
-        deal_mix(act, 8, 2)
+        deal_mix(on_scalar, 8, 2)
         sigmoid_gate(2)
-        deal_mix(vec, 5, 1)
-        deal_mix(vec, 6, 2)
-        for n in range(EARLY + 1):
+        deal_mix(on_vector, 5, 1)
+        deal_mix(on_vector, 6, 2)
+        for n in range(EARLY):
             stage2(n, [LAST])
+
         stage2(5, every)
         add_u(0)
         add_u(1)
         turn_v([0, 1])
         sigmoid_gate(3)
         stage2(6, every)
-        add_u(2)
-        add_u(3)
-        add_u(4)
-        add_u(5)
+        for n in range(2, 6):
+            add_u(n)
         quant_v(0)
         quant_v(1)
         turn_v([2, 3, 4, 5])
         stage3(0)
         stage3(1)
-        move_out(1, 1)
+        move_right_half(1)
         sigmoid_gate(4)
         add_u(6)
         gate_out(0, 0)
@@ -466,7 +442,7 @@ def tile_low_rank_row_mixer_t2_kernel(
         stage3(2)
         gate_out(0, 1)
         quant_v(3)
-        move_out(2, 1)
+        move_right_half(2)
         sigmoid_gate(5)
         sigmoid_gate(6)
         stage3(3)
@@ -474,61 +450,50 @@ def tile_low_rank_row_mixer_t2_kernel(
         quant_v(4)
         quant_v(5)
         gate_out(1, 1)
-        deal_mix(pool, 10, 2)
+        deal_mix(on_gpsimd, 10, 2)
         stage3(4)
         add_u(7)
-        gate_out(2, 0)
-        gate_out(2, 1)
-        deal_mix(pool, 12, 2)
+        gate_both(2)
+        deal_mix(on_gpsimd, 12, 2)
         sigmoid_gate(7)
         sigmoid_gate(8)
 
         stage2(8, every)
         stage3(5)
-        gate_out(3, 0)
-        gate_out(3, 1)
-        gate_out(4, 0)
-        gate_out(4, 1)
+        gate_both(3)
+        gate_both(4)
         add_u(8)
         stage2(9, every)
         add_u(9)
         stage2(10, every)
-        gate_out(5, 0)
-        gate_out(5, 1)
+        gate_both(5)
         turn_v([6, 7, 8, 9])
         sigmoid_gate(9)
         add_u(10)
         stage2(11, every)
-        for n in (6, 7, 8, 9):
+        for n in range(6, 10):
             quant_v(n)
-        deal_mix(pool, 14, 2, "later9")
+        deal_mix(on_gpsimd, 14, 2, "after_v9")
         stage3(6)
         stage3(7)
         sigmoid_gate(10)
-        move_out(7, 1)
+        move_right_half(7)
         sigmoid_gate(11)
         add_u(11)
-        gate_out(6, 0)
-        gate_out(6, 1)
-        gate_out(7, 0)
-        gate_out(7, 1)
+        gate_both(6)
+        gate_both(7)
         stage3(8)
 
-        first_round, last_round = 12, TILES - 2
-        for n in range(first_round, TILES, 2):
+        last_round = TILES - 2
+        for n in (last_round - 2, last_round):
             stage2(n, every)
-            if n > first_round:
+            if n == last_round:
                 add_u(n - 1)
-            gate_out(n - 4, 0)
-            gate_out(n - 4, 1)
+            gate_both(n - 4)
             turn_v([n - 2, n - 1])
             stage3(n - 3)
-            if n in SHARE:
-                move_out(n - 3, 1)
-            if n < last_round:
-                stage2(n + 1, every)
-            else:
-                stage2(n + 1, every[:LAST])
+            move_right_half(n - 3)
+            stage2(n + 1, every if n < last_round else every[:LAST])
             add_u(n)
             quant_v(n - 2)
             gate_out(n - 3, 0)
@@ -536,9 +501,6 @@ def tile_low_rank_row_mixer_t2_kernel(
             sigmoid_gate(n)
             if n < last_round:
                 sigmoid_gate(n + 1)
-            if n <= 10:
-                deal_mix(pool, n + 4, 2, "later%d" % (n - 1))
-            if n < last_round or n not in SHARE:
                 gate_out(n - 3, 1)
             stage3(n - 2)
 
@@ -547,18 +509,15 @@ def tile_low_rank_row_mixer_t2_kernel(
         turn_v([n - 2])
         sigmoid_gate(n - 1)
         gate_out(n - 4, 0)
-        if last_round in SHARE:
-            gate_out(n - 5, 1)
+        gate_out(n - 5, 1)
         add_u(n - 1)
         stage3(n - 3)
         gate_out(n - 4, 1)
         quant_v(n - 2)
         turn_v([n - 1])
-        gate_out(n - 3, 0)
-        gate_out(n - 3, 1)
+        gate_both(n - 3)
         stage3(n - 2)
         quant_v(n - 1)
         stage3(n - 1)
-        for last_two in (n - 2, n - 1):
-            gate_out(last_two, 0)
-            gate_out(last_two, 1)
+        gate_both(n - 2)
+        gate_both(n - 1)

@@ -80,7 +80,10 @@ def tile_low_rank_row_mixer_t2_kernel(
         x_sb, pos_sb, gate_sb, mix_raw, mix_sb = {}, {}, {}, {}, {}
 
         def load_x(first, count):
-            rows = work.tile([P, count * D], BF16, name="x", tag="rows", bufs=8, align_bytes=ALIGN)
+            if count == 1:
+                rows = work.tile([P, D], BF16, name="x", tag="single", bufs=4, align_bytes=ALIGN)
+            else:
+                rows = work.tile([P, count * D], BF16, name="x", tag="rows", bufs=6, align_bytes=ALIGN)
             g, t = divmod(first, 4)
             nc.sync.dma_start(out=rows[:].rearrange("p (t k) -> p t k", t=count), in_=x_rows[g][:, t : t + count])
             for i in range(count):
@@ -141,7 +144,8 @@ def tile_low_rank_row_mixer_t2_kernel(
         load_x(0, 1)
         load_x(1, 1)
         load_scales(down_sc, down_scales, 2)
-        load_x(2, 2)
+        load_x(2, 1)
+        load_x(3, 1)
         nc.sync.dma_start(
             out=down_sb[:].bitcast(I32).rearrange("p (s n) -> p s n", s=2),
             in_=down_words.bitcast(I32).rearrange("s p n -> p s n"),
@@ -237,12 +241,12 @@ def tile_low_rank_row_mixer_t2_kernel(
                 op=ADD,
             )
 
-        def round_u(copy, g, quarter):
-            if quarter == 0:
+        def round_u(copy, g, first, count):
+            if first == 0:
                 ug[g] = work.tile([P, 4 * R], BF16, name="ug", bufs=2, align_bytes=ALIGN)
             copy(
-                out=ug[g][:, R * quarter : R * (quarter + 1)].rearrange("p (c i t) -> p c t i", t=4, i=4),
-                in_=u[g][:, :, P * quarter : P * (quarter + 1)].rearrange("p t (c i) -> p c t i", i=4),
+                out=ug[g][:, R * first : R * (first + count)].rearrange("p (c i t) -> p c t i", t=4, i=4),
+                in_=u[g][:, :, P * first : P * (first + count)].rearrange("p t (c i) -> p c t i", i=4),
             )
 
         def quant_u(g, half):
@@ -282,8 +286,10 @@ def tile_low_rank_row_mixer_t2_kernel(
                 out=vb[n][:], in0=u[g][:, t], scalar=keep_sb[:, g, t : t + 1], in1=s2_banks[n][:], op0=MULT, op1=ADD
             )
 
-        def turn_v(tiles):
+        def turn_v(tiles, borrowed_first=False):
             banks = [psum_bank(6)] + ([ring_bank()] if len(tiles) > 2 else [])
+            if borrowed_first:
+                banks.reverse()
             for i, n in enumerate(tiles):
                 words = vb[n][:].bitcast(F32)
                 for h in range(2):
@@ -330,7 +336,7 @@ def tile_low_rank_row_mixer_t2_kernel(
             cols = slice(BANK * half, BANK * (half + 1))
             rows = out_rows[n // 4][n % 4]
             if half == 0:
-                o_tiles[n] = work.tile([P, D], F32, name="o", tag="rows", bufs=8, align_bytes=ALIGN)
+                o_tiles[n] = work.tile([P, D], F32, name="o", tag="rows", bufs=6, align_bytes=ALIGN)
             product = o_tiles[n][:, cols]
             if half == 1 and n in OWN_BUFFER:
                 own = const.tile([P, BANK], F32, name="o", tag="after_v%d" % OWN_BUFFER[n], align_bytes=ALIGN)
@@ -359,17 +365,18 @@ def tile_low_rank_row_mixer_t2_kernel(
             for n in fresh:
                 copy_x(n)
             if j == 1:
+                sort_x(on_scalar, 4)
                 sort_x(on_scalar, 5)
             if j >= 3:
                 g, half = divmod(j - 3, 2)
-                round_u(on_scalar, g, 2 * half)
-                round_u(on_scalar, g, 2 * half + 1)
+                round_u(on_scalar, g, 2 * half, 2)
             if j >= 5 and j % 2:
                 quant_u((j - 4) // 2, 1)
             if j == 0:
+                sort_x(on_vector, 2)
                 sort_x(on_vector, 3)
-            if j == 4:
-                sort_x(on_vector, 11)
+            if j in (3, 4):
+                sort_x(on_vector, 2 * j + 3)
             quant_x(fresh[0])
             if j >= 4 and j % 2 == 0:
                 quant_u((j - 4) // 2, 0)
@@ -380,9 +387,9 @@ def tile_low_rank_row_mixer_t2_kernel(
                 deal_mix(on_gpsimd, X_OPENS.index(fresh[1]), 1, "after_x%d" % fresh[1])
             for n in before:
                 add_pos(n)
-            if j in (1, 2):
-                deal_mix_scales(j - 1)
-            if j == 2:
+                if j == 1:
+                    deal_mix_scales(n)
+            if j == 1:
                 later_loads()
 
         stage2(0, [0])
@@ -390,17 +397,15 @@ def tile_low_rank_row_mixer_t2_kernel(
         stage1(TILES - 2)
         stage2(2, [0])
         stage1(TILES - 1)
-        round_u(on_scalar, LAST - 1, 2)
-        round_u(on_scalar, LAST - 1, 3)
+        round_u(on_scalar, LAST - 1, 2, 2)
         deal_mix(on_scalar, 4, 1)
         add_pos(TILES - 2)
         quant_u(LAST - 1, 0)
         add_pos(TILES - 1)
         quant_u(LAST - 1, 1)
-        round_u(on_vector, LAST, 0)
-        round_u(on_scalar, LAST, 3)
-        round_u(on_vector, LAST, 1)
-        round_u(on_vector, LAST, 2)
+        round_u(on_vector, LAST, 0, 2)
+        round_u(on_scalar, LAST, 3, 1)
+        round_u(on_vector, LAST, 2, 1)
         quant_u(LAST, 0)
         quant_u(LAST, 1)
 
@@ -430,7 +435,7 @@ def tile_low_rank_row_mixer_t2_kernel(
             add_u(n)
         quant_v(0)
         quant_v(1)
-        turn_v([2, 3, 4, 5])
+        turn_v([2, 3, 4, 5], borrowed_first=True)
         stage3(0)
         stage3(1)
         move_right_half(1)

@@ -21,16 +21,14 @@ SIGMOID = mybir.ActivationFunctionType.Sigmoid
 P = 128
 GROUPS = T // 512
 TILES = T // P
-STEPS = TILES // 2
 LAST = GROUPS - 1
 BANK = 512
 ALIGN = 256
 EARLY = 5
-RING = (0, 1, 2, 3, 4, 5, 7)
-X_OPENS = (9, 11, 13, 15)
-V_OPENS = (5, 9, 11, 13)
-OWN_BUFFER = {1: 5, 9: 11, 11: 13}
-HALVED = range(TILES - 5, TILES)
+G_COLS = 384
+HOLDS = {4: "hold0", 6: "hold1"}
+U_HOLDS = ("hold0", "hold1", "hold1", "hold0")
+HALVED = range(TILES - 6, TILES)
 
 
 def tile_low_rank_row_mixer_t2_kernel(
@@ -139,51 +137,11 @@ def tile_low_rank_row_mixer_t2_kernel(
             for r in range(4):
                 nc.sync.dma_start(out=dst[r:P:32], in_=dealt_sc[:].bitcast(I32)[4 * s + r : P : 32])
 
-        nc.scalar.activation(warm[:], warm[:], SIGMOID)
-
-        load_x(0, 1)
-        load_x(1, 1)
-        load_scales(down_sc, down_scales, 2)
-        load_x(2, 1)
-        load_x(3, 1)
-        nc.sync.dma_start(
-            out=down_sb[:].bitcast(I32).rearrange("p (s n) -> p s n", s=2),
-            in_=down_words.bitcast(I32).rearrange("s p n -> p s n"),
-        )
-        load_x(4, 2)
-        load_pos(0, 2)
-        load_mix_scales()
-        load_x(6, 2)
-        load_pos(2, 2)
-        load_x(8, 2)
-        nc.sync.dma_start(out=keep_sb[:], in_=keep.rearrange("(g p t) -> p g t", p=P, t=4))
-        load_pos(4, 4)
-        load_x(10, 2)
-        load_mix(0)
-        load_x(12, 2)
-        load_pos(8, 4)
-        load_x(14, 2)
-
-        def later_loads():
-            spread_mix_scales(1)
-            load_pos(12, 4)
-            load_mix(1)
-            spread_mix_scales(2)
-            load_gate(0, 2)
-            load_mix(2)
-            spread_mix_scales(3)
-            nc.sync.dma_start(out=up_sb[:].bitcast(I32), in_=up_words.bitcast(I32).rearrange("s p n -> p (s n)"))
-            load_scales(up_sc, up_scales, 1)
-            load_gate(2, 2)
-            load_gate(4, 4)
-            load_mix(3)
-            load_gate(8, 4)
-            load_gate(12, 4)
 
         sorted_x, xt_banks, xg, xc, xs, s1_banks, u, ug, uc, us = {}, {}, {}, {}, {}, {}, {}, {}, {}, {}
 
         def sort_x(copy, n):
-            sorted_x[n] = work.tile([P, 512], F32, name="sorted_x", bufs=3, align_bytes=ALIGN)
+            sorted_x[n] = work.tile([P, 512], F32, name="sorted_x", bufs=4, align_bytes=ALIGN)
             copy(
                 out=sorted_x[n][:].rearrange("p (k h c i) -> p k c h i", k=2, h=2, i=4),
                 in_=x_sb[n].bitcast(F32).rearrange("p (k c i h) -> p k c h i", k=2, h=2, i=4),
@@ -202,28 +160,35 @@ def tile_low_rank_row_mixer_t2_kernel(
                     nc.tensor.transpose(xt_banks[n][:, col : col + P], src, ident[:])
 
         def copy_x(n):
-            if n in X_OPENS:
-                xg[n] = const.tile([P, D], BF16, name="xg", tag="after_x%d" % n, align_bytes=ALIGN)
-            else:
-                xg[n] = work.tile([P, D], BF16, name="xg", bufs=3, align_bytes=ALIGN)
+            q, i = divmod(n, 2)
+            if i == 0 and q in HOLDS:
+                xg[q] = const.tile([P, 2 * D], BF16, name="xg", tag=HOLDS[q], align_bytes=ALIGN)
+            elif i == 0:
+                xg[q] = work.tile([P, 2 * D], BF16, name="xg", bufs=2, align_bytes=ALIGN)
             on_scalar(
-                out=xg[n][:].bitcast(F32).rearrange("p (k r h) -> p k r h", k=2, h=2),
+                out=xg[q][:, D * i : D * (i + 1)].bitcast(F32).rearrange("p (k r h) -> p k r h", k=2, h=2),
                 in_=xt_banks[n][:].rearrange("p (k h r) -> p k r h", k=2, h=2),
             )
 
-        def quant_x(n):
-            xc[n] = work.tile([P, 2 * P], U32, name="xc", bufs=4, align_bytes=ALIGN)
-            xs[n] = work.tile([P, 2 * P], U8, name="xs", bufs=4, align_bytes=ALIGN)
-            nc.vector.quantize_mx(out=xc[n][:].bitcast(FP8X4), scales=xs[n][:], in_=xg[n][:])
+        def quant_x(first, count):
+            q, i = divmod(first, 2)
+            if i == 0:
+                xc[q] = work.tile([P, 4 * P], U32, name="xc", bufs=3, align_bytes=ALIGN)
+                xs[q] = work.tile([P, 4 * P], U8, name="xs", bufs=3, align_bytes=ALIGN)
+            cols = slice(2 * P * i, 2 * P * (i + count))
+            nc.vector.quantize_mx(
+                out=xc[q][:, cols].bitcast(FP8X4), scales=xs[q][:, cols], in_=xg[q][:, D * i : D * (i + count)]
+            )
 
         def stage1(n):
+            q, i = divmod(n, 2)
             s1_banks[n] = psum_bank(4 + n % 4)
             for k in range(2):
-                cols = slice(P * k, P * (k + 1))
+                cols = slice(P * (2 * i + k), P * (2 * i + k + 1))
                 nc.tensor.matmul_mx(
                     out=s1_banks[n][:],
-                    lhsT=xc[n][:, cols].bitcast(FP8X4),
-                    lhsT_scale=xs[n][:, cols],
+                    lhsT=xc[q][:, cols].bitcast(FP8X4),
+                    lhsT_scale=xs[q][:, cols],
                     rhs=down_sb[:, 2 * R * k : 2 * R * (k + 1)].bitcast(FP4X4),
                     rhs_scale=down_sc[:, R * k : R * (k + 1)],
                     start=(k == 0),
@@ -241,27 +206,39 @@ def tile_low_rank_row_mixer_t2_kernel(
                 op=ADD,
             )
 
-        def round_u(copy, g, first, count):
-            if first == 0:
-                ug[g] = work.tile([P, 4 * R], BF16, name="ug", bufs=2, align_bytes=ALIGN)
+        def rounded(g):
+            if g not in ug:
+                ug[g] = const.tile([P, 4 * R], BF16, name="ug", tag=U_HOLDS[g], align_bytes=ALIGN)
+            return ug[g]
+
+        def round_u(copy, g, first, last):
             copy(
-                out=ug[g][:, R * first : R * (first + count)].rearrange("p (c i t) -> p c t i", t=4, i=4),
-                in_=u[g][:, :, P * first : P * (first + count)].rearrange("p t (c i) -> p c t i", i=4),
+                out=rounded(g)[:, 4 * first : 4 * last].rearrange("p (c i t) -> p c t i", t=4, i=4),
+                in_=u[g][:, :, first:last].rearrange("p t (c i) -> p c t i", i=4),
             )
 
-        def quant_u(g, half):
-            if half == 0:
+        def round_u_gpsimd(g, first, last):
+            nc.gpsimd.tensor_scalar(
+                out=rounded(g)[:, 4 * first : 4 * last].rearrange("p (c t) -> p c t", t=4),
+                in0=u[g][:, :, first:last].rearrange("p t c -> p c t"),
+                scalar1=1.0,
+                scalar2=0.0,
+                op0=MULT,
+                op1=ADD,
+            )
+
+        def quant_u(g, first, last):
+            if g not in uc:
                 uc[g] = const.tile([P, R], U32, name="uc%d" % g, align_bytes=ALIGN)
                 us[g] = const.tile([P, R], U8, name="us%d" % g, align_bytes=ALIGN)
-            cols = slice(256 * half, 256 * (half + 1))
             nc.vector.quantize_mx(
-                out=uc[g][:, cols].bitcast(FP8X4), scales=us[g][:, cols], in_=ug[g][:, 1024 * half : 1024 * (half + 1)]
+                out=uc[g][:, first:last].bitcast(FP8X4), scales=us[g][:, first:last], in_=ug[g][:, 4 * first : 4 * last]
             )
 
-        ring, s2_banks, vb, vg, vc, vs, s3_banks, sig, moved, o_tiles = [], {}, {}, {}, {}, {}, {}, {}, {}, {}
+        ring, s2_banks, vb, vt, vg, vc, vs, s3_banks, sig, moved, o_tiles = [], {}, {}, {}, {}, {}, {}, {}, {}, {}, {}
 
         def ring_bank():
-            ring.append(psum_bank(RING[len(ring) % len(RING)]))
+            ring.append(psum_bank(len(ring) % 8))
             return ring[-1]
 
         def stage2(n, passes):
@@ -281,52 +258,54 @@ def tile_low_rank_row_mixer_t2_kernel(
 
         def add_u(n):
             g, t = divmod(n, 4)
-            vb[n] = work.tile([P, R], BF16, name="vb", bufs=5, align_bytes=ALIGN)
+            vb[n] = work.tile([P, R], BF16, name="vb", bufs=6, align_bytes=ALIGN)
             nc.vector.scalar_tensor_tensor(
                 out=vb[n][:], in0=u[g][:, t], scalar=keep_sb[:, g, t : t + 1], in1=s2_banks[n][:], op0=MULT, op1=ADD
             )
 
-        def turn_v(tiles, borrowed_first=False):
-            banks = [psum_bank(6)] + ([ring_bank()] if len(tiles) > 2 else [])
-            if borrowed_first:
-                banks.reverse()
-            for i, n in enumerate(tiles):
-                words = vb[n][:].bitcast(F32)
+        def turn_v(first, count):
+            vt[first] = ring_bank()
+            for i in range(count):
+                words = vb[first + i][:].bitcast(F32)
                 for h in range(2):
-                    col = P * (2 * (i % 2) + h)
-                    nc.tensor.transpose(banks[i // 2][:, col : col + P], words[:, P * h : P * (h + 1)], ident[:])
-            for i, n in enumerate(tiles):
-                if n in V_OPENS:
-                    vg[n] = const.tile([P, R], BF16, name="vg", tag="after_v%d" % n, align_bytes=ALIGN)
-                else:
-                    vg[n] = work.tile([P, R], BF16, name="vg", bufs=4, align_bytes=ALIGN)
-                col = 2 * P * (i % 2)
-                on_scalar(
-                    out=vg[n][:].bitcast(F32).rearrange("m (p h) -> m p h", h=2),
-                    in_=banks[i // 2][:, col : col + 2 * P].rearrange("m (h p) -> m p h", h=2),
-                )
+                    col = P * (2 * i + h)
+                    nc.tensor.transpose(vt[first][:, col : col + P], words[:, P * h : P * (h + 1)], ident[:])
 
-        def quant_v(n):
-            vc[n] = work.tile([P, P], U32, name="vc", bufs=6, align_bytes=ALIGN)
-            vs[n] = work.tile([P, P], U8, name="vs", bufs=6, align_bytes=ALIGN)
-            nc.vector.quantize_mx(out=vc[n][:].bitcast(FP8X4), scales=vs[n][:], in_=vg[n][:])
+        def copy_v(first, count):
+            if first == 0:
+                vg[first] = const.tile([P, count * R], BF16, name="vg", tag="hold2", align_bytes=ALIGN)
+            else:
+                vg[first] = work.tile([P, count * R], BF16, name="vg", bufs=3, align_bytes=ALIGN)
+            on_scalar(
+                out=vg[first][:].bitcast(F32).rearrange("m (i p h) -> m i p h", i=count, h=2),
+                in_=vt[first][:, : 2 * P * count].rearrange("m (i h p) -> m i p h", i=count, h=2),
+            )
+
+        def quant_v(first, count):
+            codes = work.tile([P, count * P], U32, name="vc", bufs=4, align_bytes=ALIGN)
+            scales = work.tile([P, count * P], U8, name="vs", bufs=4, align_bytes=ALIGN)
+            nc.vector.quantize_mx(out=codes[:].bitcast(FP8X4), scales=scales[:], in_=vg[first][:])
+            for i in range(count):
+                vc[first + i] = codes[:, P * i : P * (i + 1)]
+                vs[first + i] = scales[:, P * i : P * (i + 1)]
 
         def stage3(n):
             for half in range(2):
                 s3_banks[n, half] = ring_bank()
                 nc.tensor.matmul_mx(
                     out=s3_banks[n, half][:],
-                    lhsT=vc[n][:].bitcast(FP8X4),
-                    lhsT_scale=vs[n][:],
+                    lhsT=vc[n].bitcast(FP8X4),
+                    lhsT_scale=vs[n],
                     rhs=up_sb[:, 2 * BANK * half : 2 * BANK * (half + 1)].bitcast(FP4X4),
                     rhs_scale=up_sc[:, BANK * half : BANK * (half + 1)],
                     start=True,
                     stop=True,
                 )
 
-        def sigmoid_gate(n):
-            sig[n] = work.tile([P, D], F32, name="sig", tag="wide", bufs=6, align_bytes=ALIGN)
-            nc.scalar.activation(sig[n][:], gate_sb[n], SIGMOID)
+        def sigmoid_gate(n, first=0, last=D):
+            if first == 0:
+                sig[n] = work.tile([P, D], F32, name="sig", tag="wide", bufs=6, align_bytes=ALIGN)
+            nc.scalar.activation(sig[n][:, first:last], gate_sb[n][:, first:last], SIGMOID)
 
         def move_right_half(n):
             moved[n] = work.tile([P, BANK], F32, name="moved", bufs=2, align_bytes=ALIGN)
@@ -338,14 +317,11 @@ def tile_low_rank_row_mixer_t2_kernel(
             if half == 0:
                 o_tiles[n] = work.tile([P, D], F32, name="o", tag="rows", bufs=6, align_bytes=ALIGN)
             product = o_tiles[n][:, cols]
-            if half == 1 and n in OWN_BUFFER:
-                own = const.tile([P, BANK], F32, name="o", tag="after_v%d" % OWN_BUFFER[n], align_bytes=ALIGN)
-                product = own[:]
             if half == 1 and n in moved:
                 nc.gpsimd.tensor_tensor(out=product, in0=moved[n][:], in1=sig[n][:, cols], op=MULT)
             else:
                 nc.vector.tensor_tensor(out=product, in0=s3_banks[n, half][:], in1=sig[n][:, cols], op=MULT)
-            if n in HALVED or n in OWN_BUFFER:
+            if n in HALVED:
                 nc.sync.dma_start(out=rows[:, cols], in_=product)
             elif half == 1:
                 nc.sync.dma_start(out=rows, in_=o_tiles[n][:])
@@ -354,175 +330,243 @@ def tile_low_rank_row_mixer_t2_kernel(
             gate_out(n, 0)
             gate_out(n, 1)
 
-        sort_x(on_vector, 1)
-        for j in range(STEPS):
-            fresh = [2 * j, 2 * j + 1]
-            before = [2 * j - 2, 2 * j - 1] if j >= 1 else []
-            for n in fresh:
-                turn_x(n)
-            for n in before:
-                stage1(n)
-            for n in fresh:
-                copy_x(n)
-            if j == 1:
-                sort_x(on_scalar, 4)
-                sort_x(on_scalar, 5)
-            if j >= 3:
-                g, half = divmod(j - 3, 2)
-                round_u(on_scalar, g, 2 * half, 2)
-            if j >= 5 and j % 2:
-                quant_u((j - 4) // 2, 1)
-            if j == 0:
-                sort_x(on_vector, 2)
-                sort_x(on_vector, 3)
-            if j in (3, 4):
-                sort_x(on_vector, 2 * j + 3)
-            quant_x(fresh[0])
-            if j >= 4 and j % 2 == 0:
-                quant_u((j - 4) // 2, 0)
-            if j == STEPS - 1:
-                add_pos(before.pop(0))
-            quant_x(fresh[1])
-            if fresh[1] in X_OPENS:
-                deal_mix(on_gpsimd, X_OPENS.index(fresh[1]), 1, "after_x%d" % fresh[1])
-            for n in before:
-                add_pos(n)
-                if j == 1:
-                    deal_mix_scales(n)
-            if j == 1:
-                later_loads()
-
-        stage2(0, [0])
-        stage2(1, [0])
-        stage1(TILES - 2)
-        stage2(2, [0])
-        stage1(TILES - 1)
-        round_u(on_scalar, LAST - 1, 2, 2)
-        deal_mix(on_scalar, 4, 1)
-        add_pos(TILES - 2)
-        quant_u(LAST - 1, 0)
-        add_pos(TILES - 1)
-        quant_u(LAST - 1, 1)
-        round_u(on_vector, LAST, 0, 2)
-        round_u(on_scalar, LAST, 3, 1)
-        round_u(on_vector, LAST, 2, 1)
-        quant_u(LAST, 0)
-        quant_u(LAST, 1)
+        def load_words(tile, words, passes):
+            nc.sync.dma_start(
+                out=tile[:].bitcast(I32).rearrange("p (s n) -> p s n", s=passes),
+                in_=words.bitcast(I32).rearrange("s p n -> p s n"),
+            )
 
         every = list(range(GROUPS))
-        for n in range(3):
-            stage2(n, [1])
-        for n in range(3, EARLY):
+
+        nc.scalar.activation(warm[:], warm[:], SIGMOID)
+
+        load_x(0, 1)
+        load_x(1, 1)
+        load_scales(down_sc, down_scales, 2)
+        load_x(2, 1)
+        load_x(3, 1)
+        load_words(down_sb, down_words, 2)
+        load_x(4, 2)
+        load_pos(0, 2)
+        load_x(6, 2)
+        load_mix_scales()
+        load_pos(2, 2)
+        load_x(8, 2)
+        load_x(10, 2)
+        load_pos(4, 4)
+        load_x(12, 2)
+        load_mix(0)
+        load_x(14, 2)
+        load_pos(8, 4)
+
+        def later_loads():
+            spread_mix_scales(1)
+            load_pos(12, 4)
+            load_mix(1)
+            spread_mix_scales(2)
+            nc.sync.dma_start(out=keep_sb[:], in_=keep.rearrange("(g p t) -> p g t", p=P, t=4))
+            load_gate(0, 2)
+            spread_mix_scales(3)
+            load_mix(2)
+            load_words(up_sb, up_words, 1)
+            load_scales(up_sc, up_scales, 1)
+            load_gate(2, 2)
+            load_gate(4, 4)
+            load_mix(3)
+            load_gate(8, 4)
+            load_gate(12, 4)
+
+        for n in range(4):
+            if n:
+                sort_x(on_vector, n)
+            turn_x(n)
+            copy_x(n)
+        quant_x(0, 1)
+        quant_x(1, 1)
+        stage1(0)
+        stage1(1)
+        sort_x(on_vector, 4)
+        sort_x(on_scalar, 5)
+        quant_x(2, 2)
+        for n in (4, 5):
+            turn_x(n)
+            copy_x(n)
+        add_pos(0)
+        sort_x(on_vector, 6)
+        add_pos(1)
+        sort_x(on_vector, 7)
+        stage1(2)
+        stage1(3)
+        deal_mix_scales(0)
+        quant_x(4, 2)
+        add_pos(2)
+        add_pos(3)
+
+        for g in range(1, LAST):
+            fresh = range(4 * g + 2, 4 * g + 6)
+            for n in fresh:
+                turn_x(n)
+                copy_x(n)
+            quant_x(fresh[0], 2)
+            if g == 1:
+                deal_mix_scales(1)
+                later_loads()
+            else:
+                quant_u(g - 2, 0, R)
+            quant_x(fresh[2], 2)
+            for n in range(4 * g, 4 * g + 4):
+                stage1(n)
+            round_u_gpsimd(g - 1, 0, G_COLS)
+            if g == 1:
+                sort_x(on_scalar, 4 * g + 6)
+                sort_x(on_scalar, 4 * g + 7)
+            else:
+                deal_mix(on_scalar, 0, 2)
+            round_u(on_scalar, g - 1, G_COLS, R)
+            for n in range(4 * g, 4 * g + 4):
+                add_pos(n)
+
+        for n in (14, 15):
+            turn_x(n)
+            copy_x(n)
+        quant_x(14, 2)
+        quant_u(1, 0, R)
+        stage1(12)
+        stage1(13)
+        stage2(0, [0])
+        stage2(1, [0])
+        stage1(14)
+        stage1(15)
+        round_u_gpsimd(2, 0, G_COLS)
+        deal_mix(on_scalar, 2, 2)
+        round_u(on_scalar, 2, G_COLS, R)
+        deal_mix(on_scalar, 4, 2)
+        for n in range(12, 16):
+            add_pos(n)
+        quant_u(2, 0, R)
+        round_u(on_vector, LAST, 0, 256)
+        round_u(on_scalar, LAST, 256, R)
+        quant_u(LAST, 256, R)
+        quant_u(LAST, 0, 256)
+        stage2(0, [1])
+        stage2(1, [1])
+        for n in range(2, EARLY):
             stage2(n, [0, 1])
+        stage2(EARLY, [0])
         for n in range(EARLY):
             stage2(n, [2])
-        sigmoid_gate(0)
-        sigmoid_gate(1)
-        deal_mix(on_scalar, 8, 2)
-        sigmoid_gate(2)
-        deal_mix(on_vector, 5, 1)
-        deal_mix(on_vector, 6, 2)
         for n in range(EARLY):
             stage2(n, [LAST])
 
-        stage2(5, every)
+        deal_mix(on_gpsimd, 6, 2, "hold0")
+        deal_mix(on_gpsimd, 8, 2)
+        sigmoid_gate(0)
+        sigmoid_gate(1)
+        sigmoid_gate(2)
+        stage2(5, [1])
         add_u(0)
         add_u(1)
-        turn_v([0, 1])
+        turn_v(0, 2)
+        copy_v(0, 2)
         sigmoid_gate(3)
+        sigmoid_gate(4)
+        sigmoid_gate(5, 0, BANK)
+        stage2(5, [2, 3])
         stage2(6, every)
-        for n in range(2, 6):
-            add_u(n)
-        quant_v(0)
-        quant_v(1)
-        turn_v([2, 3, 4, 5], borrowed_first=True)
+        add_u(2)
+        add_u(3)
+        quant_v(0, 2)
+        deal_mix(on_gpsimd, 10, 2, "hold2")
+        deal_mix(on_gpsimd, 12, 2)
+        add_u(4)
+        add_u(5)
+        add_u(6)
         stage3(0)
         stage3(1)
-        move_right_half(1)
-        sigmoid_gate(4)
-        add_u(6)
-        gate_out(0, 0)
-        quant_v(2)
-        stage2(7, every)
-        stage3(2)
-        gate_out(0, 1)
-        quant_v(3)
-        move_right_half(2)
-        sigmoid_gate(5)
-        sigmoid_gate(6)
-        stage3(3)
-        gate_out(1, 0)
-        quant_v(4)
-        quant_v(5)
-        gate_out(1, 1)
-        deal_mix(on_gpsimd, 10, 2)
-        stage3(4)
-        add_u(7)
-        gate_both(2)
-        deal_mix(on_gpsimd, 12, 2)
-        sigmoid_gate(7)
-        sigmoid_gate(8)
+        gate_both(0)
 
-        stage2(8, every)
-        stage3(5)
-        gate_both(3)
-        gate_both(4)
-        add_u(8)
-        stage2(9, every)
-        add_u(9)
-        stage2(10, every)
-        gate_both(5)
-        turn_v([6, 7, 8, 9])
-        sigmoid_gate(9)
-        add_u(10)
-        stage2(11, every)
-        for n in range(6, 10):
-            quant_v(n)
-        deal_mix(on_gpsimd, 14, 2, "after_v9")
-        stage3(6)
-        stage3(7)
-        sigmoid_gate(10)
-        move_right_half(7)
-        sigmoid_gate(11)
-        add_u(11)
-        gate_both(6)
-        gate_both(7)
-        stage3(8)
+        def round_of_four(a, e, sigmoids):
+            turn_v(a, 2)
+            turn_v(a + 2, 2)
+            copy_v(a, 2)
+            copy_v(a + 2, 2)
+            stage2(e, every)
+            quant_v(a, 2)
+            quant_v(a + 2, 2)
+            gate_both(a - 1)
+            add_u(e)
+            stage3(a)
+            sigmoids[0]()
+            move_right_half(a)
+            gate_both(a)
+            stage2(e + 1, every)
+            add_u(e + 1)
+            stage3(a + 1)
+            sigmoids[1]()
+            move_right_half(a + 1)
+            gate_both(a + 1)
+            stage2(e + 2, every)
+            add_u(e + 2)
+            stage3(a + 2)
+            stage3(a + 3)
+            sigmoids[2]()
+            gate_both(a + 2)
 
-        last_round = TILES - 2
-        for n in (last_round - 2, last_round):
-            stage2(n, every)
-            if n == last_round:
-                add_u(n - 1)
-            gate_both(n - 4)
-            turn_v([n - 2, n - 1])
-            stage3(n - 3)
-            move_right_half(n - 3)
-            stage2(n + 1, every if n < last_round else every[:LAST])
-            add_u(n)
-            quant_v(n - 2)
-            gate_out(n - 3, 0)
-            quant_v(n - 1)
-            sigmoid_gate(n)
-            if n < last_round:
-                sigmoid_gate(n + 1)
-                gate_out(n - 3, 1)
-            stage3(n - 2)
+        def halves(first, count):
+            def run():
+                for i in range(first, first + count):
+                    if i % 2 == 0 and i + 1 < first + count:
+                        sigmoid_gate(i // 2)
+                    elif i % 2 == 0:
+                        sigmoid_gate(i // 2, 0, BANK)
+                    elif i == first:
+                        sigmoid_gate(i // 2, BANK)
+            return run
 
-        n = TILES
-        stage2(n - 1, [LAST])
-        turn_v([n - 2])
-        sigmoid_gate(n - 1)
-        gate_out(n - 4, 0)
-        gate_out(n - 5, 1)
-        add_u(n - 1)
-        stage3(n - 3)
-        gate_out(n - 4, 1)
-        quant_v(n - 2)
-        turn_v([n - 1])
-        gate_both(n - 3)
-        stage3(n - 2)
-        quant_v(n - 1)
-        stage3(n - 1)
-        gate_both(n - 2)
-        gate_both(n - 1)
+        round_of_four(2, 7, [halves(11, 2), halves(13, 2), halves(15, 3)])
+        round_of_four(6, 10, [halves(18, 2), halves(20, 2), halves(22, 3)])
+        deal_mix(on_gpsimd, 14, 2)
+
+        turn_v(10, 2)
+        turn_v(12, 1)
+        copy_v(10, 2)
+        copy_v(12, 1)
+        stage2(13, every)
+        stage2(14, [0, 1])
+        gate_out(9, 0)
+        quant_v(10, 2)
+        quant_v(12, 1)
+        gate_out(9, 1)
+        add_u(13)
+        stage3(10)
+        halves(25, 2)()
+        move_right_half(10)
+        stage2(14, [2, 3])
+        gate_both(10)
+        add_u(14)
+        stage3(11)
+        halves(27, 2)()
+        gate_both(11)
+        stage2(15, [0])
+        turn_v(13, 2)
+        copy_v(13, 2)
+        halves(29, 2)()
+        stage2(15, [1, 2, 3])
+        quant_v(13, 2)
+        add_u(15)
+        stage3(12)
+        halves(31, 1)()
+        stage3(13)
+        turn_v(15, 1)
+        copy_v(15, 1)
+        move_right_half(13)
+        gate_both(12)
+        stage3(14)
+        move_right_half(14)
+        quant_v(15, 1)
+        gate_out(13, 0)
+        stage3(15)
+        gate_out(14, 0)
+        gate_out(13, 1)
+        gate_both(15)
+        gate_out(14, 1)

@@ -25,9 +25,11 @@ LAST = GROUPS - 1
 BANK = 512
 ALIGN = 256
 EARLY = 5
-G_COLS = 384
-HOLDS = {4: "hold0", 6: "hold1"}
-U_HOLDS = ("hold0", "hold1", "hold1", "hold0")
+G_COLS = 256
+HOLDS = {4: "hold0", 6: "hold1", 7: "hold0"}
+U_HOLDS = ("hold0", "hold1", "hold0", "hold1")
+V_HOLDS = {0: "hold2", 4: "hold3", 8: "hold4", 13: "hold0"}
+OWN_BUFFER = {12: 13}
 HALVED = range(TILES - 6, TILES)
 
 
@@ -206,20 +208,22 @@ def tile_low_rank_row_mixer_t2_kernel(
                 op=ADD,
             )
 
-        def rounded(g):
-            if g not in ug:
-                ug[g] = const.tile([P, 4 * R], BF16, name="ug", tag=U_HOLDS[g], align_bytes=ALIGN)
-            return ug[g]
+        def rounded(g, first, last):
+            if first == 0:
+                ug[g, first] = const.tile([P, 4 * last], BF16, name="ug", tag=U_HOLDS[g], align_bytes=ALIGN)
+            else:
+                ug[g, first] = work.tile([P, 4 * (last - first)], BF16, name="ug", bufs=2, align_bytes=ALIGN)
+            return ug[g, first]
 
         def round_u(copy, g, first, last):
             copy(
-                out=rounded(g)[:, 4 * first : 4 * last].rearrange("p (c i t) -> p c t i", t=4, i=4),
+                out=rounded(g, first, last)[:].rearrange("p (c i t) -> p c t i", t=4, i=4),
                 in_=u[g][:, :, first:last].rearrange("p t (c i) -> p c t i", i=4),
             )
 
         def round_u_gpsimd(g, first, last):
             nc.gpsimd.tensor_scalar(
-                out=rounded(g)[:, 4 * first : 4 * last].rearrange("p (c t) -> p c t", t=4),
+                out=rounded(g, first, last)[:].rearrange("p (c t) -> p c t", t=4),
                 in0=u[g][:, :, first:last].rearrange("p t c -> p c t"),
                 scalar1=1.0,
                 scalar2=0.0,
@@ -232,7 +236,7 @@ def tile_low_rank_row_mixer_t2_kernel(
                 uc[g] = const.tile([P, R], U32, name="uc%d" % g, align_bytes=ALIGN)
                 us[g] = const.tile([P, R], U8, name="us%d" % g, align_bytes=ALIGN)
             nc.vector.quantize_mx(
-                out=uc[g][:, first:last].bitcast(FP8X4), scales=us[g][:, first:last], in_=ug[g][:, 4 * first : 4 * last]
+                out=uc[g][:, first:last].bitcast(FP8X4), scales=us[g][:, first:last], in_=ug[g, first][:]
             )
 
         ring, s2_banks, vb, vt, vg, vc, vs, s3_banks, sig, moved, o_tiles = [], {}, {}, {}, {}, {}, {}, {}, {}, {}, {}
@@ -272,18 +276,18 @@ def tile_low_rank_row_mixer_t2_kernel(
                     nc.tensor.transpose(vt[first][:, col : col + P], words[:, P * h : P * (h + 1)], ident[:])
 
         def copy_v(first, count):
-            if first == 0:
-                vg[first] = const.tile([P, count * R], BF16, name="vg", tag="hold2", align_bytes=ALIGN)
+            if first in V_HOLDS:
+                vg[first] = const.tile([P, count * R], BF16, name="vg", tag=V_HOLDS[first], align_bytes=ALIGN)
             else:
-                vg[first] = work.tile([P, count * R], BF16, name="vg", bufs=3, align_bytes=ALIGN)
+                vg[first] = work.tile([P, count * R], BF16, name="vg", bufs=2, align_bytes=ALIGN)
             on_scalar(
                 out=vg[first][:].bitcast(F32).rearrange("m (i p h) -> m i p h", i=count, h=2),
                 in_=vt[first][:, : 2 * P * count].rearrange("m (i h p) -> m i p h", i=count, h=2),
             )
 
         def quant_v(first, count):
-            codes = work.tile([P, count * P], U32, name="vc", bufs=4, align_bytes=ALIGN)
-            scales = work.tile([P, count * P], U8, name="vs", bufs=4, align_bytes=ALIGN)
+            codes = work.tile([P, count * P], U32, name="vc", bufs=3, align_bytes=ALIGN)
+            scales = work.tile([P, count * P], U8, name="vs", bufs=3, align_bytes=ALIGN)
             nc.vector.quantize_mx(out=codes[:].bitcast(FP8X4), scales=scales[:], in_=vg[first][:])
             for i in range(count):
                 vc[first + i] = codes[:, P * i : P * (i + 1)]
@@ -311,20 +315,27 @@ def tile_low_rank_row_mixer_t2_kernel(
             moved[n] = work.tile([P, BANK], F32, name="moved", bufs=2, align_bytes=ALIGN)
             on_scalar(out=moved[n][:], in_=s3_banks[n, 1][:])
 
+        products = {}
+
         def gate_out(n, half):
             cols = slice(BANK * half, BANK * (half + 1))
             rows = out_rows[n // 4][n % 4]
             if half == 0:
                 o_tiles[n] = work.tile([P, D], F32, name="o", tag="rows", bufs=6, align_bytes=ALIGN)
             product = o_tiles[n][:, cols]
+            if half == 1 and n in OWN_BUFFER:
+                own = const.tile([P, BANK], F32, name="o", tag=V_HOLDS[OWN_BUFFER[n]], align_bytes=ALIGN)
+                product = own[:]
             if half == 1 and n in moved:
                 nc.gpsimd.tensor_tensor(out=product, in0=moved[n][:], in1=sig[n][:, cols], op=MULT)
             else:
                 nc.vector.tensor_tensor(out=product, in0=s3_banks[n, half][:], in1=sig[n][:, cols], op=MULT)
-            if n in HALVED:
-                nc.sync.dma_start(out=rows[:, cols], in_=product)
-            elif half == 1:
+            products[n, half] = product
+            if half == 1 and n not in HALVED:
                 nc.sync.dma_start(out=rows, in_=o_tiles[n][:])
+
+        def store_half(n, half):
+            nc.sync.dma_start(out=out_rows[n // 4][n % 4][:, BANK * half : BANK * (half + 1)], in_=products[n, half])
 
         def gate_both(n):
             gate_out(n, 0)
@@ -412,14 +423,14 @@ def tile_low_rank_row_mixer_t2_kernel(
                 deal_mix_scales(1)
                 later_loads()
             else:
-                quant_u(g - 2, 0, R)
+                quant_u(g - 2, G_COLS, R)
+                quant_u(g - 2, 0, G_COLS)
             quant_x(fresh[2], 2)
             for n in range(4 * g, 4 * g + 4):
                 stage1(n)
             round_u_gpsimd(g - 1, 0, G_COLS)
             if g == 1:
                 sort_x(on_scalar, 4 * g + 6)
-                sort_x(on_scalar, 4 * g + 7)
             else:
                 deal_mix(on_scalar, 0, 2)
             round_u(on_scalar, g - 1, G_COLS, R)
@@ -429,41 +440,43 @@ def tile_low_rank_row_mixer_t2_kernel(
         for n in (14, 15):
             turn_x(n)
             copy_x(n)
+        quant_u(1, G_COLS, R)
+        quant_u(1, 0, G_COLS)
         quant_x(14, 2)
-        quant_u(1, 0, R)
         stage1(12)
         stage1(13)
-        stage2(0, [0])
-        stage2(1, [0])
+        for s in range(2):
+            stage2(0, [s])
+            stage2(1, [s])
         stage1(14)
         stage1(15)
         round_u_gpsimd(2, 0, G_COLS)
         deal_mix(on_scalar, 2, 2)
         round_u(on_scalar, 2, G_COLS, R)
-        deal_mix(on_scalar, 4, 2)
+        deal_mix(on_scalar, 4, 1)
         for n in range(12, 16):
             add_pos(n)
-        quant_u(2, 0, R)
+        quant_u(2, G_COLS, R)
+        quant_u(2, 0, G_COLS)
         round_u(on_vector, LAST, 0, 256)
         round_u(on_scalar, LAST, 256, R)
         quant_u(LAST, 256, R)
         quant_u(LAST, 0, 256)
-        stage2(0, [1])
-        stage2(1, [1])
         for n in range(2, EARLY):
             stage2(n, [0, 1])
-        stage2(EARLY, [0])
         for n in range(EARLY):
             stage2(n, [2])
         for n in range(EARLY):
             stage2(n, [LAST])
 
-        deal_mix(on_gpsimd, 6, 2, "hold0")
-        deal_mix(on_gpsimd, 8, 2)
+        deal_mix(on_gpsimd, 6, 2, "hold1")
+        deal_mix(on_vector, 5, 1)
+        deal_mix(on_vector, 8, 1)
+        deal_mix(on_gpsimd, 9, 1)
         sigmoid_gate(0)
         sigmoid_gate(1)
         sigmoid_gate(2)
-        stage2(5, [1])
+        stage2(5, [0])
         add_u(0)
         add_u(1)
         turn_v(0, 2)
@@ -471,13 +484,13 @@ def tile_low_rank_row_mixer_t2_kernel(
         sigmoid_gate(3)
         sigmoid_gate(4)
         sigmoid_gate(5, 0, BANK)
-        stage2(5, [2, 3])
+        stage2(5, [1, 2, 3])
         stage2(6, every)
         add_u(2)
         add_u(3)
         quant_v(0, 2)
         deal_mix(on_gpsimd, 10, 2, "hold2")
-        deal_mix(on_gpsimd, 12, 2)
+        deal_mix(on_gpsimd, 12, 1)
         add_u(4)
         add_u(5)
         add_u(6)
@@ -485,7 +498,7 @@ def tile_low_rank_row_mixer_t2_kernel(
         stage3(1)
         gate_both(0)
 
-        def round_of_four(a, e, sigmoids):
+        def round_of_four(a, e, sigmoids, deals):
             turn_v(a, 2)
             turn_v(a + 2, 2)
             copy_v(a, 2)
@@ -493,6 +506,7 @@ def tile_low_rank_row_mixer_t2_kernel(
             stage2(e, every)
             quant_v(a, 2)
             quant_v(a + 2, 2)
+            deal_mix(on_gpsimd, deals[0], deals[1], V_HOLDS[a + 2])
             gate_both(a - 1)
             add_u(e)
             stage3(a)
@@ -523,16 +537,15 @@ def tile_low_rank_row_mixer_t2_kernel(
                         sigmoid_gate(i // 2, BANK)
             return run
 
-        round_of_four(2, 7, [halves(11, 2), halves(13, 2), halves(15, 3)])
-        round_of_four(6, 10, [halves(18, 2), halves(20, 2), halves(22, 3)])
-        deal_mix(on_gpsimd, 14, 2)
+        round_of_four(2, 7, [halves(11, 2), halves(13, 2), halves(15, 3)], (13, 1))
+        round_of_four(6, 10, [halves(18, 2), halves(20, 2), halves(22, 3)], (14, 2))
 
         turn_v(10, 2)
         turn_v(12, 1)
         copy_v(10, 2)
         copy_v(12, 1)
         stage2(13, every)
-        stage2(14, [0, 1])
+        stage2(14, [0])
         gate_out(9, 0)
         quant_v(10, 2)
         quant_v(12, 1)
@@ -541,32 +554,39 @@ def tile_low_rank_row_mixer_t2_kernel(
         stage3(10)
         halves(25, 2)()
         move_right_half(10)
-        stage2(14, [2, 3])
+        stage2(14, [1, 2, 3])
         gate_both(10)
+        store_half(10, 0)
         add_u(14)
         stage3(11)
+        stage3(12)
         halves(27, 2)()
         gate_both(11)
-        stage2(15, [0])
+        store_half(11, 0)
+        store_half(10, 1)
+        store_half(11, 1)
         turn_v(13, 2)
         copy_v(13, 2)
+        move_right_half(12)
         halves(29, 2)()
-        stage2(15, [1, 2, 3])
+        stage2(15, every)
+        gate_out(12, 0)
+        store_half(12, 0)
         quant_v(13, 2)
+        gate_out(12, 1)
         add_u(15)
-        stage3(12)
-        halves(31, 1)()
         stage3(13)
         turn_v(15, 1)
         copy_v(15, 1)
-        move_right_half(13)
-        gate_both(12)
+        halves(31, 1)()
+        gate_both(13)
+        store_half(13, 0)
+        store_half(12, 1)
+        store_half(13, 1)
         stage3(14)
-        move_right_half(14)
         quant_v(15, 1)
-        gate_out(13, 0)
         stage3(15)
-        gate_out(14, 0)
-        gate_out(13, 1)
-        gate_both(15)
-        gate_out(14, 1)
+        for n in (14, 15):
+            for half in range(2):
+                gate_out(n, half)
+                store_half(n, half)

@@ -24,13 +24,14 @@ TILES = T // P
 LAST = GROUPS - 1
 BANK = 512
 ALIGN = 256
-EARLY = 5
+EARLY = 6
 G_COLS = 256
+G_FIRST = 320
 HOLDS = {4: "hold0", 6: "hold1", 7: "hold0"}
-U_HOLDS = ("hold0", "hold1", "hold0", "hold1")
-V_HOLDS = {0: "hold2", 4: "hold3", 8: "hold4", 13: "hold0"}
-OWN_BUFFER = {12: 13}
-HALVED = range(TILES - 6, TILES)
+U_HOLDS = {(0, 0): "hold0", (1, 0): "hold1", (2, 0): "hold0", (3, 0): "hold1", (3, G_COLS): "hold3"}
+V_HOLDS = {0: "hold2", 12: "hold1", 13: "hold0"}
+OWN_BUFFER = {9: 12, 12: 13}
+HALVED = (9, 10, 11, 12, 13, 14, 15)
 
 
 def tile_low_rank_row_mixer_t2_kernel(
@@ -90,14 +91,14 @@ def tile_low_rank_row_mixer_t2_kernel(
                 x_sb[first + i] = rows[:, D * i : D * (i + 1)]
 
         def load_pos(first, count):
-            rows = work.tile([P, count, R], BF16, name="pos", tag="wide", bufs=6, align_bytes=ALIGN)
+            rows = work.tile([P, count, R], BF16, name="pos", tag="wide", bufs=8, align_bytes=ALIGN)
             g, t = divmod(first, 4)
             nc.sync.dma_start(out=rows[:], in_=pos_rows[g][:, t : t + count])
             for i in range(count):
                 pos_sb[first + i] = rows[:, i]
 
-        def load_gate(first, count):
-            rows = const.tile([P, count, D], BF16, name="gate%d" % first, align_bytes=ALIGN)
+        def load_gate(first, count, tag=None):
+            rows = const.tile([P, count, D], BF16, name="gate", tag=tag or "gate%d" % first, align_bytes=ALIGN)
             g, t = divmod(first, 4)
             nc.sync.dma_start(out=rows[:], in_=gate_rows[g][:, t : t + count])
             for i in range(count):
@@ -200,7 +201,7 @@ def tile_low_rank_row_mixer_t2_kernel(
         def add_pos(n):
             g, t = divmod(n, 4)
             if t == 0:
-                u[g] = const.tile([P, 4, R], F32, name="u%d" % g, align_bytes=ALIGN)
+                u[g] = const.tile([P, 4, R], F32, name="u", tag="u%d" % g, align_bytes=ALIGN)
             nc.vector.tensor_tensor(
                 out=u[g][:, t].rearrange("p (h m e) -> p m h e", h=2, e=2),
                 in0=s1_banks[n][:].rearrange("p (m h e) -> p m h e", h=2, e=2),
@@ -209,21 +210,24 @@ def tile_low_rank_row_mixer_t2_kernel(
             )
 
         def rounded(g, first, last):
-            if first == 0:
-                ug[g, first] = const.tile([P, 4 * last], BF16, name="ug", tag=U_HOLDS[g], align_bytes=ALIGN)
+            if g == 0 and first > 0:
+                return ug[0, 0][:, 4 * first : 4 * last]
+            width = 4 * (R if g == 0 else last - first)
+            if (g, first) in U_HOLDS:
+                ug[g, first] = const.tile([P, width], BF16, name="ug", tag=U_HOLDS[g, first], align_bytes=ALIGN)
             else:
-                ug[g, first] = work.tile([P, 4 * (last - first)], BF16, name="ug", bufs=2, align_bytes=ALIGN)
-            return ug[g, first]
+                ug[g, first] = work.tile([P, width], BF16, name="ug", tag="single", bufs=4, align_bytes=ALIGN)
+            return ug[g, first][:, : 4 * (last - first)]
 
         def round_u(copy, g, first, last):
             copy(
-                out=rounded(g, first, last)[:].rearrange("p (c i t) -> p c t i", t=4, i=4),
+                out=rounded(g, first, last).rearrange("p (c i t) -> p c t i", t=4, i=4),
                 in_=u[g][:, :, first:last].rearrange("p t (c i) -> p c t i", i=4),
             )
 
         def round_u_gpsimd(g, first, last):
             nc.gpsimd.tensor_scalar(
-                out=rounded(g, first, last)[:].rearrange("p (c t) -> p c t", t=4),
+                out=rounded(g, first, last).rearrange("p (c t) -> p c t", t=4),
                 in0=u[g][:, :, first:last].rearrange("p t c -> p c t"),
                 scalar1=1.0,
                 scalar2=0.0,
@@ -279,7 +283,7 @@ def tile_low_rank_row_mixer_t2_kernel(
             if first in V_HOLDS:
                 vg[first] = const.tile([P, count * R], BF16, name="vg", tag=V_HOLDS[first], align_bytes=ALIGN)
             else:
-                vg[first] = work.tile([P, count * R], BF16, name="vg", bufs=2, align_bytes=ALIGN)
+                vg[first] = work.tile([P, count * R], BF16, name="vg", tag="single", bufs=4, align_bytes=ALIGN)
             on_scalar(
                 out=vg[first][:].bitcast(F32).rearrange("m (i p h) -> m i p h", i=count, h=2),
                 in_=vt[first][:, : 2 * P * count].rearrange("m (i h p) -> m i p h", i=count, h=2),
@@ -308,11 +312,11 @@ def tile_low_rank_row_mixer_t2_kernel(
 
         def sigmoid_gate(n, first=0, last=D):
             if first == 0:
-                sig[n] = work.tile([P, D], F32, name="sig", tag="wide", bufs=6, align_bytes=ALIGN)
+                sig[n] = work.tile([P, D], F32, name="sig", tag="wide", bufs=8, align_bytes=ALIGN)
             nc.scalar.activation(sig[n][:, first:last], gate_sb[n][:, first:last], SIGMOID)
 
         def move_right_half(n):
-            moved[n] = work.tile([P, BANK], F32, name="moved", bufs=2, align_bytes=ALIGN)
+            moved[n] = work.tile([P, BANK], F32, name="moved", tag="sorted_x", bufs=4, align_bytes=ALIGN)
             on_scalar(out=moved[n][:], in_=s3_banks[n, 1][:])
 
         products = {}
@@ -385,7 +389,6 @@ def tile_low_rank_row_mixer_t2_kernel(
             load_gate(4, 4)
             load_mix(3)
             load_gate(8, 4)
-            load_gate(12, 4)
 
         for n in range(4):
             if n:
@@ -418,22 +421,27 @@ def tile_low_rank_row_mixer_t2_kernel(
             for n in fresh:
                 turn_x(n)
                 copy_x(n)
-            quant_x(fresh[0], 2)
+            if g == 1:
+                quant_x(fresh[0], 2)
+            else:
+                quant_x(fresh[0], 1)
+                quant_x(fresh[1], 1)
             if g == 1:
                 deal_mix_scales(1)
                 later_loads()
             else:
-                quant_u(g - 2, G_COLS, R)
-                quant_u(g - 2, 0, G_COLS)
+                quant_u(0, 0, R)
             quant_x(fresh[2], 2)
             for n in range(4 * g, 4 * g + 4):
                 stage1(n)
-            round_u_gpsimd(g - 1, 0, G_COLS)
+            split = G_FIRST if g == 1 else G_COLS
+            round_u_gpsimd(g - 1, 0, split)
             if g == 1:
                 sort_x(on_scalar, 4 * g + 6)
+                sort_x(on_scalar, 4 * g + 7)
             else:
                 deal_mix(on_scalar, 0, 2)
-            round_u(on_scalar, g - 1, G_COLS, R)
+            round_u(on_scalar, g - 1, split, R)
             for n in range(4 * g, 4 * g + 4):
                 add_pos(n)
 
@@ -452,16 +460,17 @@ def tile_low_rank_row_mixer_t2_kernel(
         stage1(15)
         round_u_gpsimd(2, 0, G_COLS)
         deal_mix(on_scalar, 2, 2)
-        round_u(on_scalar, 2, G_COLS, R)
         deal_mix(on_scalar, 4, 1)
+        round_u(on_scalar, 2, G_COLS, R)
+        deal_mix(on_scalar, 5, 1)
         for n in range(12, 16):
             add_pos(n)
-        quant_u(2, G_COLS, R)
         quant_u(2, 0, G_COLS)
+        quant_u(2, G_COLS, R)
         round_u(on_vector, LAST, 0, 256)
         round_u(on_scalar, LAST, 256, R)
-        quant_u(LAST, 256, R)
         quant_u(LAST, 0, 256)
+        quant_u(LAST, 256, R)
         for n in range(2, EARLY):
             stage2(n, [0, 1])
         for n in range(EARLY):
@@ -469,98 +478,97 @@ def tile_low_rank_row_mixer_t2_kernel(
         for n in range(EARLY):
             stage2(n, [LAST])
 
-        deal_mix(on_gpsimd, 6, 2, "hold1")
-        deal_mix(on_vector, 5, 1)
+        deal_mix(on_vector, 6, 2)
         deal_mix(on_vector, 8, 1)
-        deal_mix(on_gpsimd, 9, 1)
+        deal_mix(on_gpsimd, 9, 1, "hold3")
+        deal_mix(on_gpsimd, 10, 2)
         sigmoid_gate(0)
         sigmoid_gate(1)
         sigmoid_gate(2)
-        stage2(5, [0])
+        sigmoid_gate(3)
+        stage2(6, [0])
         add_u(0)
         add_u(1)
         turn_v(0, 2)
         copy_v(0, 2)
-        sigmoid_gate(3)
         sigmoid_gate(4)
-        sigmoid_gate(5, 0, BANK)
-        stage2(5, [1, 2, 3])
-        stage2(6, every)
+        sigmoid_gate(5)
+        sigmoid_gate(6, 0, BANK)
+        stage2(6, [1, 2, 3])
+        stage2(7, every)
         add_u(2)
         add_u(3)
-        quant_v(0, 2)
-        deal_mix(on_gpsimd, 10, 2, "hold2")
-        deal_mix(on_gpsimd, 12, 1)
+        load_gate(12, 4, "u0")
         add_u(4)
+        quant_v(0, 2)
+        deal_mix(on_gpsimd, 12, 2, "hold2")
+        deal_mix(on_gpsimd, 14, 2)
         add_u(5)
         add_u(6)
         stage3(0)
         stage3(1)
         gate_both(0)
-
-        def round_of_four(a, e, sigmoids, deals):
-            turn_v(a, 2)
-            turn_v(a + 2, 2)
-            copy_v(a, 2)
-            copy_v(a + 2, 2)
-            stage2(e, every)
-            quant_v(a, 2)
-            quant_v(a + 2, 2)
-            deal_mix(on_gpsimd, deals[0], deals[1], V_HOLDS[a + 2])
-            gate_both(a - 1)
-            add_u(e)
-            stage3(a)
-            sigmoids[0]()
-            move_right_half(a)
-            gate_both(a)
-            stage2(e + 1, every)
-            add_u(e + 1)
-            stage3(a + 1)
-            sigmoids[1]()
-            move_right_half(a + 1)
-            gate_both(a + 1)
-            stage2(e + 2, every)
-            add_u(e + 2)
-            stage3(a + 2)
-            stage3(a + 3)
-            sigmoids[2]()
-            gate_both(a + 2)
+        add_u(7)
 
         def halves(first, count):
-            def run():
-                for i in range(first, first + count):
-                    if i % 2 == 0 and i + 1 < first + count:
-                        sigmoid_gate(i // 2)
-                    elif i % 2 == 0:
-                        sigmoid_gate(i // 2, 0, BANK)
-                    elif i == first:
-                        sigmoid_gate(i // 2, BANK)
-            return run
+            for i in range(first, first + count):
+                if i % 2 == 0 and i + 1 < first + count:
+                    sigmoid_gate(i // 2)
+                elif i % 2 == 0:
+                    sigmoid_gate(i // 2, 0, BANK)
+                elif i == first:
+                    sigmoid_gate(i // 2, BANK)
 
-        round_of_four(2, 7, [halves(11, 2), halves(13, 2), halves(15, 3)], (13, 1))
-        round_of_four(6, 10, [halves(18, 2), halves(20, 2), halves(22, 3)], (14, 2))
+        def begin_round(a, count, e):
+            turn_v(a, 2)
+            turn_v(a + 2, count - 2)
+            copy_v(a, 2)
+            copy_v(a + 2, count - 2)
+            if a == 10:
+                move_right_half(a - 1)
+            stage2(e, every)
+            stage2(e + 1, [0, 1])
+            gate_out(a - 1, 0)
+            if a == 10:
+                store_half(a - 1, 0)
+            quant_v(a, 2)
+            quant_v(a + 2, count - 2)
+            gate_out(a - 1, 1)
 
-        turn_v(10, 2)
-        turn_v(12, 1)
-        copy_v(10, 2)
-        copy_v(12, 1)
-        stage2(13, every)
-        stage2(14, [0])
-        gate_out(9, 0)
-        quant_v(10, 2)
-        quant_v(12, 1)
-        gate_out(9, 1)
+        for a, e, h in ((2, 8, 13), (6, 10, 18)):
+            begin_round(a, 4, e)
+            add_u(e)
+            stage3(a)
+            halves(h, 2)
+            move_right_half(a)
+            gate_both(a)
+            stage2(e + 1, [2, 3])
+            add_u(e + 1)
+            stage3(a + 1)
+            halves(h + 2, 1 if a == 2 else 2)
+            move_right_half(a + 1)
+            gate_both(a + 1)
+            if a == 6:
+                stage2(e + 2, every)
+                add_u(e + 2)
+            stage3(a + 2)
+            stage3(a + 3)
+            halves(h + 3 if a == 2 else h + 4, 2)
+            gate_both(a + 2)
+
+        begin_round(10, 3, 13)
         add_u(13)
         stage3(10)
-        halves(25, 2)()
+        halves(24, 2)
         move_right_half(10)
-        stage2(14, [1, 2, 3])
+        stage2(14, [2, 3])
         gate_both(10)
         store_half(10, 0)
+        store_half(9, 1)
         add_u(14)
         stage3(11)
         stage3(12)
-        halves(27, 2)()
+        halves(26, 2)
         gate_both(11)
         store_half(11, 0)
         store_half(10, 1)
@@ -568,7 +576,7 @@ def tile_low_rank_row_mixer_t2_kernel(
         turn_v(13, 2)
         copy_v(13, 2)
         move_right_half(12)
-        halves(29, 2)()
+        halves(28, 2)
         stage2(15, every)
         gate_out(12, 0)
         store_half(12, 0)
@@ -578,7 +586,7 @@ def tile_low_rank_row_mixer_t2_kernel(
         stage3(13)
         turn_v(15, 1)
         copy_v(15, 1)
-        halves(31, 1)()
+        halves(30, 2)
         gate_both(13)
         store_half(13, 0)
         store_half(12, 1)

@@ -29,9 +29,9 @@ G_COLS = 256
 G_FIRST = 320
 HOLDS = {4: "hold0", 6: "hold1", 7: "hold0"}
 U_HOLDS = {(0, 0): "hold0", (1, 0): "hold1", (2, 0): "hold0", (3, 0): "hold1", (3, G_COLS): "hold3"}
-V_HOLDS = {0: "hold2", 12: "hold1", 13: "hold0"}
-OWN_BUFFER = {9: 12, 12: 13}
-HALVED = (9, 10, 11, 12, 13, 14, 15)
+V_HOLDS = {0: "hold2", 4: "hold4", 8: "hold0", 12: "hold1"}
+OWN_BUFFER = {1: 4, 5: 8, 9: 12}
+HALVED = (1, 2, 5, 6, 9, 10, 11, 12, 13, 14, 15)
 
 
 def tile_low_rank_row_mixer_t2_kernel(
@@ -78,6 +78,7 @@ def tile_low_rank_row_mixer_t2_kernel(
         keep_sb = const.tile([P, GROUPS, 4], BF16, name="keep_sb", align_bytes=ALIGN)
         down_sb = const.tile([P, 2 * 2 * R], U8, name="down_sb", align_bytes=ALIGN)
         up_sb = const.tile([P, 2 * D], U8, name="up_sb", align_bytes=ALIGN)
+        mix_all = const.tile([P, GROUPS * 2 * T], U8, name="mix_all", align_bytes=ALIGN)
         x_sb, pos_sb, gate_sb, mix_raw, mix_sb = {}, {}, {}, {}, {}
 
         def load_x(first, count):
@@ -104,22 +105,23 @@ def tile_low_rank_row_mixer_t2_kernel(
             for i in range(count):
                 gate_sb[first + i] = rows[:, i]
 
-        def load_mix(g):
-            mix_raw[g] = work.tile([P, GROUPS * 1024], U8, name="mix_raw", bufs=3, align_bytes=ALIGN)
-            nc.sync.dma_start(
-                out=mix_raw[g][:].bitcast(I32).rearrange("p (s n) -> p s n", s=GROUPS),
-                in_=mix_words.bitcast(I32).rearrange("s p n -> p s n")[:, :, 256 * g : 256 * (g + 1)],
-            )
+        def load_mix(s):
+            mix_raw[s] = mix_all[:, 2 * T * s : 2 * T * (s + 1)]
+            nc.sync.dma_start(out=mix_raw[s].bitcast(I32), in_=mix_words.bitcast(I32)[s])
 
-        def deal_mix(copy, first, count, tag=None):
-            dealt = const.tile([P, count * 1024], U8, name="mix", tag=tag or "mix%d" % first, align_bytes=ALIGN)
-            g, t = divmod(first, 4)
-            for i in range(count):
-                mix_sb[first + i] = dealt[:, 1024 * i : 1024 * (i + 1)]
-            copy(
-                out=dealt[:].bitcast(U16).rearrange("p (t c i) -> p c t i", t=count, i=8),
-                in_=mix_raw[g][:].bitcast(U16).rearrange("p (c i t) -> p c t i", t=4, i=8)[:, :, t : t + count],
-            )
+        def deal_mix(copy, passes, groups, tag=None):
+            name = "mix%d_%d" % (passes[0], groups[0])
+            dealt = const.tile([P, T], U8, name="mix", tag=tag or name, align_bytes=ALIGN)
+            words = mix_all[:].bitcast(U16).rearrange("p (s g c i t) -> p s g c t i", s=GROUPS, g=GROUPS, t=4, i=8)
+            if len(passes) == 1:
+                source = words[:, passes[0], groups[0] : groups[0] + 2]
+            else:
+                source = words[:, passes[0] : passes[0] + 2, groups[0]]
+            for j, (s, g) in enumerate((s, g) for s in passes for g in groups):
+                for t in range(4):
+                    col = 2 * P * (4 * j + t)
+                    mix_sb[4 * g + t, s] = dealt[:, col : col + 2 * P]
+            copy(out=dealt[:].bitcast(U16).rearrange("p (j t c i) -> p j c t i", j=2, t=4, i=8), in_=source)
 
         def load_mix_scales():
             src = mix_scales.bitcast(I32)
@@ -256,7 +258,7 @@ def tile_low_rank_row_mixer_t2_kernel(
                 plane = dealt_sc[:] if s == 0 else mix_sc[:, T * (s - 1) : T * s]
                 nc.tensor.matmul_mx(
                     out=s2_banks[n][:],
-                    lhsT=mix_sb[n][:, 2 * P * s : 2 * P * (s + 1)].bitcast(FP4X4),
+                    lhsT=mix_sb[n, s].bitcast(FP4X4),
                     lhsT_scale=plane[:, P * n : P * (n + 1)],
                     rhs=uc[s][:].bitcast(FP8X4),
                     rhs_scale=us[s][:],
@@ -371,23 +373,24 @@ def tile_low_rank_row_mixer_t2_kernel(
         load_pos(4, 4)
         load_x(12, 2)
         load_mix(0)
+        load_pos(8, 2)
         load_x(14, 2)
-        load_pos(8, 4)
+        load_pos(10, 2)
 
         def later_loads():
+            load_mix(1)
             spread_mix_scales(1)
             load_pos(12, 4)
-            load_mix(1)
+            load_mix(2)
             spread_mix_scales(2)
             nc.sync.dma_start(out=keep_sb[:], in_=keep.rearrange("(g p t) -> p g t", p=P, t=4))
             load_gate(0, 2)
+            load_mix(3)
             spread_mix_scales(3)
-            load_mix(2)
+            load_gate(2, 2)
             load_words(up_sb, up_words, 1)
             load_scales(up_sc, up_scales, 1)
-            load_gate(2, 2)
             load_gate(4, 4)
-            load_mix(3)
             load_gate(8, 4)
 
         for n in range(4):
@@ -408,8 +411,10 @@ def tile_low_rank_row_mixer_t2_kernel(
         add_pos(0)
         sort_x(on_vector, 6)
         add_pos(1)
-        sort_x(on_vector, 7)
         stage1(2)
+        for n in (6, 7):
+            turn_x(n)
+            copy_x(n)
         stage1(3)
         deal_mix_scales(0)
         quant_x(4, 2)
@@ -418,7 +423,7 @@ def tile_low_rank_row_mixer_t2_kernel(
 
         for g in range(1, LAST):
             fresh = range(4 * g + 2, 4 * g + 6)
-            for n in fresh:
+            for n in fresh[2 if g == 1 else 0 :]:
                 turn_x(n)
                 copy_x(n)
             if g == 1:
@@ -440,7 +445,7 @@ def tile_low_rank_row_mixer_t2_kernel(
                 sort_x(on_scalar, 4 * g + 6)
                 sort_x(on_scalar, 4 * g + 7)
             else:
-                deal_mix(on_scalar, 0, 2)
+                deal_mix(on_scalar, [0], [0, 1])
             round_u(on_scalar, g - 1, split, R)
             for n in range(4 * g, 4 * g + 4):
                 add_pos(n)
@@ -453,16 +458,14 @@ def tile_low_rank_row_mixer_t2_kernel(
         quant_x(14, 2)
         stage1(12)
         stage1(13)
-        for s in range(2):
-            stage2(0, [s])
-            stage2(1, [s])
+        for n in range(4):
+            stage2(n, [0])
         stage1(14)
         stage1(15)
         round_u_gpsimd(2, 0, G_COLS)
-        deal_mix(on_scalar, 2, 2)
-        deal_mix(on_scalar, 4, 1)
+        deal_mix(on_scalar, [1], [0, 1])
         round_u(on_scalar, 2, G_COLS, R)
-        deal_mix(on_scalar, 5, 1)
+        deal_mix(on_scalar, [2], [0, 1])
         for n in range(12, 16):
             add_pos(n)
         quant_u(2, 0, G_COLS)
@@ -471,29 +474,30 @@ def tile_low_rank_row_mixer_t2_kernel(
         round_u(on_scalar, LAST, 256, R)
         quant_u(LAST, 0, 256)
         quant_u(LAST, 256, R)
-        for n in range(2, EARLY):
+        deal_mix(on_vector, [LAST], [0, 1])
+        for n in range(4):
+            stage2(n, [1])
+        for n in range(4, EARLY):
             stage2(n, [0, 1])
         for n in range(EARLY):
             stage2(n, [2])
         for n in range(EARLY):
             stage2(n, [LAST])
 
-        deal_mix(on_vector, 6, 2)
-        deal_mix(on_vector, 8, 1)
-        deal_mix(on_gpsimd, 9, 1, "hold3")
-        deal_mix(on_gpsimd, 10, 2)
+        deal_mix(on_gpsimd, [0, 1], [2], "hold3")
+        deal_mix(on_gpsimd, [2, 3], [2])
         sigmoid_gate(0)
         sigmoid_gate(1)
         sigmoid_gate(2)
-        sigmoid_gate(3)
+        sigmoid_gate(3, 0, BANK)
         stage2(6, [0])
         add_u(0)
         add_u(1)
         turn_v(0, 2)
         copy_v(0, 2)
+        sigmoid_gate(3, BANK)
         sigmoid_gate(4)
         sigmoid_gate(5)
-        sigmoid_gate(6, 0, BANK)
         stage2(6, [1, 2, 3])
         stage2(7, every)
         add_u(2)
@@ -501,8 +505,8 @@ def tile_low_rank_row_mixer_t2_kernel(
         load_gate(12, 4, "u0")
         add_u(4)
         quant_v(0, 2)
-        deal_mix(on_gpsimd, 12, 2, "hold2")
-        deal_mix(on_gpsimd, 14, 2)
+        deal_mix(on_gpsimd, [0, 1], [3], "hold2")
+        deal_mix(on_gpsimd, [2, 3], [3])
         add_u(5)
         add_u(6)
         stage3(0)
@@ -524,73 +528,68 @@ def tile_low_rank_row_mixer_t2_kernel(
             turn_v(a + 2, count - 2)
             copy_v(a, 2)
             copy_v(a + 2, count - 2)
-            if a == 10:
-                move_right_half(a - 1)
+            move_right_half(a - 1)
             stage2(e, every)
             stage2(e + 1, [0, 1])
             gate_out(a - 1, 0)
-            if a == 10:
-                store_half(a - 1, 0)
+            store_half(a - 1, 0)
             quant_v(a, 2)
             quant_v(a + 2, count - 2)
             gate_out(a - 1, 1)
-
-        for a, e, h in ((2, 8, 13), (6, 10, 18)):
-            begin_round(a, 4, e)
             add_u(e)
             stage3(a)
-            halves(h, 2)
+
+        def second_half(a, e):
             move_right_half(a)
             gate_both(a)
+            store_half(a, 0)
+            store_half(a - 1, 1)
             stage2(e + 1, [2, 3])
             add_u(e + 1)
             stage3(a + 1)
-            halves(h + 2, 1 if a == 2 else 2)
-            move_right_half(a + 1)
+            if a < 10:
+                store_half(a, 1)
+
+        for a, e, h in ((2, 8, 12), (6, 10, 17)):
+            begin_round(a, 4, e)
+            halves(h, 2)
+            second_half(a, e)
             gate_both(a + 1)
             if a == 6:
                 stage2(e + 2, every)
                 add_u(e + 2)
             stage3(a + 2)
             stage3(a + 3)
-            halves(h + 3 if a == 2 else h + 4, 2)
+            halves(h + 2, 3 if a == 2 else 5)
             gate_both(a + 2)
 
         begin_round(10, 3, 13)
-        add_u(13)
-        stage3(10)
-        halves(24, 2)
-        move_right_half(10)
-        stage2(14, [2, 3])
-        gate_both(10)
-        store_half(10, 0)
-        store_half(9, 1)
-        add_u(14)
-        stage3(11)
+        halves(24, 1)
+        second_half(10, 13)
         stage3(12)
-        halves(26, 2)
-        gate_both(11)
-        store_half(11, 0)
-        store_half(10, 1)
-        store_half(11, 1)
+        halves(25, 2)
+        for half in range(2):
+            gate_out(11, half)
+            store_half(11, half)
+            if half == 0:
+                store_half(10, 1)
         turn_v(13, 2)
         copy_v(13, 2)
-        move_right_half(12)
-        halves(28, 2)
+        halves(27, 3)
         stage2(15, every)
         gate_out(12, 0)
         store_half(12, 0)
         quant_v(13, 2)
-        gate_out(12, 1)
         add_u(15)
+        gate_out(12, 1)
+        store_half(12, 1)
         stage3(13)
         turn_v(15, 1)
         copy_v(15, 1)
         halves(30, 2)
-        gate_both(13)
-        store_half(13, 0)
-        store_half(12, 1)
-        store_half(13, 1)
+        for half in range(2):
+            gate_out(13, half)
+            store_half(13, half)
         stage3(14)
         quant_v(15, 1)
         stage3(15)

@@ -26,9 +26,8 @@ BANK = 512
 ALIGN = 256
 EARLY = 6
 G_COLS = 256
-G_FIRST = 320
-HOLDS = {4: "hold0", 6: "hold1", 7: "hold0"}
-U_HOLDS = {(0, 0): "hold0", (1, 0): "hold1", (2, 0): "hold0", (3, 0): "hold1", (3, G_COLS): "hold3"}
+HOLDS = {4: "hold0", 6: "hold1"}
+U_HOLDS = {(0, 0): "hold0", (1, 0): "hold1", (2, 0): "hold1", (3, 0): "hold0", (3, G_COLS): "hold3"}
 V_HOLDS = {0: "hold2", 4: "hold4", 8: "hold0", 12: "hold1"}
 OWN_BUFFER = {1: 4, 5: 8, 9: 12}
 HALVED = (1, 2, 5, 6, 9, 10, 11, 12, 13, 14, 15)
@@ -65,11 +64,13 @@ def tile_low_rank_row_mixer_t2_kernel(
         gate_rows = gate.rearrange("(g p t) c -> g p t c", p=P, t=4)
         out_rows = out.rearrange("(g p t) c -> g t p c", p=P, t=4)
 
+        mix_sc = const.tile([P, LAST * T], U8, name="mix_sc", align_bytes=ALIGN)
+        nc.vector.memset(mix_sc[:, :D].bitcast(I32), 0)
         down_sc = scale_plane(2 * R, "down_sc")
         warm = const.tile([P, 1], F32, name="warm", align_bytes=ALIGN)
         nc.vector.memset(warm[:], 0.0)
         packed_sc = scale_plane(T, "packed_sc")
-        mix_sc = scale_plane(LAST * T, "mix_sc")
+        nc.vector.memset(mix_sc[:, D:].bitcast(I32), 0)
         up_sc = scale_plane(D, "up_sc")
         dealt_sc = const.tile([P, T], U8, name="dealt_sc", align_bytes=ALIGN)
         ident = const.tile([P, P], F32, name="ident", align_bytes=ALIGN)
@@ -111,17 +112,18 @@ def tile_low_rank_row_mixer_t2_kernel(
 
         def deal_mix(copy, passes, groups, tag=None):
             name = "mix%d_%d" % (passes[0], groups[0])
-            dealt = const.tile([P, T], U8, name="mix", tag=tag or name, align_bytes=ALIGN)
+            count = len(passes) * len(groups)
+            dealt = const.tile([P, 1024 * count], U8, name="mix", tag=tag or name, align_bytes=ALIGN)
             words = mix_all[:].bitcast(U16).rearrange("p (s g c i t) -> p s g c t i", s=GROUPS, g=GROUPS, t=4, i=8)
             if len(passes) == 1:
-                source = words[:, passes[0], groups[0] : groups[0] + 2]
+                source = words[:, passes[0], groups[0] : groups[-1] + 1]
             else:
                 source = words[:, passes[0] : passes[0] + 2, groups[0]]
             for j, (s, g) in enumerate((s, g) for s in passes for g in groups):
                 for t in range(4):
                     col = 2 * P * (4 * j + t)
                     mix_sb[4 * g + t, s] = dealt[:, col : col + 2 * P]
-            copy(out=dealt[:].bitcast(U16).rearrange("p (j t c i) -> p j c t i", j=2, t=4, i=8), in_=source)
+            copy(out=dealt[:].bitcast(U16).rearrange("p (j t c i) -> p j c t i", j=count, t=4, i=8), in_=source)
 
         def load_mix_scales():
             src = mix_scales.bitcast(I32)
@@ -212,9 +214,7 @@ def tile_low_rank_row_mixer_t2_kernel(
             )
 
         def rounded(g, first, last):
-            if g == 0 and first > 0:
-                return ug[0, 0][:, 4 * first : 4 * last]
-            width = 4 * (R if g == 0 else last - first)
+            width = 4 * (last - first)
             if (g, first) in U_HOLDS:
                 ug[g, first] = const.tile([P, width], BF16, name="ug", tag=U_HOLDS[g, first], align_bytes=ALIGN)
             else:
@@ -365,8 +365,8 @@ def tile_low_rank_row_mixer_t2_kernel(
         load_words(down_sb, down_words, 2)
         load_x(4, 2)
         load_pos(0, 2)
-        load_x(6, 2)
         load_mix_scales()
+        load_x(6, 2)
         load_pos(2, 2)
         load_x(8, 2)
         load_x(10, 2)
@@ -393,10 +393,26 @@ def tile_low_rank_row_mixer_t2_kernel(
             load_gate(4, 4)
             load_gate(8, 4)
 
+        def warm_tensor(count):
+            bank = psum_bank(7)
+            for i in range(count):
+                nc.tensor.matmul_mx(
+                    out=bank[:],
+                    lhsT=mix_sc[:, :BANK].bitcast(U32).bitcast(FP8X4),
+                    lhsT_scale=mix_sc[:, :P],
+                    rhs=mix_sc[:, : 2 * BANK].bitcast(FP4X4),
+                    rhs_scale=mix_sc[:, :BANK],
+                    start=True,
+                    stop=True,
+                )
+
+        warm_tensor(4)
         for n in range(4):
-            if n:
+            if n >= 2:
                 sort_x(on_vector, n)
             turn_x(n)
+            if n == 1:
+                warm_tensor(2)
             copy_x(n)
         quant_x(0, 1)
         quant_x(1, 1)
@@ -409,53 +425,56 @@ def tile_low_rank_row_mixer_t2_kernel(
             turn_x(n)
             copy_x(n)
         add_pos(0)
-        sort_x(on_vector, 6)
+        deal_mix_scales(0)
+        quant_x(4, 2)
         add_pos(1)
+        deal_mix_scales(1)
+        later_loads()
         stage1(2)
+        stage1(3)
         for n in (6, 7):
             turn_x(n)
             copy_x(n)
-        stage1(3)
-        deal_mix_scales(0)
-        quant_x(4, 2)
+        stage1(4)
         add_pos(2)
+        quant_x(6, 2)
         add_pos(3)
+        for n in (8, 9):
+            turn_x(n)
+            copy_x(n)
+        sort_x(on_vector, 10)
+        sort_x(on_vector, 11)
+        quant_x(8, 2)
+        for n in range(5, 8):
+            stage1(n)
+        round_u_gpsimd(0, 0, G_COLS)
+        round_u(on_scalar, 0, G_COLS, R)
+        sort_x(on_scalar, 13)
+        for n in range(4, 8):
+            add_pos(n)
 
-        for g in range(1, LAST):
-            fresh = range(4 * g + 2, 4 * g + 6)
-            for n in fresh[2 if g == 1 else 0 :]:
-                turn_x(n)
-                copy_x(n)
-            if g == 1:
-                quant_x(fresh[0], 2)
-            else:
-                quant_x(fresh[0], 1)
-                quant_x(fresh[1], 1)
-            if g == 1:
-                deal_mix_scales(1)
-                later_loads()
-            else:
-                quant_u(0, 0, R)
-            quant_x(fresh[2], 2)
-            for n in range(4 * g, 4 * g + 4):
-                stage1(n)
-            split = G_FIRST if g == 1 else G_COLS
-            round_u_gpsimd(g - 1, 0, split)
-            if g == 1:
-                sort_x(on_scalar, 4 * g + 6)
-                sort_x(on_scalar, 4 * g + 7)
-            else:
-                deal_mix(on_scalar, [0], [0, 1])
-            round_u(on_scalar, g - 1, split, R)
-            for n in range(4 * g, 4 * g + 4):
-                add_pos(n)
+        for n in range(10, 14):
+            turn_x(n)
+            copy_x(n)
+        quant_x(10, 1)
+        quant_x(11, 1)
+        quant_u(0, G_COLS, R)
+        quant_u(0, 0, G_COLS)
+        quant_x(12, 2)
+        for n in range(8, 12):
+            stage1(n)
+        round_u_gpsimd(1, 0, G_COLS)
+        deal_mix(on_scalar, [0], [0])
+        round_u(on_scalar, 1, G_COLS, R)
+        for n in range(8, 12):
+            add_pos(n)
 
         for n in (14, 15):
             turn_x(n)
             copy_x(n)
+        quant_x(14, 2)
         quant_u(1, G_COLS, R)
         quant_u(1, 0, G_COLS)
-        quant_x(14, 2)
         stage1(12)
         stage1(13)
         for n in range(4):
@@ -463,8 +482,9 @@ def tile_low_rank_row_mixer_t2_kernel(
         stage1(14)
         stage1(15)
         round_u_gpsimd(2, 0, G_COLS)
-        deal_mix(on_scalar, [1], [0, 1])
+        deal_mix(on_scalar, [1], [0])
         round_u(on_scalar, 2, G_COLS, R)
+        deal_mix(on_scalar, [0, 1], [1])
         deal_mix(on_scalar, [2], [0, 1])
         for n in range(12, 16):
             add_pos(n)
@@ -474,7 +494,8 @@ def tile_low_rank_row_mixer_t2_kernel(
         round_u(on_scalar, LAST, 256, R)
         quant_u(LAST, 0, 256)
         quant_u(LAST, 256, R)
-        deal_mix(on_vector, [LAST], [0, 1])
+        deal_mix(on_vector, [LAST], [0])
+        deal_mix(on_gpsimd, [LAST], [1], "hold3")
         for n in range(4):
             stage2(n, [1])
         for n in range(4, EARLY):
@@ -484,7 +505,7 @@ def tile_low_rank_row_mixer_t2_kernel(
         for n in range(EARLY):
             stage2(n, [LAST])
 
-        deal_mix(on_gpsimd, [0, 1], [2], "hold3")
+        deal_mix(on_gpsimd, [0, 1], [2])
         deal_mix(on_gpsimd, [2, 3], [2])
         sigmoid_gate(0)
         sigmoid_gate(1)

@@ -79,8 +79,8 @@ def tile_low_rank_row_mixer_t2_kernel(
         keep_sb = const.tile([P, GROUPS, 4], BF16, name="keep_sb", align_bytes=ALIGN)
         down_sb = const.tile([P, 2 * 2 * R], U8, name="down_sb", align_bytes=ALIGN)
         up_sb = const.tile([P, 2 * D], U8, name="up_sb", align_bytes=ALIGN)
-        mix_all = const.tile([P, GROUPS * 2 * T], U8, name="mix_all", align_bytes=ALIGN)
-        x_sb, pos_sb, gate_sb, mix_raw, mix_sb = {}, {}, {}, {}, {}
+        mix_raw = [const.tile([P, GROUPS * T], U8, name="mix_raw%d" % h, align_bytes=ALIGN) for h in range(2)]
+        x_sb, pos_sb, gate_sb, mix_sb = {}, {}, {}, {}
 
         def load_x(first, count):
             if count == 1:
@@ -106,30 +106,35 @@ def tile_low_rank_row_mixer_t2_kernel(
             for i in range(count):
                 gate_sb[first + i] = rows[:, i]
 
-        def load_mix(s):
-            mix_raw[s] = mix_all[:, 2 * T * s : 2 * T * (s + 1)]
-            nc.sync.dma_start(out=mix_raw[s].bitcast(I32), in_=mix_words.bitcast(I32)[s])
+        def load_mix(first, count, half):
+            cols = slice(T // 4 * half, T // 4 * (half + 1))
+            nc.sync.dma_start(
+                out=mix_raw[half][:, T * first : T * (first + count)].bitcast(I32).rearrange("p (s n) -> p s n", s=count),
+                in_=mix_words.bitcast(I32).rearrange("s p n -> p s n")[:, first : first + count, cols],
+            )
 
         def deal_mix(copy, passes, groups, tag=None):
             name = "mix%d_%d" % (passes[0], groups[0])
             count = len(passes) * len(groups)
             dealt = const.tile([P, 1024 * count], U8, name="mix", tag=tag or name, align_bytes=ALIGN)
-            words = mix_all[:].bitcast(U16).rearrange("p (s g c i t) -> p s g c t i", s=GROUPS, g=GROUPS, t=4, i=8)
+            half, first = divmod(groups[0], 2)
+            words = mix_raw[half][:].bitcast(U16).rearrange("p (s g c i t) -> p s g c t i", s=GROUPS, g=2, t=4, i=8)
             if len(passes) == 1:
-                source = words[:, passes[0], groups[0] : groups[-1] + 1]
+                source = words[:, passes[0], first : first + len(groups)]
             else:
-                source = words[:, passes[0] : passes[0] + 2, groups[0]]
+                source = words[:, passes[0] : passes[0] + 2, first]
             for j, (s, g) in enumerate((s, g) for s in passes for g in groups):
                 for t in range(4):
                     col = 2 * P * (4 * j + t)
                     mix_sb[4 * g + t, s] = dealt[:, col : col + 2 * P]
             copy(out=dealt[:].bitcast(U16).rearrange("p (j t c i) -> p j c t i", j=count, t=4, i=8), in_=source)
 
-        def load_mix_scales():
-            src = mix_scales.bitcast(I32)
+        def load_mix_scales(half):
+            cols = slice(T // 8 * half, T // 8 * (half + 1))
             for quad in (0, 2, 1, 3):
                 nc.sync.dma_start(
-                    out=packed_sc[:].bitcast(I32)[32 * quad : 32 * quad + 16], in_=src[:, 4 * quad : 4 * quad + 4]
+                    out=packed_sc[:].bitcast(I32)[32 * quad : 32 * quad + 16, cols],
+                    in_=mix_scales.bitcast(I32)[:, 4 * quad : 4 * quad + 4, cols],
                 )
 
         def deal_mix_scales(half):
@@ -139,11 +144,11 @@ def tile_low_rank_row_mixer_t2_kernel(
                 in_=packed_sc[:, cols].rearrange("p (g c i t) -> p g c t i", g=2, t=4, i=16),
             )
 
-        def spread_mix_scales(s):
+        def spread_mix_scales(s, half):
+            cols = slice(T // 8 * half, T // 8 * (half + 1))
             dst = mix_sc[:, T * (s - 1) : T * s].bitcast(I32)
             for r in range(4):
-                nc.sync.dma_start(out=dst[r:P:32], in_=dealt_sc[:].bitcast(I32)[4 * s + r : P : 32])
-
+                nc.sync.dma_start(out=dst[r:P:32, cols], in_=dealt_sc[:].bitcast(I32)[4 * s + r : P : 32, cols])
 
         sorted_x, xt_banks, xg, xc, xs, s1_banks, u, ug, uc, us = {}, {}, {}, {}, {}, {}, {}, {}, {}, {}
 
@@ -365,33 +370,36 @@ def tile_low_rank_row_mixer_t2_kernel(
         load_words(down_sb, down_words, 2)
         load_x(4, 2)
         load_pos(0, 2)
-        load_mix_scales()
         load_x(6, 2)
         load_pos(2, 2)
         load_x(8, 2)
+        load_mix_scales(0)
         load_x(10, 2)
-        load_pos(4, 4)
+        load_pos(4, 2)
         load_x(12, 2)
-        load_mix(0)
+        load_pos(6, 2)
+        load_mix(0, 1, 0)
         load_pos(8, 2)
         load_x(14, 2)
         load_pos(10, 2)
+        load_mix(1, 1, 0)
 
         def later_loads():
-            load_mix(1)
-            spread_mix_scales(1)
+            spread_mix_scales(1, 0)
             load_pos(12, 4)
-            load_mix(2)
-            spread_mix_scales(2)
+            load_mix(2, 1, 0)
+            spread_mix_scales(2, 0)
             nc.sync.dma_start(out=keep_sb[:], in_=keep.rearrange("(g p t) -> p g t", p=P, t=4))
+            load_mix(3, 1, 0)
+            spread_mix_scales(3, 0)
             load_gate(0, 2)
-            load_mix(3)
-            spread_mix_scales(3)
+            load_mix_scales(1)
+            load_mix(0, 2, 1)
             load_gate(2, 2)
+            load_mix(2, 2, 1)
             load_words(up_sb, up_words, 1)
             load_scales(up_sc, up_scales, 1)
-            load_gate(4, 4)
-            load_gate(8, 4)
+            load_gate(4, 2)
 
         def warm_tensor(count):
             bank = psum_bank(7)
@@ -425,11 +433,9 @@ def tile_low_rank_row_mixer_t2_kernel(
             turn_x(n)
             copy_x(n)
         add_pos(0)
-        deal_mix_scales(0)
-        quant_x(4, 2)
         add_pos(1)
-        deal_mix_scales(1)
-        later_loads()
+        sort_x(on_vector, 7)
+        quant_x(4, 2)
         stage1(2)
         stage1(3)
         for n in (6, 7):
@@ -437,19 +443,21 @@ def tile_low_rank_row_mixer_t2_kernel(
             copy_x(n)
         stage1(4)
         add_pos(2)
-        quant_x(6, 2)
+        sort_x(on_vector, 9)
         add_pos(3)
+        quant_x(6, 2)
         for n in (8, 9):
             turn_x(n)
             copy_x(n)
+        deal_mix_scales(0)
+        later_loads()
         sort_x(on_vector, 10)
-        sort_x(on_vector, 11)
         quant_x(8, 2)
         for n in range(5, 8):
             stage1(n)
         round_u_gpsimd(0, 0, G_COLS)
+        sort_x(on_scalar, 11)
         round_u(on_scalar, 0, G_COLS, R)
-        sort_x(on_scalar, 13)
         for n in range(4, 8):
             add_pos(n)
 
@@ -495,7 +503,12 @@ def tile_low_rank_row_mixer_t2_kernel(
         quant_u(LAST, 0, 256)
         quant_u(LAST, 256, R)
         deal_mix(on_vector, [LAST], [0])
-        deal_mix(on_gpsimd, [LAST], [1], "hold3")
+        deal_mix(on_vector, [LAST], [1])
+        deal_mix_scales(1)
+        for s in range(1, GROUPS):
+            spread_mix_scales(s, 1)
+        load_gate(6, 2)
+        load_gate(8, 4)
         for n in range(4):
             stage2(n, [1])
         for n in range(4, EARLY):
@@ -505,7 +518,7 @@ def tile_low_rank_row_mixer_t2_kernel(
         for n in range(EARLY):
             stage2(n, [LAST])
 
-        deal_mix(on_gpsimd, [0, 1], [2])
+        deal_mix(on_gpsimd, [0, 1], [2], "hold3")
         deal_mix(on_gpsimd, [2, 3], [2])
         sigmoid_gate(0)
         sigmoid_gate(1)

@@ -434,8 +434,9 @@ def tile_low_rank_row_mixer_t2_kernel(
             copy_x(n)
         add_pos(0)
         add_pos(1)
+        quant_x(4, 1)
         sort_x(on_vector, 7)
-        quant_x(4, 2)
+        quant_x(5, 1)
         stage1(2)
         stage1(3)
         for n in (6, 7):
@@ -461,7 +462,11 @@ def tile_low_rank_row_mixer_t2_kernel(
         for n in range(4, 8):
             add_pos(n)
 
-        for n in range(10, 14):
+        for n in (10, 11):
+            turn_x(n)
+            copy_x(n)
+        stage1(8)
+        for n in (12, 13):
             turn_x(n)
             copy_x(n)
         quant_x(10, 1)
@@ -469,7 +474,7 @@ def tile_low_rank_row_mixer_t2_kernel(
         quant_u(0, G_COLS, R)
         quant_u(0, 0, G_COLS)
         quant_x(12, 2)
-        for n in range(8, 12):
+        for n in range(9, 12):
             stage1(n)
         round_u_gpsimd(1, 0, G_COLS)
         deal_mix(on_scalar, [0], [0])
@@ -564,7 +569,7 @@ def tile_low_rank_row_mixer_t2_kernel(
             copy_v(a + 2, count - 2)
             move_right_half(a - 1)
             stage2(e, every)
-            stage2(e + 1, [0, 1])
+            stage2(e + 1, [0, 1, 2] if a == 6 else [0, 1])
             gate_out(a - 1, 0)
             store_half(a - 1, 0)
             quant_v(a, 2)
@@ -578,7 +583,7 @@ def tile_low_rank_row_mixer_t2_kernel(
             gate_both(a)
             store_half(a, 0)
             store_half(a - 1, 1)
-            stage2(e + 1, [2, 3])
+            stage2(e + 1, [LAST] if a == 6 else [2, 3])
             add_u(e + 1)
             stage3(a + 1)
             if a < 10:

@@ -30,7 +30,7 @@ HOLDS = {4: "hold0", 6: "hold1"}
 U_HOLDS = {(0, 0): "hold0", (1, 0): "hold1", (2, 0): "hold1", (3, 0): "hold0", (3, G_COLS): "hold3"}
 V_HOLDS = {0: "hold2", 4: "hold4", 8: "hold0", 12: "hold1"}
 OWN_BUFFER = {1: 4, 5: 8, 9: 12}
-HALVED = (1, 2, 5, 6, 9, 10, 11, 12, 13, 14, 15)
+HALVED = (1, 5, 9, 10, 11, 12, 13, 14, 15)
 
 
 def tile_low_rank_row_mixer_t2_kernel(
@@ -388,17 +388,17 @@ def tile_low_rank_row_mixer_t2_kernel(
             spread_mix_scales(1, 0)
             load_pos(12, 4)
             load_mix(2, 1, 0)
-            spread_mix_scales(2, 0)
             nc.sync.dma_start(out=keep_sb[:], in_=keep.rearrange("(g p t) -> p g t", p=P, t=4))
+            spread_mix_scales(2, 0)
             load_mix(3, 1, 0)
+            load_mix(0, 2, 1)
             spread_mix_scales(3, 0)
             load_gate(0, 2)
             load_mix_scales(1)
-            load_mix(0, 2, 1)
             load_gate(2, 2)
             load_mix(2, 2, 1)
-            load_words(up_sb, up_words, 1)
             load_scales(up_sc, up_scales, 1)
+            load_words(up_sb, up_words, 1)
             load_gate(4, 2)
 
         def warm_tensor(count):
@@ -510,10 +510,12 @@ def tile_low_rank_row_mixer_t2_kernel(
         deal_mix(on_vector, [LAST], [0])
         deal_mix(on_vector, [LAST], [1])
         deal_mix_scales(1)
-        for s in range(1, GROUPS):
-            spread_mix_scales(s, 1)
+        spread_mix_scales(1, 1)
         load_gate(6, 2)
-        load_gate(8, 4)
+        spread_mix_scales(2, 1)
+        load_gate(8, 2)
+        spread_mix_scales(3, 1)
+        load_gate(10, 2)
         for n in range(4):
             stage2(n, [1])
         for n in range(4, EARLY):
@@ -580,14 +582,16 @@ def tile_low_rank_row_mixer_t2_kernel(
 
         def second_half(a, e):
             move_right_half(a)
+            if a < 10:
+                store_half(a - 1, 1)
             gate_both(a)
-            store_half(a, 0)
-            store_half(a - 1, 1)
+            if a == 10:
+                store_half(a, 0)
             stage2(e + 1, [LAST] if a == 6 else [2, 3])
             add_u(e + 1)
             stage3(a + 1)
-            if a < 10:
-                store_half(a, 1)
+            if a == 10:
+                store_half(a - 1, 1)
 
         for a, e, h in ((2, 8, 12), (6, 10, 17)):
             begin_round(a, 4, e)

@@ -371,8 +371,8 @@ def tile_low_rank_row_mixer_t2_kernel(
         load_x(4, 2)
         load_pos(0, 2)
         load_x(6, 2)
-        load_pos(2, 2)
         load_x(8, 2)
+        load_pos(2, 2)
         load_mix_scales(0)
         load_x(10, 2)
         load_pos(4, 2)
@@ -442,19 +442,19 @@ def tile_low_rank_row_mixer_t2_kernel(
         for n in (6, 7):
             turn_x(n)
             copy_x(n)
-        stage1(4)
-        add_pos(2)
+        sort_x(on_vector, 8)
         sort_x(on_vector, 9)
+        add_pos(2)
+        quant_x(6, 1)
         add_pos(3)
-        quant_x(6, 2)
+        quant_x(7, 1)
         for n in (8, 9):
             turn_x(n)
             copy_x(n)
         deal_mix_scales(0)
         later_loads()
-        sort_x(on_vector, 10)
         quant_x(8, 2)
-        for n in range(5, 8):
+        for n in range(4, 8):
             stage1(n)
         round_u_gpsimd(0, 0, G_COLS)
         sort_x(on_scalar, 11)
@@ -462,11 +462,7 @@ def tile_low_rank_row_mixer_t2_kernel(
         for n in range(4, 8):
             add_pos(n)
 
-        for n in (10, 11):
-            turn_x(n)
-            copy_x(n)
-        stage1(8)
-        for n in (12, 13):
+        for n in range(10, 14):
             turn_x(n)
             copy_x(n)
         quant_x(10, 1)
@@ -474,7 +470,7 @@ def tile_low_rank_row_mixer_t2_kernel(
         quant_u(0, G_COLS, R)
         quant_u(0, 0, G_COLS)
         quant_x(12, 2)
-        for n in range(9, 12):
+        for n in range(8, 12):
             stage1(n)
         round_u_gpsimd(1, 0, G_COLS)
         deal_mix(on_scalar, [0], [0])

@@ -462,7 +462,11 @@ def tile_low_rank_row_mixer_t2_kernel(
         for n in range(4, 8):
             add_pos(n)
 
-        for n in range(10, 14):
+        for n in (10, 11):
+            turn_x(n)
+            copy_x(n)
+        stage1(8)
+        for n in (12, 13):
             turn_x(n)
             copy_x(n)
         quant_x(10, 1)
@@ -470,7 +474,7 @@ def tile_low_rank_row_mixer_t2_kernel(
         quant_u(0, G_COLS, R)
         quant_u(0, 0, G_COLS)
         quant_x(12, 2)
-        for n in range(8, 12):
+        for n in range(9, 12):
             stage1(n)
         round_u_gpsimd(1, 0, G_COLS)
         deal_mix(on_scalar, [0], [0])

@@ -64,13 +64,11 @@ def tile_low_rank_row_mixer_t2_kernel(
         gate_rows = gate.rearrange("(g p t) c -> g p t c", p=P, t=4)
         out_rows = out.rearrange("(g p t) c -> g t p c", p=P, t=4)
 
-        mix_sc = const.tile([P, LAST * T], U8, name="mix_sc", align_bytes=ALIGN)
-        nc.vector.memset(mix_sc[:, :D].bitcast(I32), 0)
         down_sc = scale_plane(2 * R, "down_sc")
         warm = const.tile([P, 1], F32, name="warm", align_bytes=ALIGN)
         nc.vector.memset(warm[:], 0.0)
         packed_sc = scale_plane(T, "packed_sc")
-        nc.vector.memset(mix_sc[:, D:].bitcast(I32), 0)
+        mix_sc = scale_plane(LAST * T, "mix_sc")
         up_sc = scale_plane(D, "up_sc")
         dealt_sc = const.tile([P, T], U8, name="dealt_sc", align_bytes=ALIGN)
         ident = const.tile([P, P], F32, name="ident", align_bytes=ALIGN)
@@ -401,26 +399,10 @@ def tile_low_rank_row_mixer_t2_kernel(
             load_words(up_sb, up_words, 1)
             load_gate(4, 2)
 
-        def warm_tensor(count):
-            bank = psum_bank(7)
-            for i in range(count):
-                nc.tensor.matmul_mx(
-                    out=bank[:],
-                    lhsT=mix_sc[:, :BANK].bitcast(U32).bitcast(FP8X4),
-                    lhsT_scale=mix_sc[:, :P],
-                    rhs=mix_sc[:, : 2 * BANK].bitcast(FP4X4),
-                    rhs_scale=mix_sc[:, :BANK],
-                    start=True,
-                    stop=True,
-                )
-
-        warm_tensor(4)
         for n in range(4):
-            if n >= 2:
+            if n >= 1:
                 sort_x(on_vector, n)
             turn_x(n)
-            if n == 1:
-                warm_tensor(2)
             copy_x(n)
         quant_x(0, 1)
         quant_x(1, 1)
@@ -442,6 +424,7 @@ def tile_low_rank_row_mixer_t2_kernel(
         for n in (6, 7):
             turn_x(n)
             copy_x(n)
+        stage1(4)
         sort_x(on_vector, 8)
         sort_x(on_vector, 9)
         add_pos(2)
@@ -454,7 +437,7 @@ def tile_low_rank_row_mixer_t2_kernel(
         deal_mix_scales(0)
         later_loads()
         quant_x(8, 2)
-        for n in range(4, 8):
+        for n in range(5, 8):
             stage1(n)
         round_u_gpsimd(0, 0, G_COLS)
         sort_x(on_scalar, 11)

@@ -64,7 +64,12 @@ def tile_low_rank_row_mixer_t2_kernel(
         gate_rows = gate.rearrange("(g p t) c -> g p t c", p=P, t=4)
         out_rows = out.rearrange("(g p t) c -> g t p c", p=P, t=4)
 
+        zeros = const.tile([P, D], BF16, name="zeros", tag="hold2", align_bytes=ALIGN)
+        zero_codes = const.tile([P, D // 4], U32, name="zero_codes", tag="hold3", align_bytes=ALIGN)
+        nc.vector.memset(zeros[:].bitcast(I32), 0)
+        zero_scales = scale_plane(BANK, "zero_scales")
         down_sc = scale_plane(2 * R, "down_sc")
+        nc.vector.quantize_mx(out=zero_codes[:].bitcast(FP8X4), scales=zero_scales[:, : D // 4], in_=zeros[:])
         warm = const.tile([P, 1], F32, name="warm", align_bytes=ALIGN)
         nc.vector.memset(warm[:], 0.0)
         packed_sc = scale_plane(T, "packed_sc")
@@ -399,10 +404,26 @@ def tile_low_rank_row_mixer_t2_kernel(
             load_words(up_sb, up_words, 1)
             load_gate(4, 2)
 
+        def warm_tensor(count):
+            bank = psum_bank(7)
+            for i in range(count):
+                nc.tensor.matmul_mx(
+                    out=bank[:],
+                    lhsT=zero_codes[:, :P].bitcast(FP8X4),
+                    lhsT_scale=zero_scales[:, :P],
+                    rhs=zero_codes[:].bitcast(U8).bitcast(FP4X4),
+                    rhs_scale=zero_scales[:],
+                    start=True,
+                    stop=True,
+                )
+
+        warm_tensor(3)
         for n in range(4):
             if n >= 1:
                 sort_x(on_vector, n)
             turn_x(n)
+            if n == 1:
+                warm_tensor(2)
             copy_x(n)
         quant_x(0, 1)
         quant_x(1, 1)

@@ -20,17 +20,18 @@ SIGMOID = mybir.ActivationFunctionType.Sigmoid
 
 P = 128
 GROUPS = T // 512
-TILES = T // P
 LAST = GROUPS - 1
 BANK = 512
 ALIGN = 256
-EARLY = 6
-G_COLS = 256
-HOLDS = {4: "hold0", 6: "hold1"}
-U_HOLDS = {(0, 0): "hold0", (1, 0): "hold1", (2, 0): "hold1", (3, 0): "hold0", (3, G_COLS): "hold3"}
-V_HOLDS = {0: "hold2", 4: "hold4", 8: "hold0", 12: "hold1"}
-OWN_BUFFER = {1: 4, 5: 8, 9: 12}
-HALVED = (1, 5, 9, 10, 11, 12, 13, 14, 15)
+HALF = T // 2
+SINGLES, ROWS, WIDE, SORTED, CODES, VB, STAGES = 4, 6, 8, 4, 4, 8, 4
+XG = [0, 1, 2, 3, 0, 1, 2, 3]
+UG = [1, 3, 3, 0]
+G_COLS = 288
+SHIFT = 4 * (R - G_COLS)
+ORDER = list(range(16))
+ALL = [0, 1, 2, 3]
+V_COLS = 352
 
 
 def tile_low_rank_row_mixer_t2_kernel(
@@ -38,20 +39,54 @@ def tile_low_rank_row_mixer_t2_kernel(
 ):
     nc = tc.nc
     with ExitStack() as ctx:
-        const = ctx.enter_context(tc.tile_pool(name="const", bufs=1))
-        work = ctx.enter_context(tc.tile_pool(name="work", bufs=2))
+        sbuf = ctx.enter_context(tc.tile_pool(name="sbuf", bufs=1))
         psum = ctx.enter_context(tc.psum_pool(name="psum", bufs=1))
         ctx.enter_context(tc.manual_schedule())
         on_vector, on_scalar, on_gpsimd = nc.vector.tensor_copy, nc.scalar.copy, nc.gpsimd.tensor_copy
 
-        def psum_bank(index):
-            bank = psum.tile([P, BANK], F32, name="bank%d" % index, tag="bank%d" % index)
+        def buffer(width, dtype, tag, bufs=1):
+            tile = sbuf.tile([P, width], dtype, name=tag, tag=tag, bufs=bufs, align_bytes=ALIGN)
+            return tile
+
+        free_banks, held = list(range(8)), {}
+
+        def next_bank(key):
+            held[key] = free_banks.pop(0)
+            name = "bank%d" % held[key]
+            bank = psum.tile([P, BANK], F32, name=name, tag=name)
             return bank
 
-        def scale_plane(width, name):
-            plane = const.tile([P, width], U8, name=name, align_bytes=ALIGN)
-            nc.vector.memset(plane[:].bitcast(I32), 0)
-            return plane
+        def release(key):
+            free_banks.append(held.pop(key))
+
+        def zero(tile, first, last, engine=nc.vector):
+            engine.memset(tile[:, first:last].bitcast(I32), 0)
+
+        x_rows = x.rearrange("(g p t) k -> g p t k", p=P, t=4)
+        pos_rows = pos.rearrange("(g p t) r -> g p t r", p=P, t=4)
+        gate_rows = gate.rearrange("(g p t) c -> g p t c", p=P, t=4)
+        out_rows = out.rearrange("(g p t) c -> g p t c", p=P, t=4)
+
+        x_sb, pos_sb, gate_sb, mix_sb, mix_raw = {}, {}, {}, {}, {}
+
+        def load_rows(rows, width, into, first, count, tag, bufs=1):
+            tile = buffer(count * width, BF16, tag, bufs)
+            g, t = divmod(first, 4)
+            nc.sync.dma_start(out=tile[:].rearrange("p (t k) -> p t k", t=count), in_=rows[g][:, t : t + count])
+            for i in range(count):
+                into[first + i] = tile[:, width * i : width * (i + 1)]
+
+        def load_x(first, count):
+            if count == 1:
+                load_rows(x_rows, D, x_sb, first, count, "single", SINGLES)
+            else:
+                load_rows(x_rows, D, x_sb, first, count, "rows", ROWS)
+
+        def load_pos(first, count):
+            load_rows(pos_rows, R, pos_sb, first, count, "wide", WIDE)
+
+        def load_gate(first, count, tag=None):
+            load_rows(gate_rows, D, gate_sb, first, count, tag or "gate%d" % first)
 
         def load_scales(plane, scales, passes):
             src = scales.bitcast(I32).rearrange("s q n -> q s n")
@@ -59,112 +94,67 @@ def tile_low_rank_row_mixer_t2_kernel(
             for r in range(4):
                 nc.sync.dma_start(out=dst[r:P:32], in_=src[r:16:4])
 
-        x_rows = x.rearrange("(g p t) k -> g p t k", p=P, t=4)
-        pos_rows = pos.rearrange("(g p t) r -> g p t r", p=P, t=4)
-        gate_rows = gate.rearrange("(g p t) c -> g p t c", p=P, t=4)
-        out_rows = out.rearrange("(g p t) c -> g t p c", p=P, t=4)
-
-        zeros = const.tile([P, D], BF16, name="zeros", tag="hold2", align_bytes=ALIGN)
-        zero_codes = const.tile([P, D // 4], U32, name="zero_codes", tag="hold3", align_bytes=ALIGN)
-        nc.vector.memset(zeros[:].bitcast(I32), 0)
-        zero_scales = scale_plane(BANK, "zero_scales")
-        down_sc = scale_plane(2 * R, "down_sc")
-        nc.vector.quantize_mx(out=zero_codes[:].bitcast(FP8X4), scales=zero_scales[:, : D // 4], in_=zeros[:])
-        warm = const.tile([P, 1], F32, name="warm", align_bytes=ALIGN)
-        nc.vector.memset(warm[:], 0.0)
-        packed_sc = scale_plane(T, "packed_sc")
-        mix_sc = scale_plane(LAST * T, "mix_sc")
-        up_sc = scale_plane(D, "up_sc")
-        dealt_sc = const.tile([P, T], U8, name="dealt_sc", align_bytes=ALIGN)
-        ident = const.tile([P, P], F32, name="ident", align_bytes=ALIGN)
-        make_identity(nc, ident[:])
-
-        keep_sb = const.tile([P, GROUPS, 4], BF16, name="keep_sb", align_bytes=ALIGN)
-        down_sb = const.tile([P, 2 * 2 * R], U8, name="down_sb", align_bytes=ALIGN)
-        up_sb = const.tile([P, 2 * D], U8, name="up_sb", align_bytes=ALIGN)
-        mix_raw = [const.tile([P, GROUPS * T], U8, name="mix_raw%d" % h, align_bytes=ALIGN) for h in range(2)]
-        x_sb, pos_sb, gate_sb, mix_sb = {}, {}, {}, {}
-
-        def load_x(first, count):
-            if count == 1:
-                rows = work.tile([P, D], BF16, name="x", tag="single", bufs=4, align_bytes=ALIGN)
-            else:
-                rows = work.tile([P, count * D], BF16, name="x", tag="rows", bufs=6, align_bytes=ALIGN)
-            g, t = divmod(first, 4)
-            nc.sync.dma_start(out=rows[:].rearrange("p (t k) -> p t k", t=count), in_=x_rows[g][:, t : t + count])
-            for i in range(count):
-                x_sb[first + i] = rows[:, D * i : D * (i + 1)]
-
-        def load_pos(first, count):
-            rows = work.tile([P, count, R], BF16, name="pos", tag="wide", bufs=8, align_bytes=ALIGN)
-            g, t = divmod(first, 4)
-            nc.sync.dma_start(out=rows[:], in_=pos_rows[g][:, t : t + count])
-            for i in range(count):
-                pos_sb[first + i] = rows[:, i]
-
-        def load_gate(first, count, tag=None):
-            rows = const.tile([P, count, D], BF16, name="gate", tag=tag or "gate%d" % first, align_bytes=ALIGN)
-            g, t = divmod(first, 4)
-            nc.sync.dma_start(out=rows[:], in_=gate_rows[g][:, t : t + count])
-            for i in range(count):
-                gate_sb[first + i] = rows[:, i]
+        def load_words(tile, words, passes):
+            nc.sync.dma_start(
+                out=tile[:].bitcast(I32).rearrange("p (s n) -> p s n", s=passes),
+                in_=words.bitcast(I32).rearrange("s p n -> p s n"),
+            )
 
         def load_mix(first, count, half):
+            if half not in mix_raw:
+                mix_raw[half] = buffer(GROUPS * T, U8, "mix_raw%d" % half)
             cols = slice(T // 4 * half, T // 4 * (half + 1))
             nc.sync.dma_start(
                 out=mix_raw[half][:, T * first : T * (first + count)].bitcast(I32).rearrange("p (s n) -> p s n", s=count),
                 in_=mix_words.bitcast(I32).rearrange("s p n -> p s n")[:, first : first + count, cols],
             )
 
-        def deal_mix(copy, passes, groups, tag=None):
-            name = "mix%d_%d" % (passes[0], groups[0])
-            count = len(passes) * len(groups)
-            dealt = const.tile([P, 1024 * count], U8, name="mix", tag=tag or name, align_bytes=ALIGN)
+        def deal_mix(copy, passes, groups, slots, tag=None):
+            count, width = len(passes) * len(groups), len(slots)
+            dealt = buffer(2 * P * width * count, U8, tag or "mix%d_%d_%d" % (passes[0], groups[0], slots[0]))
             half, first = divmod(groups[0], 2)
-            words = mix_raw[half][:].bitcast(U16).rearrange("p (s g c i t) -> p s g c t i", s=GROUPS, g=2, t=4, i=8)
-            if len(passes) == 1:
-                source = words[:, passes[0], first : first + len(groups)]
-            else:
-                source = words[:, passes[0] : passes[0] + 2, first]
+            words = mix_raw[half][:].bitcast(U16).rearrange("p (j c i t) -> p j c t i", j=2 * GROUPS, t=4, i=8)
+            start, step = 2 * passes[0] + first, 3 - len(groups)
+            source = words[:, start : start + step * (count - 1) + 1 : step, :, slots[0] : slots[0] + width]
             for j, (s, g) in enumerate((s, g) for s in passes for g in groups):
-                for t in range(4):
-                    col = 2 * P * (4 * j + t)
+                for i, t in enumerate(slots):
+                    col = 2 * P * (width * j + i)
                     mix_sb[4 * g + t, s] = dealt[:, col : col + 2 * P]
-            copy(out=dealt[:].bitcast(U16).rearrange("p (j t c i) -> p j c t i", j=count, t=4, i=8), in_=source)
+            copy(out=dealt[:].bitcast(U16).rearrange("p (j t c i) -> p j c t i", j=count, t=width, i=8), in_=source)
 
-        def load_mix_scales(half):
-            cols = slice(T // 8 * half, T // 8 * (half + 1))
-            for quad in (0, 2, 1, 3):
-                nc.sync.dma_start(
-                    out=packed_sc[:].bitcast(I32)[32 * quad : 32 * quad + 16, cols],
-                    in_=mix_scales.bitcast(I32)[:, 4 * quad : 4 * quad + 4, cols],
-                )
+        def load_mix_scales():
+            nc.sync.dma_start(
+                out=packed_sc[:].bitcast(I32), in_=mix_scales.bitcast(I32).rearrange("s q (h n) -> (s q h) n", h=2)
+            )
 
-        def deal_mix_scales(half):
-            cols = slice(1024 * half, 1024 * (half + 1))
+        def deal_mix_scales():
             on_vector(
-                out=dealt_sc[:, cols].rearrange("p (g t c i) -> p g c t i", g=2, t=4, i=16),
-                in_=packed_sc[:, cols].rearrange("p (g c i t) -> p g c t i", g=2, t=4, i=16),
+                out=dealt_sc[:].rearrange("p (g t c i) -> p g c t i", g=2, t=4, i=16),
+                in_=packed_sc[:].rearrange("p (g c i t) -> p g c t i", g=2, t=4, i=16),
             )
 
         def spread_mix_scales(s, half):
-            cols = slice(T // 8 * half, T // 8 * (half + 1))
-            dst = mix_sc[:, T * (s - 1) : T * s].bitcast(I32)
+            col = T * s + HALF * half
+            dst = mix_sc[:, col : col + HALF].bitcast(I32)
             for r in range(4):
-                nc.sync.dma_start(out=dst[r:P:32, cols], in_=dealt_sc[:].bitcast(I32)[4 * s + r : P : 32, cols])
+                first = 32 * s + 2 * r + half
+                nc.sync.dma_start(out=dst[r:P:32], in_=dealt_sc[:].bitcast(I32)[first : first + 25 : 8])
+
+        def sort_pairs(copy, dst, src):
+            copy(
+                out=dst.rearrange("p (k h c i) -> p k c h i", k=2, h=2, i=4),
+                in_=src.rearrange("p (k c i h) -> p k c h i", k=2, h=2, i=4),
+            )
 
         sorted_x, xt_banks, xg, xc, xs, s1_banks, u, ug, uc, us = {}, {}, {}, {}, {}, {}, {}, {}, {}, {}
 
         def sort_x(copy, n):
-            sorted_x[n] = work.tile([P, 512], F32, name="sorted_x", bufs=4, align_bytes=ALIGN)
-            copy(
-                out=sorted_x[n][:].rearrange("p (k h c i) -> p k c h i", k=2, h=2, i=4),
-                in_=x_sb[n].bitcast(F32).rearrange("p (k c i h) -> p k c h i", k=2, h=2, i=4),
-            )
+            sorted_x[n] = buffer(512, F32, "sorted", SORTED)
+            sort_pairs(copy, sorted_x[n][:], x_sb[n].bitcast(F32))
 
         def turn_x(n):
             words = x_sb[n].bitcast(F32)
-            xt_banks[n] = psum_bank(n % 4)
+            xt_banks[n] = next_bank(("xt", n))
             for k in range(2):
                 for h in range(2):
                     col = P * (2 * k + h)
@@ -174,22 +164,21 @@ def tile_low_rank_row_mixer_t2_kernel(
                         src = words[:, 256 * k + h : 256 * (k + 1) : 2]
                     nc.tensor.transpose(xt_banks[n][:, col : col + P], src, ident[:])
 
-        def copy_x(n):
+        def copy_x(n, copy=on_scalar):
             q, i = divmod(n, 2)
-            if i == 0 and q in HOLDS:
-                xg[q] = const.tile([P, 2 * D], BF16, name="xg", tag=HOLDS[q], align_bytes=ALIGN)
-            elif i == 0:
-                xg[q] = work.tile([P, 2 * D], BF16, name="xg", bufs=2, align_bytes=ALIGN)
-            on_scalar(
+            if i == 0:
+                xg[q] = stage[XG[q]][:, : 2 * D]
+            copy(
                 out=xg[q][:, D * i : D * (i + 1)].bitcast(F32).rearrange("p (k r h) -> p k r h", k=2, h=2),
                 in_=xt_banks[n][:].rearrange("p (k h r) -> p k r h", k=2, h=2),
             )
+            release(("xt", n))
 
         def quant_x(first, count):
             q, i = divmod(first, 2)
             if i == 0:
-                xc[q] = work.tile([P, 4 * P], U32, name="xc", bufs=3, align_bytes=ALIGN)
-                xs[q] = work.tile([P, 4 * P], U8, name="xs", bufs=3, align_bytes=ALIGN)
+                xc[q] = buffer(4 * P, U32, "codes", CODES)
+                xs[q] = buffer(4 * P, U8, "scales", CODES)
             cols = slice(2 * P * i, 2 * P * (i + count))
             nc.vector.quantize_mx(
                 out=xc[q][:, cols].bitcast(FP8X4), scales=xs[q][:, cols], in_=xg[q][:, D * i : D * (i + count)]
@@ -197,7 +186,7 @@ def tile_low_rank_row_mixer_t2_kernel(
 
         def stage1(n):
             q, i = divmod(n, 2)
-            s1_banks[n] = psum_bank(4 + n % 4)
+            s1_banks[n] = next_bank(("s1", n))
             for k in range(2):
                 cols = slice(P * (2 * i + k), P * (2 * i + k + 1))
                 nc.tensor.matmul_mx(
@@ -213,21 +202,19 @@ def tile_low_rank_row_mixer_t2_kernel(
         def add_pos(n):
             g, t = divmod(n, 4)
             if t == 0:
-                u[g] = const.tile([P, 4, R], F32, name="u", tag="u%d" % g, align_bytes=ALIGN)
+                u[g] = sbuf.tile([P, 4, R], F32, name="u", tag="u%d" % g, align_bytes=ALIGN)
             nc.vector.tensor_tensor(
-                out=u[g][:, t].rearrange("p (h m e) -> p m h e", h=2, e=2),
-                in0=s1_banks[n][:].rearrange("p (m h e) -> p m h e", h=2, e=2),
-                in1=pos_sb[n].rearrange("p (m h e) -> p m h e", h=2, e=2),
+                out=u[g][:, t].rearrange("p (h m e) -> p h m e", h=2, e=2),
+                in0=s1_banks[n][:].rearrange("p (h m e) -> p h m e", h=2, e=2),
+                in1=pos_sb[n].rearrange("p (m h e) -> p h m e", h=2, e=2),
                 op=ADD,
             )
+            release(("s1", n))
 
         def rounded(g, first, last):
-            width = 4 * (last - first)
-            if (g, first) in U_HOLDS:
-                ug[g, first] = const.tile([P, width], BF16, name="ug", tag=U_HOLDS[g, first], align_bytes=ALIGN)
-            else:
-                ug[g, first] = work.tile([P, width], BF16, name="ug", tag="single", bufs=4, align_bytes=ALIGN)
-            return ug[g, first][:, : 4 * (last - first)]
+            if g not in ug:
+                ug[g] = stage[UG[g]][:, SHIFT : SHIFT + 4 * R]
+            return ug[g][:, 4 * first : 4 * last]
 
         def round_u(copy, g, first, last):
             copy(
@@ -245,29 +232,24 @@ def tile_low_rank_row_mixer_t2_kernel(
                 op1=ADD,
             )
 
-        def quant_u(g, first, last):
+        def quant_u(g, first=0, last=R):
             if g not in uc:
-                uc[g] = const.tile([P, R], U32, name="uc%d" % g, align_bytes=ALIGN)
-                us[g] = const.tile([P, R], U8, name="us%d" % g, align_bytes=ALIGN)
+                uc[g] = buffer(R, U32, "uc%d" % g)
+                us[g] = buffer(R, U8, "us%d" % g)
             nc.vector.quantize_mx(
-                out=uc[g][:, first:last].bitcast(FP8X4), scales=us[g][:, first:last], in_=ug[g, first][:]
+                out=uc[g][:, first:last].bitcast(FP8X4), scales=us[g][:, first:last], in_=ug[g][:, 4 * first : 4 * last]
             )
 
-        ring, s2_banks, vb, vt, vg, vc, vs, s3_banks, sig, moved, o_tiles = [], {}, {}, {}, {}, {}, {}, {}, {}, {}, {}
+        s2_banks, vb, vt, vg, vc, vs, s3_banks, sig, moved, o_tiles = {}, {}, {}, {}, {}, {}, {}, {}, {}, {}
 
-        def ring_bank():
-            ring.append(psum_bank(len(ring) % 8))
-            return ring[-1]
-
-        def stage2(n, passes):
+        def stage2(n, passes=(0, 1, 2, 3)):
             if passes[0] == 0:
-                s2_banks[n] = ring_bank()
+                s2_banks[n] = next_bank(("s2", n))
             for s in passes:
-                plane = dealt_sc[:] if s == 0 else mix_sc[:, T * (s - 1) : T * s]
                 nc.tensor.matmul_mx(
                     out=s2_banks[n][:],
-                    lhsT=mix_sb[n, s].bitcast(FP4X4),
-                    lhsT_scale=plane[:, P * n : P * (n + 1)],
+                    lhsT=mix_sb[ORDER[n], s].bitcast(FP4X4),
+                    lhsT_scale=mix_sc[:, T * s + P * ORDER[n] : T * s + P * (ORDER[n] + 1)],
                     rhs=uc[s][:].bitcast(FP8X4),
                     rhs_scale=us[s][:],
                     start=(s == 0),
@@ -275,41 +257,43 @@ def tile_low_rank_row_mixer_t2_kernel(
                 )
 
         def add_u(n):
-            g, t = divmod(n, 4)
-            vb[n] = work.tile([P, R], BF16, name="vb", bufs=6, align_bytes=ALIGN)
+            g, t = divmod(ORDER[n], 4)
+            vb[n] = buffer(R, BF16, "vb", VB)
             nc.vector.scalar_tensor_tensor(
                 out=vb[n][:], in0=u[g][:, t], scalar=keep_sb[:, g, t : t + 1], in1=s2_banks[n][:], op0=MULT, op1=ADD
             )
+            release(("s2", n))
 
         def turn_v(first, count):
-            vt[first] = ring_bank()
+            vt[first] = next_bank(("vt", first))
             for i in range(count):
                 words = vb[first + i][:].bitcast(F32)
                 for h in range(2):
                     col = P * (2 * i + h)
                     nc.tensor.transpose(vt[first][:, col : col + P], words[:, P * h : P * (h + 1)], ident[:])
 
-        def copy_v(first, count):
-            if first in V_HOLDS:
-                vg[first] = const.tile([P, count * R], BF16, name="vg", tag=V_HOLDS[first], align_bytes=ALIGN)
+        def copy_v(first, count, tag=None):
+            if tag:
+                vg[first] = buffer(count * R, BF16, tag)
             else:
-                vg[first] = work.tile([P, count * R], BF16, name="vg", tag="single", bufs=4, align_bytes=ALIGN)
+                vg[first] = buffer(count * R, BF16, "single", SINGLES)
             on_scalar(
                 out=vg[first][:].bitcast(F32).rearrange("m (i p h) -> m i p h", i=count, h=2),
                 in_=vt[first][:, : 2 * P * count].rearrange("m (i h p) -> m i p h", i=count, h=2),
             )
+            release(("vt", first))
 
         def quant_v(first, count):
-            codes = work.tile([P, count * P], U32, name="vc", bufs=3, align_bytes=ALIGN)
-            scales = work.tile([P, count * P], U8, name="vs", bufs=3, align_bytes=ALIGN)
+            codes = buffer(count * P, U32, "codes", CODES)
+            scales = buffer(count * P, U8, "scales", CODES)
             nc.vector.quantize_mx(out=codes[:].bitcast(FP8X4), scales=scales[:], in_=vg[first][:])
             for i in range(count):
                 vc[first + i] = codes[:, P * i : P * (i + 1)]
                 vs[first + i] = scales[:, P * i : P * (i + 1)]
 
-        def stage3(n):
-            for half in range(2):
-                s3_banks[n, half] = ring_bank()
+        def stage3(n, halves=(0, 1)):
+            for half in halves:
+                s3_banks[n, half] = next_bank(("s3", n, half))
                 nc.tensor.matmul_mx(
                     out=s3_banks[n, half][:],
                     lhsT=vc[n].bitcast(FP8X4),
@@ -322,321 +306,319 @@ def tile_low_rank_row_mixer_t2_kernel(
 
         def sigmoid_gate(n, first=0, last=D):
             if first == 0:
-                sig[n] = work.tile([P, D], F32, name="sig", tag="wide", bufs=8, align_bytes=ALIGN)
-            nc.scalar.activation(sig[n][:, first:last], gate_sb[n][:, first:last], SIGMOID)
+                sig[n] = buffer(D, F32, "wide", WIDE)
+            nc.scalar.activation(sig[n][:, first:last], gate_sb[ORDER[n]][:, first:last], SIGMOID)
 
-        def move_right_half(n):
-            moved[n] = work.tile([P, BANK], F32, name="moved", tag="sorted_x", bufs=4, align_bytes=ALIGN)
-            on_scalar(out=moved[n][:], in_=s3_banks[n, 1][:])
+        def move_half(n, half=1):
+            moved[n, half] = buffer(BANK, F32, "sorted", SORTED)
+            on_scalar(out=moved[n, half][:], in_=s3_banks[n, half][:])
+            release(("s3", n, half))
 
         products = {}
 
-        def gate_out(n, half):
+        def gate_out(n, half, tag=None):
             cols = slice(BANK * half, BANK * (half + 1))
-            rows = out_rows[n // 4][n % 4]
-            if half == 0:
-                o_tiles[n] = work.tile([P, D], F32, name="o", tag="rows", bufs=6, align_bytes=ALIGN)
-            product = o_tiles[n][:, cols]
-            if half == 1 and n in OWN_BUFFER:
-                own = const.tile([P, BANK], F32, name="o", tag=V_HOLDS[OWN_BUFFER[n]], align_bytes=ALIGN)
+            if tag:
+                own = buffer(BANK, F32, tag)
                 product = own[:]
-            if half == 1 and n in moved:
-                nc.gpsimd.tensor_tensor(out=product, in0=moved[n][:], in1=sig[n][:, cols], op=MULT)
+            else:
+                if n not in o_tiles:
+                    o_tiles[n] = buffer(D, F32, "rows", ROWS)
+                product = o_tiles[n][:, cols]
+            if (n, half) in moved:
+                nc.gpsimd.tensor_tensor(out=product, in0=moved[n, half][:], in1=sig[n][:, cols], op=MULT)
             else:
                 nc.vector.tensor_tensor(out=product, in0=s3_banks[n, half][:], in1=sig[n][:, cols], op=MULT)
+                release(("s3", n, half))
             products[n, half] = product
-            if half == 1 and n not in HALVED:
-                nc.sync.dma_start(out=rows, in_=o_tiles[n][:])
+
+        def store(n):
+            nc.sync.dma_start(out=out_rows[ORDER[n] // 4][:, ORDER[n] % 4], in_=o_tiles[n][:])
 
         def store_half(n, half):
-            nc.sync.dma_start(out=out_rows[n // 4][n % 4][:, BANK * half : BANK * (half + 1)], in_=products[n, half])
+            rows = out_rows[ORDER[n] // 4][:, ORDER[n] % 4]
+            nc.sync.dma_start(out=rows[:, BANK * half : BANK * (half + 1)], in_=products[n, half])
 
-        def gate_both(n):
-            gate_out(n, 0)
-            gate_out(n, 1)
+        stage = [buffer(SHIFT + 4 * R, BF16, "stage%d" % i) for i in range(STAGES)]
+        warm = buffer(1, F32, "warm")
+        ident = buffer(P, F32, "ident")
+        down_raw = buffer(2 * 2 * R, U8, "down_raw")
+        down_sb = buffer(2 * 2 * R, U8, "down_sb")
+        down_sc_raw = buffer(2 * R, U8, "down_sc_raw")
+        down_sc = buffer(2 * R, U8, "down_sc")
+        up_sb = buffer(2 * D, U8, "up_sb")
+        up_sc = buffer(D, U8, "up_sc")
+        packed_sc = buffer(HALF, U8, "packed_sc")
+        dealt_sc = buffer(HALF, U8, "dealt_sc")
+        mix_sc = buffer(GROUPS * T, U8, "mix_sc")
+        keep_sb = sbuf.tile([P, GROUPS, 4], BF16, name="keep_sb", align_bytes=ALIGN)
 
-        def load_words(tile, words, passes):
-            nc.sync.dma_start(
-                out=tile[:].bitcast(I32).rearrange("p (s n) -> p s n", s=passes),
-                in_=words.bitcast(I32).rearrange("s p n -> p s n"),
-            )
+        def load_keep():
+            nc.sync.dma_start(out=keep_sb[:], in_=keep.rearrange("(g p t) -> p g t", p=P, t=4))
 
-        every = list(range(GROUPS))
 
+        nc.vector.memset(warm[:], 0.0)
+        zero(down_sc_raw, 0, 2 * R)
+        zero(up_sc, 0, D)
+        make_identity(nc, ident[:])
+        zero(mix_sc, 0, 2 * T, nc.gpsimd)
         nc.scalar.activation(warm[:], warm[:], SIGMOID)
-
         load_x(0, 1)
         load_x(1, 1)
-        load_scales(down_sc, down_scales, 2)
+        load_scales(down_sc_raw, down_scales, 2)
+        load_words(down_raw, down_words, 2)
         load_x(2, 1)
         load_x(3, 1)
-        load_words(down_sb, down_words, 2)
+        load_mix_scales()
         load_x(4, 2)
-        load_pos(0, 2)
         load_x(6, 2)
+        load_pos(0, 2)
         load_x(8, 2)
-        load_pos(2, 2)
-        load_mix_scales(0)
         load_x(10, 2)
-        load_pos(4, 2)
+        load_pos(2, 2)
         load_x(12, 2)
+        load_pos(4, 2)
+        load_x(14, 2)
         load_pos(6, 2)
         load_mix(0, 1, 0)
-        load_pos(8, 2)
-        load_x(14, 2)
-        load_pos(10, 2)
-        load_mix(1, 1, 0)
 
-        def later_loads():
-            spread_mix_scales(1, 0)
-            load_pos(12, 4)
-            load_mix(2, 1, 0)
-            nc.sync.dma_start(out=keep_sb[:], in_=keep.rearrange("(g p t) -> p g t", p=P, t=4))
-            spread_mix_scales(2, 0)
-            load_mix(3, 1, 0)
-            load_mix(0, 2, 1)
-            spread_mix_scales(3, 0)
-            load_gate(0, 2)
-            load_mix_scales(1)
-            load_gate(2, 2)
-            load_mix(2, 2, 1)
-            load_scales(up_sc, up_scales, 1)
-            load_words(up_sb, up_words, 1)
-            load_gate(4, 2)
-
-        def warm_tensor(count):
-            bank = psum_bank(7)
-            for i in range(count):
-                nc.tensor.matmul_mx(
-                    out=bank[:],
-                    lhsT=zero_codes[:, :P].bitcast(FP8X4),
-                    lhsT_scale=zero_scales[:, :P],
-                    rhs=zero_codes[:].bitcast(U8).bitcast(FP4X4),
-                    rhs_scale=zero_scales[:],
-                    start=True,
-                    stop=True,
-                )
-
-        warm_tensor(3)
-        for n in range(4):
-            if n >= 1:
-                sort_x(on_vector, n)
+        for n in (0, 1):
             turn_x(n)
-            if n == 1:
-                warm_tensor(2)
             copy_x(n)
+        sort_pairs(on_vector, down_sc[:].bitcast(U16), down_sc_raw[:].bitcast(U16))
+        sort_pairs(on_vector, down_sb[:].bitcast(I32), down_raw[:].bitcast(I32))
         quant_x(0, 1)
+        sort_x(on_vector, 2)
         quant_x(1, 1)
         stage1(0)
         stage1(1)
-        sort_x(on_vector, 4)
-        sort_x(on_scalar, 5)
-        quant_x(2, 2)
-        for n in (4, 5):
+        sort_x(on_vector, 3)
+        deal_mix_scales()
+        zero(mix_sc, 2 * T, 4 * T)
+        spread_mix_scales(0, 0)
+        load_pos(8, 4)
+        load_mix(1, 1, 0)
+        spread_mix_scales(1, 0)
+        load_pos(12, 4)
+        load_mix(2, 1, 0)
+        spread_mix_scales(2, 0)
+        load_mix(3, 1, 0)
+        load_keep()
+        spread_mix_scales(3, 0)
+        load_mix(0, 2, 1)
+        load_gate(0, 2)
+        spread_mix_scales(0, 1)
+        load_mix(2, 2, 1)
+        load_gate(2, 2)
+        spread_mix_scales(1, 1)
+        load_gate(4, 2)
+        spread_mix_scales(2, 1)
+        load_words(up_sb, up_words, 1)
+        spread_mix_scales(3, 1)
+        load_gate(6, 2)
+        load_scales(up_sc, up_scales, 1)
+        load_gate(8, 4)
+        for n in range(2, 8):
+            if n >= 4:
+                sort_x(on_vector, n)
             turn_x(n)
             copy_x(n)
+        quant_x(2, 1)
+        quant_x(3, 1)
         add_pos(0)
-        add_pos(1)
-        quant_x(4, 1)
-        sort_x(on_vector, 7)
-        quant_x(5, 1)
         stage1(2)
         stage1(3)
-        for n in (6, 7):
-            turn_x(n)
-            copy_x(n)
-        stage1(4)
         sort_x(on_vector, 8)
         sort_x(on_vector, 9)
-        add_pos(2)
-        quant_x(6, 1)
-        add_pos(3)
-        quant_x(7, 1)
-        for n in (8, 9):
+        add_pos(1)
+        for n in range(8, 12):
             turn_x(n)
             copy_x(n)
-        deal_mix_scales(0)
-        later_loads()
-        quant_x(8, 2)
-        for n in range(5, 8):
+        quant_x(4, 2)
+        quant_x(6, 2)
+        add_pos(2)
+        add_pos(3)
+        for n in range(4, 8):
             stage1(n)
-        round_u_gpsimd(0, 0, G_COLS)
-        sort_x(on_scalar, 11)
+        quant_x(8, 2)
+        quant_x(10, 2)
+        sort_x(on_scalar, 12)
+        sort_x(on_scalar, 13)
         round_u(on_scalar, 0, G_COLS, R)
+        round_u_gpsimd(0, 0, G_COLS)
+        for n in range(12, 16):
+            turn_x(n)
+            copy_x(n)
         for n in range(4, 8):
             add_pos(n)
-
-        for n in (10, 11):
-            turn_x(n)
-            copy_x(n)
-        stage1(8)
-        for n in (12, 13):
-            turn_x(n)
-            copy_x(n)
-        quant_x(10, 1)
-        quant_x(11, 1)
-        quant_u(0, G_COLS, R)
-        quant_u(0, 0, G_COLS)
+        for n in range(8, 12):
+            stage1(n)
         quant_x(12, 2)
-        for n in range(9, 12):
+        quant_u(0)
+        quant_x(14, 2)
+        for n in range(12, 16):
             stage1(n)
         round_u_gpsimd(1, 0, G_COLS)
-        deal_mix(on_scalar, [0], [0])
+        deal_mix(on_scalar, [0], [0, 1], ALL)
         round_u(on_scalar, 1, G_COLS, R)
+        deal_mix(on_scalar, [1], [0, 1], ALL)
         for n in range(8, 12):
             add_pos(n)
-
-        for n in (14, 15):
-            turn_x(n)
-            copy_x(n)
-        quant_x(14, 2)
-        quant_u(1, G_COLS, R)
-        quant_u(1, 0, G_COLS)
-        stage1(12)
-        stage1(13)
-        for n in range(4):
-            stage2(n, [0])
-        stage1(14)
-        stage1(15)
-        round_u_gpsimd(2, 0, G_COLS)
-        deal_mix(on_scalar, [1], [0])
+        quant_u(1)
+        for s in (0, 1):
+            for n in range(4):
+                stage2(n, [s])
+        deal_mix(on_scalar, [2], [0, 1], ALL)
         round_u(on_scalar, 2, G_COLS, R)
-        deal_mix(on_scalar, [0, 1], [1])
-        deal_mix(on_scalar, [2], [0, 1])
+        round_u_gpsimd(2, 0, G_COLS)
+        deal_mix(on_scalar, [3], [0, 1], ALL)
         for n in range(12, 16):
             add_pos(n)
-        quant_u(2, 0, G_COLS)
-        quant_u(2, G_COLS, R)
-        round_u(on_vector, LAST, 0, 256)
-        round_u(on_scalar, LAST, 256, R)
-        quant_u(LAST, 0, 256)
-        quant_u(LAST, 256, R)
-        deal_mix(on_vector, [LAST], [0])
-        deal_mix(on_vector, [LAST], [1])
-        deal_mix_scales(1)
-        spread_mix_scales(1, 1)
-        load_gate(6, 2)
-        spread_mix_scales(2, 1)
-        load_gate(8, 2)
-        spread_mix_scales(3, 1)
-        load_gate(10, 2)
+            stage2(n - 8, [0, 1])
+        quant_u(2)
+        round_u(on_vector, 3, 0, V_COLS)
+        round_u(on_scalar, 3, V_COLS, R)
+        quant_u(3)
+        for s in (2, 3):
+            for n in range(4):
+                stage2(n, [s])
+        for n in range(4, 7):
+            stage2(n, [2, 3])
+
+        def products_of(n):
+            gate_out(n, 0)
+            gate_out(n, 1)
+
+        def turn_and_copy(first, count, tag=None):
+            turn_v(first, count)
+            copy_v(first, count, tag)
+
+        deal_mix(on_gpsimd, [0, 1], [2], ALL, "stage0")
+        deal_mix(on_gpsimd, [2, 3], [2], ALL)
+        deal_mix(on_gpsimd, [0, 1], [3], ALL)
         for n in range(4):
-            stage2(n, [1])
-        for n in range(4, EARLY):
-            stage2(n, [0, 1])
-        for n in range(EARLY):
-            stage2(n, [2])
-        for n in range(EARLY):
-            stage2(n, [LAST])
-
-        deal_mix(on_gpsimd, [0, 1], [2], "hold3")
-        deal_mix(on_gpsimd, [2, 3], [2])
-        sigmoid_gate(0)
-        sigmoid_gate(1)
-        sigmoid_gate(2)
-        sigmoid_gate(3, 0, BANK)
-        stage2(6, [0])
-        add_u(0)
-        add_u(1)
-        turn_v(0, 2)
-        copy_v(0, 2)
-        sigmoid_gate(3, BANK)
-        sigmoid_gate(4)
-        sigmoid_gate(5)
-        stage2(6, [1, 2, 3])
-        stage2(7, every)
-        add_u(2)
-        add_u(3)
+            sigmoid_gate(n)
+        sigmoid_gate(4, 0, BANK)
+        for n in range(4):
+            add_u(n)
         load_gate(12, 4, "u0")
+        turn_and_copy(0, 2)
+        turn_and_copy(2, 2, "stage2")
+        stage2(7, [2, 3])
         add_u(4)
-        quant_v(0, 2)
-        deal_mix(on_gpsimd, [0, 1], [3], "hold2")
-        deal_mix(on_gpsimd, [2, 3], [3])
         add_u(5)
+        stage2(8)
         add_u(6)
-        stage3(0)
-        stage3(1)
-        gate_both(0)
+        quant_v(0, 2)
+        quant_v(2, 2)
         add_u(7)
-
-        def halves(first, count):
-            for i in range(first, first + count):
-                if i % 2 == 0 and i + 1 < first + count:
-                    sigmoid_gate(i // 2)
-                elif i % 2 == 0:
-                    sigmoid_gate(i // 2, 0, BANK)
-                elif i == first:
-                    sigmoid_gate(i // 2, BANK)
-
-        def begin_round(a, count, e):
-            turn_v(a, 2)
-            turn_v(a + 2, count - 2)
-            copy_v(a, 2)
-            copy_v(a + 2, count - 2)
-            move_right_half(a - 1)
-            stage2(e, every)
-            stage2(e + 1, [0, 1, 2] if a == 6 else [0, 1])
-            gate_out(a - 1, 0)
-            store_half(a - 1, 0)
-            quant_v(a, 2)
-            quant_v(a + 2, count - 2)
-            gate_out(a - 1, 1)
-            add_u(e)
-            stage3(a)
-
-        def second_half(a, e):
-            move_right_half(a)
-            if a < 10:
-                store_half(a - 1, 1)
-            gate_both(a)
-            if a == 10:
-                store_half(a, 0)
-            stage2(e + 1, [LAST] if a == 6 else [2, 3])
-            add_u(e + 1)
-            stage3(a + 1)
-            if a == 10:
-                store_half(a - 1, 1)
-
-        for a, e, h in ((2, 8, 12), (6, 10, 17)):
-            begin_round(a, 4, e)
-            halves(h, 2)
-            second_half(a, e)
-            gate_both(a + 1)
-            if a == 6:
-                stage2(e + 2, every)
-                add_u(e + 2)
-            stage3(a + 2)
-            stage3(a + 3)
-            halves(h + 2, 3 if a == 2 else 5)
-            gate_both(a + 2)
-
-        begin_round(10, 3, 13)
-        halves(24, 1)
-        second_half(10, 13)
+        sigmoid_gate(4, BANK)
+        sigmoid_gate(5)
+        stage3(0)
+        stage3(1, (1, 0))
+        deal_mix(on_gpsimd, [2, 3], [3], ALL, "stage2")
+        move_half(1)
+        products_of(0)
+        store(0)
+        add_u(8)
+        stage2(9)
+        products_of(1)
+        store(1)
+        sigmoid_gate(6)
+        stage3(2)
+        add_u(9)
+        stage3(3, (1, 0))
+        sigmoid_gate(7, 0, BANK)
+        move_half(3)
+        products_of(2)
+        store(2)
+        gate_out(3, 0)
+        store_half(3, 0)
+        turn_and_copy(4, 2)
+        turn_and_copy(6, 2, "stage1")
+        stage2(10)
+        stage2(11, [0, 1])
+        quant_v(4, 2)
+        quant_v(6, 2)
+        gate_out(3, 1, "stage1")
+        sigmoid_gate(7, BANK)
+        sigmoid_gate(8, 0, BANK)
+        stage3(4, (1, 0))
+        move_half(4)
+        add_u(10)
+        products_of(4)
+        store_half(4, 0)
+        store_half(3, 1)
+        store_half(4, 1)
+        stage2(11, [2, 3])
+        sigmoid_gate(8, BANK)
+        stage3(5, (1, 0))
+        move_half(5)
+        sigmoid_gate(9, 0, BANK)
+        add_u(11)
+        products_of(5)
+        store_half(5, 0)
+        stage3(6)
+        products_of(6)
+        stage3(7, (1, 0))
+        move_half(7)
+        store(6)
+        store_half(5, 1)
+        gate_out(7, 0)
+        store_half(7, 0)
+        turn_and_copy(8, 2)
+        turn_and_copy(10, 2, "stage3")
+        stage2(12)
+        stage2(13, [0, 1])
+        quant_v(8, 2)
+        quant_v(10, 2)
+        gate_out(7, 1, "stage3")
+        sigmoid_gate(9, BANK)
+        sigmoid_gate(10, 0, BANK)
+        stage3(8, (1, 0))
+        move_half(8)
+        add_u(12)
+        products_of(8)
+        store_half(8, 0)
+        store_half(7, 1)
+        sigmoid_gate(10, BANK)
+        sigmoid_gate(11)
+        stage2(13, [2, 3])
+        stage3(9)
+        add_u(13)
+        products_of(9)
+        store(9)
+        store_half(8, 1)
+        stage3(10)
+        products_of(10)
+        turn_and_copy(12, 2, "stage0")
+        sigmoid_gate(12)
+        stage2(14)
+        quant_v(12, 2)
+        store(10)
+        add_u(14)
+        stage3(11, (1, 0))
+        move_half(11)
+        sigmoid_gate(13)
+        gate_out(11, 1, "stage0")
+        gate_out(11, 0)
+        store_half(11, 0)
+        stage2(15, [0, 1])
         stage3(12)
-        halves(25, 2)
-        for half in range(2):
-            gate_out(11, half)
-            store_half(11, half)
-            if half == 0:
-                store_half(10, 1)
-        turn_v(13, 2)
-        copy_v(13, 2)
-        halves(27, 3)
-        stage2(15, every)
-        gate_out(12, 0)
-        store_half(12, 0)
-        quant_v(13, 2)
+        products_of(12)
+        store(12)
+        store_half(11, 1)
+        turn_and_copy(14, 1)
+        sigmoid_gate(14)
+        sigmoid_gate(15, 0, BANK)
+        stage2(15, [2, 3])
         add_u(15)
-        gate_out(12, 1)
-        store_half(12, 1)
+        quant_v(14, 1)
         stage3(13)
-        turn_v(15, 1)
-        copy_v(15, 1)
-        halves(30, 2)
-        for half in range(2):
-            gate_out(13, half)
-            store_half(13, half)
+        products_of(13)
+        store(13)
+        turn_and_copy(15, 1)
+        sigmoid_gate(15, BANK)
         stage3(14)
         quant_v(15, 1)
         stage3(15)

@@ -24,10 +24,10 @@ LAST = GROUPS - 1
 BANK = 512
 ALIGN = 256
 HALF = T // 2
-SINGLES, ROWS, WIDE, SORTED, CODES, VB, STAGES = 4, 6, 8, 4, 4, 8, 4
+SINGLES, ROWS, WIDE, SORTED, CODES, VB, STAGES = 4, 6, 8, 4, 4, 6, 4
 XG = [0, 1, 2, 3, 0, 1, 2, 3]
 UG = [1, 3, 3, 0]
-G_COLS = 288
+G_COLS = 256
 SHIFT = 4 * (R - G_COLS)
 ORDER = list(range(16))
 ALL = [0, 1, 2, 3]
@@ -124,20 +124,19 @@ def tile_low_rank_row_mixer_t2_kernel(
 
         def load_mix_scales():
             nc.sync.dma_start(
-                out=packed_sc[:].bitcast(I32), in_=mix_scales.bitcast(I32).rearrange("s q (h n) -> (s q h) n", h=2)
+                out=packed_sc[:].bitcast(I32)[0:P:2], in_=mix_scales.bitcast(I32).rearrange("s q n -> (s q) n")
             )
 
         def deal_mix_scales():
             on_vector(
-                out=dealt_sc[:].rearrange("p (g t c i) -> p g c t i", g=2, t=4, i=16),
-                in_=packed_sc[:].rearrange("p (g c i t) -> p g c t i", g=2, t=4, i=16),
+                out=dealt_sc[:].rearrange("p (g t c i) -> p g c t i", g=GROUPS, t=4, i=16),
+                in_=packed_sc[:].rearrange("p (g c i t) -> p g c t i", g=GROUPS, t=4, i=16),
             )
 
-        def spread_mix_scales(s, half):
-            col = T * s + HALF * half
-            dst = mix_sc[:, col : col + HALF].bitcast(I32)
+        def spread_mix_scales(s):
+            dst = mix_sc[:, T * s : T * (s + 1)].bitcast(I32)
             for r in range(4):
-                first = 32 * s + 2 * r + half
+                first = 32 * s + 2 * r
                 nc.sync.dma_start(out=dst[r:P:32], in_=dealt_sc[:].bitcast(I32)[first : first + 25 : 8])
 
         def sort_pairs(copy, dst, src):
@@ -316,9 +315,11 @@ def tile_low_rank_row_mixer_t2_kernel(
 
         products = {}
 
-        def gate_out(n, half, tag=None):
+        def gate_out(n, half, tag=None, whole=False):
             cols = slice(BANK * half, BANK * (half + 1))
-            if tag:
+            if tag and whole:
+                o_tiles[n] = buffer(D, F32, tag)
+            if tag and not whole:
                 own = buffer(BANK, F32, tag)
                 product = own[:]
             else:
@@ -348,8 +349,8 @@ def tile_low_rank_row_mixer_t2_kernel(
         down_sc = buffer(2 * R, U8, "down_sc")
         up_sb = buffer(2 * D, U8, "up_sb")
         up_sc = buffer(D, U8, "up_sc")
-        packed_sc = buffer(HALF, U8, "packed_sc")
-        dealt_sc = buffer(HALF, U8, "dealt_sc")
+        packed_sc = buffer(T, U8, "packed_sc")
+        dealt_sc = buffer(T, U8, "dealt_sc")
         mix_sc = buffer(GROUPS * T, U8, "mix_sc")
         keep_sb = sbuf.tile([P, GROUPS, 4], BF16, name="keep_sb", align_bytes=ALIGN)
 
@@ -360,6 +361,8 @@ def tile_low_rank_row_mixer_t2_kernel(
         nc.vector.memset(warm[:], 0.0)
         zero(down_sc_raw, 0, 2 * R)
         zero(up_sc, 0, D)
+        zero(packed_sc, 0, T)
+        zero(mix_sc, 2 * T, 4 * T)
         make_identity(nc, ident[:])
         zero(mix_sc, 0, 2 * T, nc.gpsimd)
         nc.scalar.activation(warm[:], warm[:], SIGMOID)
@@ -388,38 +391,35 @@ def tile_low_rank_row_mixer_t2_kernel(
         sort_pairs(on_vector, down_sc[:].bitcast(U16), down_sc_raw[:].bitcast(U16))
         sort_pairs(on_vector, down_sb[:].bitcast(I32), down_raw[:].bitcast(I32))
         quant_x(0, 1)
-        sort_x(on_vector, 2)
+        sort_x(on_scalar, 2)
         quant_x(1, 1)
         stage1(0)
         stage1(1)
-        sort_x(on_vector, 3)
+        sort_x(on_scalar, 3)
         deal_mix_scales()
-        zero(mix_sc, 2 * T, 4 * T)
-        spread_mix_scales(0, 0)
+        spread_mix_scales(0)
         load_pos(8, 4)
         load_mix(1, 1, 0)
-        spread_mix_scales(1, 0)
+        spread_mix_scales(1)
         load_pos(12, 4)
         load_mix(2, 1, 0)
-        spread_mix_scales(2, 0)
+        spread_mix_scales(2)
         load_mix(3, 1, 0)
-        load_keep()
-        spread_mix_scales(3, 0)
-        load_mix(0, 2, 1)
         load_gate(0, 2)
-        spread_mix_scales(0, 1)
+        spread_mix_scales(3)
+        load_mix(0, 2, 1)
+        load_keep()
         load_mix(2, 2, 1)
         load_gate(2, 2)
-        spread_mix_scales(1, 1)
-        load_gate(4, 2)
-        spread_mix_scales(2, 1)
-        load_words(up_sb, up_words, 1)
-        spread_mix_scales(3, 1)
-        load_gate(6, 2)
         load_scales(up_sc, up_scales, 1)
+        load_gate(4, 2)
+        load_words(up_sb, up_words, 1)
+        load_gate(6, 2)
         load_gate(8, 4)
+        sort_x(on_scalar, 4)
+        sort_x(on_scalar, 5)
         for n in range(2, 8):
-            if n >= 4:
+            if n >= 6:
                 sort_x(on_vector, n)
             turn_x(n)
             copy_x(n)
@@ -448,9 +448,10 @@ def tile_low_rank_row_mixer_t2_kernel(
         round_u_gpsimd(0, 0, G_COLS)
         for n in range(12, 16):
             turn_x(n)
-            copy_x(n)
         for n in range(4, 8):
             add_pos(n)
+        for n in range(12, 16):
+            copy_x(n)
         for n in range(8, 12):
             stage1(n)
         quant_x(12, 2)
@@ -480,9 +481,9 @@ def tile_low_rank_row_mixer_t2_kernel(
         round_u(on_scalar, 3, V_COLS, R)
         quant_u(3)
         for s in (2, 3):
-            for n in range(4):
+            for n in range(5):
                 stage2(n, [s])
-        for n in range(4, 7):
+        for n in range(5, 7):
             stage2(n, [2, 3])
 
         def products_of(n):
@@ -493,8 +494,8 @@ def tile_low_rank_row_mixer_t2_kernel(
             turn_v(first, count)
             copy_v(first, count, tag)
 
-        deal_mix(on_gpsimd, [0, 1], [2], ALL, "stage0")
-        deal_mix(on_gpsimd, [2, 3], [2], ALL)
+        deal_mix(on_vector, [0, 1], [2], ALL)
+        deal_mix(on_gpsimd, [2, 3], [2], ALL, "stage0")
         deal_mix(on_gpsimd, [0, 1], [3], ALL)
         for n in range(4):
             sigmoid_gate(n)
@@ -549,21 +550,19 @@ def tile_low_rank_row_mixer_t2_kernel(
         products_of(4)
         store_half(4, 0)
         store_half(3, 1)
-        store_half(4, 1)
         stage2(11, [2, 3])
+        stage3(5)
         sigmoid_gate(8, BANK)
-        stage3(5, (1, 0))
-        move_half(5)
-        sigmoid_gate(9, 0, BANK)
+        sigmoid_gate(9)
         add_u(11)
         products_of(5)
-        store_half(5, 0)
+        store(5)
+        store_half(4, 1)
         stage3(6)
         products_of(6)
         stage3(7, (1, 0))
         move_half(7)
         store(6)
-        store_half(5, 1)
         gate_out(7, 0)
         store_half(7, 0)
         turn_and_copy(8, 2)
@@ -573,16 +572,15 @@ def tile_low_rank_row_mixer_t2_kernel(
         quant_v(8, 2)
         quant_v(10, 2)
         gate_out(7, 1, "stage3")
-        sigmoid_gate(9, BANK)
-        sigmoid_gate(10, 0, BANK)
+        sigmoid_gate(10)
         stage3(8, (1, 0))
         move_half(8)
         add_u(12)
         products_of(8)
         store_half(8, 0)
         store_half(7, 1)
-        sigmoid_gate(10, BANK)
         sigmoid_gate(11)
+        sigmoid_gate(12, 0, BANK)
         stage2(13, [2, 3])
         stage3(9)
         add_u(13)
@@ -592,7 +590,7 @@ def tile_low_rank_row_mixer_t2_kernel(
         stage3(10)
         products_of(10)
         turn_and_copy(12, 2, "stage0")
-        sigmoid_gate(12)
+        sigmoid_gate(12, BANK)
         stage2(14)
         quant_v(12, 2)
         store(10)

@@ -358,8 +358,28 @@ def tile_low_rank_row_mixer_t2_kernel(
             nc.sync.dma_start(out=keep_sb[:], in_=keep.rearrange("(g p t) -> p g t", p=P, t=4))
 
 
+        def warm_tensor(count):
+            bank = next_bank("warm")
+            for i in range(count):
+                nc.tensor.matmul_mx(
+                    out=bank[:],
+                    lhsT=zero_codes[:, :P].bitcast(FP8X4),
+                    lhsT_scale=zero_scales[:, :P],
+                    rhs=zero_codes[:].bitcast(U8).bitcast(FP4X4),
+                    rhs_scale=zero_scales[:],
+                    start=True,
+                    stop=True,
+                )
+            release("warm")
+
+        zero_codes = buffer(D // 4, U32, "codes", CODES)
+        zero_scales = buffer(BANK, U8, "scales", CODES)
+
         nc.vector.memset(warm[:], 0.0)
         zero(down_sc_raw, 0, 2 * R)
+        nc.vector.memset(stage[3][:, :D].bitcast(I32), 0)
+        zero(zero_scales, 0, BANK)
+        nc.vector.quantize_mx(out=zero_codes[:].bitcast(FP8X4), scales=zero_scales[:, : D // 4], in_=stage[3][:, :D])
         zero(up_sc, 0, D)
         zero(packed_sc, 0, T)
         zero(mix_sc, 2 * T, 4 * T)
@@ -388,6 +408,7 @@ def tile_low_rank_row_mixer_t2_kernel(
         for n in (0, 1):
             turn_x(n)
             copy_x(n)
+        warm_tensor(2)
         sort_pairs(on_vector, down_sc[:].bitcast(U16), down_sc_raw[:].bitcast(U16))
         sort_pairs(on_vector, down_sb[:].bitcast(I32), down_raw[:].bitcast(I32))
         quant_x(0, 1)

from contextlib import ExitStack

import concourse.mybir as mybir
from concourse.masks import make_identity

T, D, R = 2048, 1024, 512
FLOPS = 2 * T * D * R + 2 * T * T * R + 2 * T * R * D

F32 = mybir.dt.float32
BF16 = mybir.dt.bfloat16
I32 = mybir.dt.int32
U32 = mybir.dt.uint32
U16 = mybir.dt.uint16
U8 = mybir.dt.uint8
FP8X4 = mybir.dt.float8_e4m3fn_x4
FP4X4 = mybir.dt.float4_e2m1fn_x4
ADD = mybir.AluOpType.add
MULT = mybir.AluOpType.mult
SIGMOID = mybir.ActivationFunctionType.Sigmoid

P = 128
GROUPS = T // 512
LAST = GROUPS - 1
BANK = 512
ALIGN = 256
HALF = T // 2
SINGLES, ROWS, WIDE, SORTED, CODES, VB, STAGES = 4, 6, 8, 4, 4, 6, 4
XG = [0, 1, 2, 3, 0, 1, 2, 3]
UG = [1, 3, 3, 0]
G_COLS = 256
SHIFT = 4 * (R - G_COLS)
ORDER = list(range(16))
ALL = [0, 1, 2, 3]
V_COLS = 352


def tile_low_rank_row_mixer_t2_kernel(
    tc, x, pos, keep, gate, down_words, down_scales, mix_words, mix_scales, up_words, up_scales, out
):
    nc = tc.nc
    with ExitStack() as ctx:
        sbuf = ctx.enter_context(tc.tile_pool(name="sbuf", bufs=1))
        psum = ctx.enter_context(tc.psum_pool(name="psum", bufs=1))
        ctx.enter_context(tc.manual_schedule())
        on_vector, on_scalar, on_gpsimd = nc.vector.tensor_copy, nc.scalar.copy, nc.gpsimd.tensor_copy

        def buffer(width, dtype, tag, bufs=1):
            tile = sbuf.tile([P, width], dtype, name=tag, tag=tag, bufs=bufs, align_bytes=ALIGN)
            return tile

        free_banks, held = list(range(8)), {}

        def next_bank(key):
            held[key] = free_banks.pop(0)
            name = "bank%d" % held[key]
            bank = psum.tile([P, BANK], F32, name=name, tag=name)
            return bank

        def release(key):
            free_banks.append(held.pop(key))

        def zero(tile, first, last, engine=nc.vector):
            engine.memset(tile[:, first:last].bitcast(I32), 0)

        x_rows = x.rearrange("(g p t) k -> g p t k", p=P, t=4)
        pos_rows = pos.rearrange("(g p t) r -> g p t r", p=P, t=4)
        gate_rows = gate.rearrange("(g p t) c -> g p t c", p=P, t=4)
        out_rows = out.rearrange("(g p t) c -> g p t c", p=P, t=4)

        x_sb, pos_sb, gate_sb, mix_sb, mix_raw = {}, {}, {}, {}, {}

        def load_rows(rows, width, into, first, count, tag, bufs=1):
            tile = buffer(count * width, BF16, tag, bufs)
            g, t = divmod(first, 4)
            nc.sync.dma_start(out=tile[:].rearrange("p (t k) -> p t k", t=count), in_=rows[g][:, t : t + count])
            for i in range(count):
                into[first + i] = tile[:, width * i : width * (i + 1)]

        def load_x(first, count):
            if count == 1:
                load_rows(x_rows, D, x_sb, first, count, "single", SINGLES)
            else:
                load_rows(x_rows, D, x_sb, first, count, "rows", ROWS)

        def load_pos(first, count):
            load_rows(pos_rows, R, pos_sb, first, count, "wide", WIDE)

        def load_gate(first, count, tag=None):
            load_rows(gate_rows, D, gate_sb, first, count, tag or "gate%d" % first)

        def load_scales(plane, scales, passes):
            src = scales.bitcast(I32).rearrange("s q n -> q s n")
            dst = plane[:].bitcast(I32).rearrange("p (s n) -> p s n", s=passes)
            for r in range(4):
                nc.sync.dma_start(out=dst[r:P:32], in_=src[r:16:4])

        def load_words(tile, words, passes):
            nc.sync.dma_start(
                out=tile[:].bitcast(I32).rearrange("p (s n) -> p s n", s=passes),
                in_=words.bitcast(I32).rearrange("s p n -> p s n"),
            )

        def load_mix(first, count, half):
            if half not in mix_raw:
                mix_raw[half] = buffer(GROUPS * T, U8, "mix_raw%d" % half)
            cols = slice(T // 4 * half, T // 4 * (half + 1))
            nc.sync.dma_start(
                out=mix_raw[half][:, T * first : T * (first + count)].bitcast(I32).rearrange("p (s n) -> p s n", s=count),
                in_=mix_words.bitcast(I32).rearrange("s p n -> p s n")[:, first : first + count, cols],
            )

        def deal_mix(copy, passes, groups, slots, tag=None):
            count, width = len(passes) * len(groups), len(slots)
            dealt = buffer(2 * P * width * count, U8, tag or "mix%d_%d_%d" % (passes[0], groups[0], slots[0]))
            half, first = divmod(groups[0], 2)
            words = mix_raw[half][:].bitcast(U16).rearrange("p (j c i t) -> p j c t i", j=2 * GROUPS, t=4, i=8)
            start, step = 2 * passes[0] + first, 3 - len(groups)
            source = words[:, start : start + step * (count - 1) + 1 : step, :, slots[0] : slots[0] + width]
            for j, (s, g) in enumerate((s, g) for s in passes for g in groups):
                for i, t in enumerate(slots):
                    col = 2 * P * (width * j + i)
                    mix_sb[4 * g + t, s] = dealt[:, col : col + 2 * P]
            copy(out=dealt[:].bitcast(U16).rearrange("p (j t c i) -> p j c t i", j=count, t=width, i=8), in_=source)

        def load_mix_scales():
            nc.sync.dma_start(
                out=packed_sc[:].bitcast(I32)[0:P:2], in_=mix_scales.bitcast(I32).rearrange("s q n -> (s q) n")
            )

        def deal_mix_scales():
            on_vector(
                out=dealt_sc[:].rearrange("p (g t c i) -> p g c t i", g=GROUPS, t=4, i=16),
                in_=packed_sc[:].rearrange("p (g c i t) -> p g c t i", g=GROUPS, t=4, i=16),
            )

        def spread_mix_scales(s):
            dst = mix_sc[:, T * s : T * (s + 1)].bitcast(I32)
            for r in range(4):
                first = 32 * s + 2 * r
                nc.sync.dma_start(out=dst[r:P:32], in_=dealt_sc[:].bitcast(I32)[first : first + 25 : 8])

        def sort_pairs(copy, dst, src):
            copy(
                out=dst.rearrange("p (k h c i) -> p k c h i", k=2, h=2, i=4),
                in_=src.rearrange("p (k c i h) -> p k c h i", k=2, h=2, i=4),
            )

        sorted_x, xt_banks, xg, xc, xs, s1_banks, u, ug, uc, us = {}, {}, {}, {}, {}, {}, {}, {}, {}, {}

        def sort_x(copy, n):
            sorted_x[n] = buffer(512, F32, "sorted", SORTED)
            sort_pairs(copy, sorted_x[n][:], x_sb[n].bitcast(F32))

        def turn_x(n):
            words = x_sb[n].bitcast(F32)
            xt_banks[n] = next_bank(("xt", n))
            for k in range(2):
                for h in range(2):
                    col = P * (2 * k + h)
                    if n in sorted_x:
                        src = sorted_x[n][:, col : col + P]
                    else:
                        src = words[:, 256 * k + h : 256 * (k + 1) : 2]
                    nc.tensor.transpose(xt_banks[n][:, col : col + P], src, ident[:])

        def copy_x(n, copy=on_scalar):
            q, i = divmod(n, 2)
            if i == 0:
                xg[q] = stage[XG[q]][:, : 2 * D]
            copy(
                out=xg[q][:, D * i : D * (i + 1)].bitcast(F32).rearrange("p (k r h) -> p k r h", k=2, h=2),
                in_=xt_banks[n][:].rearrange("p (k h r) -> p k r h", k=2, h=2),
            )
            release(("xt", n))

        def quant_x(first, count):
            q, i = divmod(first, 2)
            if i == 0:
                xc[q] = buffer(4 * P, U32, "codes", CODES)
                xs[q] = buffer(4 * P, U8, "scales", CODES)
            cols = slice(2 * P * i, 2 * P * (i + count))
            nc.vector.quantize_mx(
                out=xc[q][:, cols].bitcast(FP8X4), scales=xs[q][:, cols], in_=xg[q][:, D * i : D * (i + count)]
            )

        def stage1(n):
            q, i = divmod(n, 2)
            s1_banks[n] = next_bank(("s1", n))
            for k in range(2):
                cols = slice(P * (2 * i + k), P * (2 * i + k + 1))
                nc.tensor.matmul_mx(
                    out=s1_banks[n][:],
                    lhsT=xc[q][:, cols].bitcast(FP8X4),
                    lhsT_scale=xs[q][:, cols],
                    rhs=down_sb[:, 2 * R * k : 2 * R * (k + 1)].bitcast(FP4X4),
                    rhs_scale=down_sc[:, R * k : R * (k + 1)],
                    start=(k == 0),
                    stop=(k == 1),
                )

        def add_pos(n):
            g, t = divmod(n, 4)
            if t == 0:
                u[g] = sbuf.tile([P, 4, R], F32, name="u", tag="u%d" % g, align_bytes=ALIGN)
            nc.vector.tensor_tensor(
                out=u[g][:, t].rearrange("p (h m e) -> p h m e", h=2, e=2),
                in0=s1_banks[n][:].rearrange("p (h m e) -> p h m e", h=2, e=2),
                in1=pos_sb[n].rearrange("p (m h e) -> p h m e", h=2, e=2),
                op=ADD,
            )
            release(("s1", n))

        def rounded(g, first, last):
            if g not in ug:
                ug[g] = stage[UG[g]][:, SHIFT : SHIFT + 4 * R]
            return ug[g][:, 4 * first : 4 * last]

        def round_u(copy, g, first, last):
            copy(
                out=rounded(g, first, last).rearrange("p (c i t) -> p c t i", t=4, i=4),
                in_=u[g][:, :, first:last].rearrange("p t (c i) -> p c t i", i=4),
            )

        def round_u_gpsimd(g, first, last):
            nc.gpsimd.tensor_scalar(
                out=rounded(g, first, last).rearrange("p (c t) -> p c t", t=4),
                in0=u[g][:, :, first:last].rearrange("p t c -> p c t"),
                scalar1=1.0,
                scalar2=0.0,
                op0=MULT,
                op1=ADD,
            )

        def quant_u(g, first=0, last=R):
            if g not in uc:
                uc[g] = buffer(R, U32, "uc%d" % g)
                us[g] = buffer(R, U8, "us%d" % g)
            nc.vector.quantize_mx(
                out=uc[g][:, first:last].bitcast(FP8X4), scales=us[g][:, first:last], in_=ug[g][:, 4 * first : 4 * last]
            )

        s2_banks, vb, vt, vg, vc, vs, s3_banks, sig, moved, o_tiles = {}, {}, {}, {}, {}, {}, {}, {}, {}, {}

        def stage2(n, passes=(0, 1, 2, 3)):
            if passes[0] == 0:
                s2_banks[n] = next_bank(("s2", n))
            for s in passes:
                nc.tensor.matmul_mx(
                    out=s2_banks[n][:],
                    lhsT=mix_sb[ORDER[n], s].bitcast(FP4X4),
                    lhsT_scale=mix_sc[:, T * s + P * ORDER[n] : T * s + P * (ORDER[n] + 1)],
                    rhs=uc[s][:].bitcast(FP8X4),
                    rhs_scale=us[s][:],
                    start=(s == 0),
                    stop=(s == LAST),
                )

        def add_u(n):
            g, t = divmod(ORDER[n], 4)
            vb[n] = buffer(R, BF16, "vb", VB)
            nc.vector.scalar_tensor_tensor(
                out=vb[n][:], in0=u[g][:, t], scalar=keep_sb[:, g, t : t + 1], in1=s2_banks[n][:], op0=MULT, op1=ADD
            )
            release(("s2", n))

        def turn_v(first, count):
            vt[first] = next_bank(("vt", first))
            for i in range(count):
                words = vb[first + i][:].bitcast(F32)
                for h in range(2):
                    col = P * (2 * i + h)
                    nc.tensor.transpose(vt[first][:, col : col + P], words[:, P * h : P * (h + 1)], ident[:])

        def copy_v(first, count, tag=None):
            if tag:
                vg[first] = buffer(count * R, BF16, tag)
            else:
                vg[first] = buffer(count * R, BF16, "single", SINGLES)
            on_scalar(
                out=vg[first][:].bitcast(F32).rearrange("m (i p h) -> m i p h", i=count, h=2),
                in_=vt[first][:, : 2 * P * count].rearrange("m (i h p) -> m i p h", i=count, h=2),
            )
            release(("vt", first))

        def quant_v(first, count):
            codes = buffer(count * P, U32, "codes", CODES)
            scales = buffer(count * P, U8, "scales", CODES)
            nc.vector.quantize_mx(out=codes[:].bitcast(FP8X4), scales=scales[:], in_=vg[first][:])
            for i in range(count):
                vc[first + i] = codes[:, P * i : P * (i + 1)]
                vs[first + i] = scales[:, P * i : P * (i + 1)]

        def stage3(n, halves=(0, 1)):
            for half in halves:
                s3_banks[n, half] = next_bank(("s3", n, half))
                nc.tensor.matmul_mx(
                    out=s3_banks[n, half][:],
                    lhsT=vc[n].bitcast(FP8X4),
                    lhsT_scale=vs[n],
                    rhs=up_sb[:, 2 * BANK * half : 2 * BANK * (half + 1)].bitcast(FP4X4),
                    rhs_scale=up_sc[:, BANK * half : BANK * (half + 1)],
                    start=True,
                    stop=True,
                )

        def sigmoid_gate(n, first=0, last=D):
            if first == 0:
                sig[n] = buffer(D, F32, "wide", WIDE)
            nc.scalar.activation(sig[n][:, first:last], gate_sb[ORDER[n]][:, first:last], SIGMOID)

        def move_half(n, half=1):
            moved[n, half] = buffer(BANK, F32, "sorted", SORTED)
            on_scalar(out=moved[n, half][:], in_=s3_banks[n, half][:])
            release(("s3", n, half))

        products = {}

        def gate_out(n, half, tag=None, whole=False):
            cols = slice(BANK * half, BANK * (half + 1))
            if tag and whole:
                o_tiles[n] = buffer(D, F32, tag)
            if tag and not whole:
                own = buffer(BANK, F32, tag)
                product = own[:]
            else:
                if n not in o_tiles:
                    o_tiles[n] = buffer(D, F32, "rows", ROWS)
                product = o_tiles[n][:, cols]
            if (n, half) in moved:
                nc.gpsimd.tensor_tensor(out=product, in0=moved[n, half][:], in1=sig[n][:, cols], op=MULT)
            else:
                nc.vector.tensor_tensor(out=product, in0=s3_banks[n, half][:], in1=sig[n][:, cols], op=MULT)
                release(("s3", n, half))
            products[n, half] = product

        def store(n):
            nc.sync.dma_start(out=out_rows[ORDER[n] // 4][:, ORDER[n] % 4], in_=o_tiles[n][:])

        def store_half(n, half):
            rows = out_rows[ORDER[n] // 4][:, ORDER[n] % 4]
            nc.sync.dma_start(out=rows[:, BANK * half : BANK * (half + 1)], in_=products[n, half])

        stage = [buffer(SHIFT + 4 * R, BF16, "stage%d" % i) for i in range(STAGES)]
        warm = buffer(1, F32, "warm")
        ident = buffer(P, F32, "ident")
        down_raw = buffer(2 * 2 * R, U8, "down_raw")
        down_sb = buffer(2 * 2 * R, U8, "down_sb")
        down_sc_raw = buffer(2 * R, U8, "down_sc_raw")
        down_sc = buffer(2 * R, U8, "down_sc")
        up_sb = buffer(2 * D, U8, "up_sb")
        up_sc = buffer(D, U8, "up_sc")
        packed_sc = buffer(T, U8, "packed_sc")
        dealt_sc = buffer(T, U8, "dealt_sc")
        mix_sc = buffer(GROUPS * T, U8, "mix_sc")
        keep_sb = sbuf.tile([P, GROUPS, 4], BF16, name="keep_sb", align_bytes=ALIGN)

        def load_keep():
            nc.sync.dma_start(out=keep_sb[:], in_=keep.rearrange("(g p t) -> p g t", p=P, t=4))


        def warm_tensor(count):
            bank = next_bank("warm")
            for i in range(count):
                nc.tensor.matmul_mx(
                    out=bank[:],
                    lhsT=zero_codes[:, :P].bitcast(FP8X4),
                    lhsT_scale=zero_scales[:, :P],
                    rhs=zero_codes[:].bitcast(U8).bitcast(FP4X4),
                    rhs_scale=zero_scales[:],
                    start=True,
                    stop=True,
                )
            release("warm")

        zero_codes = buffer(D // 4, U32, "codes", CODES)
        zero_scales = buffer(BANK, U8, "scales", CODES)

        nc.vector.memset(warm[:], 0.0)
        zero(down_sc_raw, 0, 2 * R)
        nc.vector.memset(stage[3][:, :D].bitcast(I32), 0)
        zero(zero_scales, 0, BANK)
        nc.vector.quantize_mx(out=zero_codes[:].bitcast(FP8X4), scales=zero_scales[:, : D // 4], in_=stage[3][:, :D])
        zero(up_sc, 0, D)
        zero(packed_sc, 0, T)
        zero(mix_sc, 2 * T, 4 * T)
        make_identity(nc, ident[:])
        zero(mix_sc, 0, 2 * T, nc.gpsimd)
        nc.scalar.activation(warm[:], warm[:], SIGMOID)
        load_x(0, 1)
        load_x(1, 1)
        load_scales(down_sc_raw, down_scales, 2)
        load_words(down_raw, down_words, 2)
        load_x(2, 1)
        load_x(3, 1)
        load_mix_scales()
        load_x(4, 2)
        load_x(6, 2)
        load_pos(0, 2)
        load_x(8, 2)
        load_x(10, 2)
        load_pos(2, 2)
        load_x(12, 2)
        load_pos(4, 2)
        load_x(14, 2)
        load_pos(6, 2)
        load_mix(0, 1, 0)

        for n in (0, 1):
            turn_x(n)
            copy_x(n)
        warm_tensor(2)
        sort_pairs(on_vector, down_sc[:].bitcast(U16), down_sc_raw[:].bitcast(U16))
        sort_pairs(on_vector, down_sb[:].bitcast(I32), down_raw[:].bitcast(I32))
        quant_x(0, 1)
        sort_x(on_scalar, 2)
        quant_x(1, 1)
        stage1(0)
        stage1(1)
        sort_x(on_scalar, 3)
        deal_mix_scales()
        spread_mix_scales(0)
        load_pos(8, 4)
        load_mix(1, 1, 0)
        spread_mix_scales(1)
        load_pos(12, 4)
        load_mix(2, 1, 0)
        spread_mix_scales(2)
        load_mix(3, 1, 0)
        load_gate(0, 2)
        spread_mix_scales(3)
        load_mix(0, 2, 1)
        load_keep()
        load_mix(2, 2, 1)
        load_gate(2, 2)
        load_scales(up_sc, up_scales, 1)
        load_gate(4, 2)
        load_words(up_sb, up_words, 1)
        load_gate(6, 2)
        load_gate(8, 4)
        sort_x(on_scalar, 4)
        sort_x(on_scalar, 5)
        for n in range(2, 8):
            if n >= 6:
                sort_x(on_vector, n)
            turn_x(n)
            copy_x(n)
        quant_x(2, 1)
        quant_x(3, 1)
        add_pos(0)
        stage1(2)
        stage1(3)
        sort_x(on_vector, 8)
        sort_x(on_vector, 9)
        add_pos(1)
        for n in range(8, 12):
            turn_x(n)
            copy_x(n)
        quant_x(4, 2)
        quant_x(6, 2)
        add_pos(2)
        add_pos(3)
        for n in range(4, 8):
            stage1(n)
        quant_x(8, 2)
        quant_x(10, 2)
        sort_x(on_scalar, 12)
        sort_x(on_scalar, 13)
        round_u(on_scalar, 0, G_COLS, R)
        round_u_gpsimd(0, 0, G_COLS)
        for n in range(12, 16):
            turn_x(n)
        for n in range(4, 8):
            add_pos(n)
        for n in range(12, 16):
            copy_x(n)
        for n in range(8, 12):
            stage1(n)
        quant_x(12, 2)
        quant_u(0)
        quant_x(14, 2)
        for n in range(12, 16):
            stage1(n)
        round_u_gpsimd(1, 0, G_COLS)
        deal_mix(on_scalar, [0], [0, 1], ALL)
        round_u(on_scalar, 1, G_COLS, R)
        deal_mix(on_scalar, [1], [0, 1], ALL)
        for n in range(8, 12):
            add_pos(n)
        quant_u(1)
        for s in (0, 1):
            for n in range(4):
                stage2(n, [s])
        deal_mix(on_scalar, [2], [0, 1], ALL)
        round_u(on_scalar, 2, G_COLS, R)
        round_u_gpsimd(2, 0, G_COLS)
        deal_mix(on_scalar, [3], [0, 1], ALL)
        for n in range(12, 16):
            add_pos(n)
            stage2(n - 8, [0, 1])
        quant_u(2)
        round_u(on_vector, 3, 0, V_COLS)
        round_u(on_scalar, 3, V_COLS, R)
        quant_u(3)
        for s in (2, 3):
            for n in range(5):
                stage2(n, [s])
        for n in range(5, 7):
            stage2(n, [2, 3])

        def products_of(n):
            gate_out(n, 0)
            gate_out(n, 1)

        def turn_and_copy(first, count, tag=None):
            turn_v(first, count)
            copy_v(first, count, tag)

        deal_mix(on_vector, [0, 1], [2], ALL)
        deal_mix(on_gpsimd, [2, 3], [2], ALL, "stage0")
        deal_mix(on_gpsimd, [0, 1], [3], ALL)
        for n in range(4):
            sigmoid_gate(n)
        sigmoid_gate(4, 0, BANK)
        for n in range(4):
            add_u(n)
        load_gate(12, 4, "u0")
        turn_and_copy(0, 2)
        turn_and_copy(2, 2, "stage2")
        stage2(7, [2, 3])
        add_u(4)
        add_u(5)
        stage2(8)
        add_u(6)
        quant_v(0, 2)
        quant_v(2, 2)
        add_u(7)
        sigmoid_gate(4, BANK)
        sigmoid_gate(5)
        stage3(0)
        stage3(1, (1, 0))
        deal_mix(on_gpsimd, [2, 3], [3], ALL, "stage2")
        move_half(1)
        products_of(0)
        store(0)
        add_u(8)
        stage2(9)
        products_of(1)
        store(1)
        sigmoid_gate(6)
        stage3(2)
        add_u(9)
        stage3(3, (1, 0))
        sigmoid_gate(7, 0, BANK)
        move_half(3)
        products_of(2)
        store(2)
        gate_out(3, 0)
        store_half(3, 0)
        turn_and_copy(4, 2)
        turn_and_copy(6, 2, "stage1")
        stage2(10)
        stage2(11, [0, 1])
        quant_v(4, 2)
        quant_v(6, 2)
        gate_out(3, 1, "stage1")
        sigmoid_gate(7, BANK)
        sigmoid_gate(8, 0, BANK)
        stage3(4, (1, 0))
        move_half(4)
        add_u(10)
        products_of(4)
        store_half(4, 0)
        store_half(3, 1)
        stage2(11, [2, 3])
        stage3(5)
        sigmoid_gate(8, BANK)
        sigmoid_gate(9)
        add_u(11)
        products_of(5)
        store(5)
        store_half(4, 1)
        stage3(6)
        products_of(6)
        stage3(7, (1, 0))
        move_half(7)
        store(6)
        gate_out(7, 0)
        store_half(7, 0)
        turn_and_copy(8, 2)
        turn_and_copy(10, 2, "stage3")
        stage2(12)
        stage2(13, [0, 1])
        quant_v(8, 2)
        quant_v(10, 2)
        gate_out(7, 1, "stage3")
        sigmoid_gate(10)
        stage3(8, (1, 0))
        move_half(8)
        add_u(12)
        products_of(8)
        store_half(8, 0)
        store_half(7, 1)
        sigmoid_gate(11)
        sigmoid_gate(12, 0, BANK)
        stage2(13, [2, 3])
        stage3(9)
        add_u(13)
        products_of(9)
        store(9)
        store_half(8, 1)
        stage3(10)
        products_of(10)
        turn_and_copy(12, 2, "stage0")
        sigmoid_gate(12, BANK)
        stage2(14)
        quant_v(12, 2)
        store(10)
        add_u(14)
        stage3(11, (1, 0))
        move_half(11)
        sigmoid_gate(13)
        gate_out(11, 1, "stage0")
        gate_out(11, 0)
        store_half(11, 0)
        stage2(15, [0, 1])
        stage3(12)
        products_of(12)
        store(12)
        store_half(11, 1)
        turn_and_copy(14, 1)
        sigmoid_gate(14)
        sigmoid_gate(15, 0, BANK)
        stage2(15, [2, 3])
        add_u(15)
        quant_v(14, 1)
        stage3(13)
        products_of(13)
        store(13)
        turn_and_copy(15, 1)
        sigmoid_gate(15, BANK)
        stage3(14)
        quant_v(15, 1)
        stage3(15)
        for n in (14, 15):
            for half in range(2):
                gate_out(n, half)
                store_half(n, half)
